import numpy as np, ml_dtypes
CORES = [6,15,38,47]
N = 4
BF = ml_dtypes.bfloat16
def gentries(a):
    return np.ascontiguousarray(a.reshape(8, 16, -1).transpose(0, 2, 1)).reshape(8, -1)
def gtable(e):
    e = np.asarray(e); return np.ascontiguousarray(e.reshape(8, -1, 16).transpose(0, 2, 1)).reshape(128, -1).astype(np.int32)
W, U, RO, D, EPS, NR = 3072, 256, 4, 256, 96, 2
S0 = W - 1 - RO * D
TOP = 784
def parts(rng):
    h = (rng.random((N, 8, 16, W)) * (1 + rng.integers(4, 8, (N, 8, 1, W)))).astype(np.int64)
    v = (0.75 + 0.5 * rng.random((N, 128, W))) * np.where(rng.random((N, 128, W)) < 0.125, -1.0, 1.0)
    f = rng.integers(1, D + 1, (N, 8, 16, W)); f[:, ::2] = np.sort(f[:, ::2], axis=2)
    w = ((D + 1) * rng.random((N, 8, 16, W)) ** 1.5).astype(np.int64)
    c = np.clip(rng.integers(0, S0 + 1, (N, 1, U)) + rng.integers(0, 97, (N, 8, U)), 0, S0)
    c = np.where(rng.random((N, 8, U)) < 0.02, rng.integers(0, S0 + 1, (N, 8, U)), c)
    tk = rng.integers(0, W, (N, 8, RO, U))
    lim = rng.integers(60, 300, (N, 1, U)) + rng.integers(-40, 41, (N, 8, U))
    return h, v, f, w, c, tk, lim
def pack(h, v, f, w, c, tk, lim):
    w = np.array(w); w[:, :, 0] = 0
    big = lambda a: np.ascontiguousarray(a.reshape(N, 128, W)).astype(np.float32).astype(BF)
    return {"hk": big(h), "vv": np.asarray(v, np.float32).astype(BF), "fw": big(f), "bw": big(w), "cur": np.stack([gtable(a) for a in c]),
            "tok": np.stack([gtable(a.reshape(8, -1)) for a in tk]), "th": np.ascontiguousarray(lim).astype(np.int32)}
def setup_inputs(rng):
    return pack(*parts(rng))
def setup_inputs_spread(rng):
    h, v, f, w, c, tk, lim = parts(rng)
    h = (rng.random((N, 8, 16, W)) * (1 + rng.integers(0, 8, (N, 8, 1, W)))).astype(np.int64)
    size = np.where(rng.random((N, 1, W)) < 0.1875, 0.5, 1.0)
    v = (0.75 + 0.25 * rng.random((N, 128, W))) * np.where(rng.random((N, 128, W)) < 0.03125, -1.0, 1.0) * size
    f = np.minimum(1 + (D * rng.random(f.shape) ** np.exp2(rng.integers(-1, 3, (N, 8, 1, W)))).astype(np.int64), D)
    w = np.minimum(((D + 1) * rng.random(w.shape) ** np.exp2(rng.integers(-1, 3, (N, 8, 1, W)))).astype(np.int64), D)
    c = np.where(rng.random((N, 1, U)) < 0.3, rng.integers(0, S0 + 1, (N, 8, U)), c)
    lim = np.minimum(np.exp2(9.62 * rng.random((N, 8, U))).astype(np.int64), TOP)
    return pack(h, v, f, w, c, tk, lim)
def setup_inputs_ends(rng):
    h, v, f, w, c, tk, lim = parts(rng)
    kind = rng.integers(0, 4, (N, 8, 1, W)); e = 7 * rng.integers(0, 2, (N, 8, 16, W))
    h = np.where(kind == 0, 7, np.where(kind == 1, 0, np.where(kind == 2, e, h)))
    f = np.where(rng.random(f.shape) < 0.8, np.where(rng.random(f.shape) < 0.5, 1, D), f)
    w = np.where(rng.random(w.shape) < 0.8, D * rng.integers(0, 2, w.shape), w)
    k = rng.random((N, 1, U))
    c = np.where(k < 0.5, S0 * rng.integers(0, 2, (N, 1, U)), np.where(k < 0.8, S0 * rng.integers(0, 2, (N, 8, U)), c))
    tk = np.where(rng.random(tk.shape) < 0.8, (W - 1) * rng.integers(0, 2, tk.shape), tk)
    lim = rng.choice(np.array([0, TOP, 0, TOP, 0, TOP, 0, TOP, TOP - 1, 392, 343, 49]), (N, 8, U))
    pos = S0 + D * np.arange(RO + 1)
    h[:, ::2, :, 0] = 0; h[:, 1::2, :, 0] = 7 * rng.integers(0, 2, (N, 4, 16)); h[:, :, :, pos[1:]] = 7
    f[:, :, 15, pos[:RO]] = D; w[:, :, 1:, W - 1] = 0; w[:, :, 1:, S0 + D] = D
    for u in (0, 3, U - 1): c[:, :, u] = S0; tk[:, :, :, u] = W - 1; lim[:, :, u] = TOP
    for u in (1, U - 2): c[:, :, u] = 0; tk[:, :, :, u] = 0; lim[:, :, u] = 0
    return pack(h, v, f, w, c, tk, lim)
def setup_inputs_corners(rng):
    h, v, f, w, c, tk, lim = parts(rng)
    h[:, 0::4] = rng.integers(1, 8, (N, 2, 1, W)); h[:, 1::4] = rng.integers(0, 2, (N, 2, 16, W)); h[:, 3::4] = rng.integers(6, 8, (N, 2, 16, W))
    lim[:, 0::4] = 16 * rng.integers(0, 8, (N, 2, U)) * rng.integers(0, 8, (N, 2, U)); lim[:, 1::4] = rng.integers(0, 12, (N, 2, U)); lim[:, 3::4] = rng.integers(600, TOP + 1, (N, 2, U))
    x = np.array([D, D - EPS, D - EPS - 1, D - EPS, D - EPS - 1, D - EPS + 1, 1, D])
    f[:, :, 15] = np.stack([rng.permutation(x) for _ in range(N)])[:, :, None]
    f[:, :, 0] = rng.choice(np.array([1, 2, 3, D - 1, D]), (N, 8, W))
    kind = rng.integers(0, 6, (N, 8, 1, W))
    w[:, :, 1:] = np.where(kind == 0, 0, np.where(kind == 1, D, rng.choice(np.array([0, 1, 2, 3, D - EPS - 1, D - EPS, D - 1, D]), (N, 8, 15, W))))
    c[:, :, 0::3] = c[:, :1, 0::3] + 0; lim[:, :, 0::3] = TOP
    c[:, :, 1::3] = S0 * rng.integers(0, 2, c[:, :, 1::3].shape)
    lim[:, :, 2::6] = 0
    return pack(h, v, f, w, c, tk, lim)
def setup_inputs_calm(rng):
    h, v, f, w, c, tk, lim = parts(rng)
    h[:, ::2] = rng.integers(0, 2, (N, 4, 16, W)); lim[:, ::2] = rng.integers(0, 9, (N, 4, U))
    near = np.arange(W) < S0
    f = np.where(near, rng.integers(1, 4, f.shape), rng.integers(D - 1, D + 1, f.shape))
    w = np.where(near, rng.integers(0, 4, w.shape), rng.choice(np.array([0, D - 2, D - 1, D]), w.shape))
    low = rng.random((N, 1, U)) < 0.7; low[:, :, 0] = True; low[:, :, U - 2] = False
    c = np.where(low, rng.integers(0, 4, (N, 1, U)) + rng.integers(0, 4, (N, 8, U)), S0)
    c[:, 7, 15::16] = S0
    tk[:, 2] = rng.integers(0, W, (N, RO, 1)); tk[:, 5] = rng.integers(0, W, (N, RO, 1))
    return pack(h, v, f, w, c, tk, lim)
def check_ranges(d):
    bad = []
    for k, lo, hi in (("hk", 0, 7), ("fw", 1, D), ("bw", 0, D), ("cur", 0, S0), ("tok", 0, W - 1), ("th", 0, TOP)):
        a = np.asarray(d[k]).astype(np.float64)
        if not (np.min(a) >= lo and np.max(a) <= hi): bad.append("range of " + k)
        if np.any(a != np.floor(a)): bad.append("whole numbers in " + k)
    if np.any(np.asarray(d["bw"]).astype(np.float64)[:, ::16] != 0): bad.append("entry 0 of bw is 0")
    a = np.abs(np.asarray(d["vv"]).astype(np.float64))
    if not np.all((a >= 0.25) & (a <= 2.0)): bad.append("sizes in vv")
    return bad
def score(h, fr, q):
    return np.matmul(h[np.arange(8)[:, None, None], fr], q[:, :, :, None])[:, :, :, 0]
def reference(hk, vv, fw, bw, cur, tok, th):
    turn = lambda a: np.ascontiguousarray(a.astype(np.float64).reshape(N, 8, 16, W).transpose(0, 1, 3, 2))
    h, v = turn(hk), turn(vv); f, w = turn(fw).astype(np.int64), turn(bw).astype(np.int64)
    c0 = np.stack([gentries(a) for a in cur]).astype(np.int64)
    tk = np.stack([gentries(a) for a in tok]).astype(np.int64).reshape(N, 8, RO, U)
    g1 = np.arange(8)[:, None]; g2 = np.arange(8)[:, None, None]
    carry = np.zeros((N, 8, U, 16))
    ym = np.zeros((N, 8, RO, U)); ys = np.zeros((N, 8, RO, U)); ya = np.zeros((N, 8, 16, RO, U))
    for t in range(RO):
        for r in range(N):
            p = (r + t) % N; c = c0[r]
            q = np.maximum(carry[r], h[p][g1, tk[r, :, t]])
            fr = c[:, :, None] + f[p][g1, c]
            hit = score(h[p], fr, q) > th[p][:, :, None]
            i = np.where(np.any(hit, axis=2), np.argmax(hit, axis=2), 15)
            stop = np.take_along_axis(fr, i[:, :, None], 2)[:, :, 0]
            last = np.max(stop, axis=0)
            b = np.where(stop < last - EPS, last, stop)
            s, back = [], []
            for k in range(NR):
                x = (p + k) % N; d = w[x][g1, b]
                at = np.maximum(b[:, :, None] - d, 0); back.append(at)
                s.append(np.where(d < (b - c)[:, :, None], score(h[x], at, q), -1.0))
            al = np.concatenate(s, axis=2); m = np.max(al, axis=2)
            e = np.where(al >= 0, np.exp((al - m[:, :, None]) * 0.0078125), 0.0)
            ym[p, :, t] = m; ys[p, :, t] = np.sum(e, axis=2)
            for k in range(NR):
                x = (p + k) % N
                part = np.matmul(e[:, :, None, 16 * k:16 * k + 16], v[x][g2, back[k]])[:, :, 0]
                ya[p][:, :, t] += part.transpose(0, 2, 1)
            if t + 1 < RO:
                j = np.argmax(s[0], axis=2)
                carry[r] = h[p][g1, np.take_along_axis(back[0], j[:, :, None], 2)[:, :, 0]]
                c0[r] = b
    return {"ym": ym.reshape(N, 8, RO * U).astype(np.float32), "ys": ys.reshape(N, 8, RO * U).astype(np.float32), "ya": ya.reshape(N, 128, RO * U).astype(np.float32)}

def check_inputs(d):
    bad = list(check_ranges(d))
    if not bad:
        for name, y in reference(**d).items():
            for q in range(N):
                v = np.abs(np.asarray(y[q], np.float64)); s = np.sqrt(np.mean(v * v))
                if v.max() > 4 * s or s < 2.0 ** 2: bad.append('%s of rank %d is uneven or too small' % (name, q))
    return bad

@@ -1,0 +1,560 @@
+import numpy as np
+from concourse.bass import DstId, RemoteDMATransfer
+from concourse.mybir import AluOpType as ALU, AxisListType as AX, ActivationFunctionType as AF
+
+W, RO, NC = 3072, 4, 2
+NK, NV, NSO, NQ, NS1, NR, NT = 5, 4, 6, 5, 4, 3, 6
+PEN, HB = 4096.0, 28.0
+F32, BF, F16, I32, U16 = "float32", "bfloat16", "float16", "int32", "uint16"
+SB = lambda n, d: ("sbuf", [128, n], d)
+SCRATCH = {
+    "hks": SB(W, BF), "vvs": SB(W, BF), "fws": SB(2816, BF), "bws": SB(W, BF), "num": SB(W, F32),
+    "curi": SB(16, I32), "toki": SB(64, I32), "toku": SB(64, U16), "tokl": SB(64, U16), "th16": SB(128, I32),
+    "lst": SB(5 * NC * 24, U16), "qcs": SB(RO * NC * 256, BF), "qcl": SB(RO * NC * 256, BF),
+    "bks": SB(RO * NC * 144, F32), "bkl": SB(RO * NC * 144, F32), "yas": SB(1024, F32), "mss": SB(1024, F32),
+    "kg": SB(NK * 2048, BF), "vg": SB(NV * 2048, BF), "so": SB(NSO * 2048, F32), "qd": SB(NQ * 1024, BF),
+    "sg": SB(2 * 512, BF), "s1": SB(NS1 * 512, F16), "rb": SB(NR * 512, F32), "rd": SB(2 * 512, BF),
+    "fg": SB(2 * 128, F32), "fr": SB(2 * 128, F32), "fm": SB(NT * 128, F32), "dd": SB(NT * 128, BF),
+    "inv": SB(NT * 128, BF), "ofk": SB(NT * 128, U16), "ofv": SB(NT * 128, U16), "ofc": SB(2 * 8, U16),
+    "ks": SB(NT * 128, F32), "ee": SB(NT * 128, F32), "msc": SB(NT * 256, F32), "hi": SB(NT * 128, BF),
+    "lo": SB(NT * 128, BF), "fa": SB(2 * 128, F32), "yt": SB(NT * 32, F32),
+    "ti": SB(NT * 32, I32), "tf": SB(NT * 64, F32), "xx": SB(2 * 48, F32),
+    "ci": SB(16, I32), "cf": SB(32, F32), "r128": SB(128, F32), "ones": SB(128, F32), "i32": SB(128, F32),
+    "idf": SB(128, BF), "inn": SB(128, BF), "in2": SB(256, BF), "a16": SB(16, F32), "a16n": SB(16, BF),
+    "selt": SB(16, F16), "selt2": SB(32, F16), "selw": SB(16, BF), "b16": SB(16, F32), "dw": SB(480, F16),
+    "dinv": SB(128, BF), "rsel": SB(2048, BF), "pvm": SB(512, F32), "ru4": SB(512, BF), "msk": SB(512, BF),
+    "rum": SB(256, F32), "cl": SB(256, F16), "cr": SB(1536, F16), "g8": SB(8, F32), "m16": SB(128, F32),
+    "ofq": SB(8, U16), "ofr": SB(2, U16), "rq": SB(8, I32), "repm": SB(128, F32), "cfr": SB(128, F32),
+    "cfb": SB(384, BF), "one1": SB(128, BF), "tmp": SB(128, BF),
+}
+for _b in range(8):
+    SCRATCH["pb%d" % _b] = ("psum", [128, 512], F32)
+LOADS = ["cur", "tok", "fwA", "hkA", "th", "hkB", "bwA", "vvA", "fwB", "bwB", "vvB"]
+SEMAPHORES = (["cV", "cA", "cP", "cG", "sent", "stored", "rtok"] + ["l" + n for n in LOADS]
+              + ["r%s%d%d" % (k, t, c) for k in "LQB" for t in range(RO) for c in range(NC)])
+
+REF = {"c": 1.0, "p": 0.5, "g": 1.56, "s": 3.8, "hop": 150.0, "net": 3000.0, "o": 30.0}
+
+
+def dur(cost, M):
+    tot = 0.0
+    for kind, n in cost:
+        if kind == "v": tot += max(64, n) * M["c"] + M["o"]
+        elif kind == "g": tot += 60 + n * M["g"] * M["c"] + M["o"]
+        elif kind == "s": tot += 60 + n * M["s"] * M["c"] + M["o"]
+        elif kind == "p": tot += n * M["p"]
+        elif kind == "n": tot += n
+    return tot
+
+
+POOLS = {"kg": NK, "vg": NV, "so": NSO, "qd": NQ, "sg": 2, "s1": NS1, "rb": NR, "rd": 2, "fg": 2, "rd_": NT, "ofk": NT, "ofc": 2,
+         "ks": NT, "msc": NT, "yt": NT, "tt": NT, "xx": 2, "ps": 8}
+OF = {"kg": ("kg", 1), "vg": ("vg", 1), "so": ("so", 2), "fr": ("fg", 0), "mm": ("msc", 0), "ms": ("msc", 0)}
+OF.update({k: (k, 0) for k in ("qd", "sg", "s1", "rb", "rd", "fg", "ofk", "ofc", "ks", "yt")})
+OF.update({k: ("rd_", 0) for k in ("fm", "dd", "inv", "ee", "hi", "lo", "ofv")})
+OF.update({k: ("tt", 0) for k in ("tia", "tib", "tfa", "tfb", "tfc")})
+OF.update({k: ("xx", 0) for k in ("xm", "xt", "xf", "xs", "fa")})
+
+
+def tile_of(key):
+    for p in OF:
+        d = key[len(p):].rstrip("x")
+        if key.startswith(p) and d.isdigit(): return OF[p][0], int(d[:len(d) - OF[p][1]])
+    return None
+
+
+def build(where=None):
+    ops, ring, who = [], {}, ["s"]
+
+    def op(eng, cost, fn, r, w, ps=None, new=False, sem=None, lat=0.0, alt=None):
+        ops.append({"alts": [(eng, cost, fn)] + (alt or []), "r": r, "w": w, "ps": ps, "new": new, "sem": sem, "lat": lat})
+
+    def slot(name, n):
+        k = ring.get(name, 0); ring[name] = k + 1
+        return k if where is None else where[(name, k)]
+
+    def tile():
+        k = ring.get("ps", 0); ring["ps"] = k + 1
+        return k
+
+    V = lambda n, fn, r, w, ps=None: op("V", [("v", n)], lambda e, T, B, X: [fn(e, T, B)], r, w, ps)
+    A = lambda n, fn, r, w, ps=None: op("A", [("v", n)], lambda e, T, B, X: [fn(e, T, B)], r, w, ps)
+    G = lambda n, fn, r, w: op("G", [("n", 170 + 2.0 * n)], lambda e, T, B, X: [fn(e, T)], r, w)
+
+    def gather(n, out, win, off, r, w):
+        op("A", [("g", n)], lambda e, T, B, X: [e.activation(out(T), win(T).indirect(off(T)), AF.Copy)], r, w,
+           alt=[("V", [("g", n)], lambda e, T, B, X: [e.tensor_copy(out(T), win(T).indirect(off(T)))])])
+        ops[-1]["role"] = who[0] + w[0][:2] + (w[0][-1] if n > 128 else "")
+
+    def P(n, mms, r, new=True, ps=None):
+        k = tile() if ps is None else ps
+        op("P", [("p", n)], lambda e, T, B, X: [e.matmul(*m) for m in mms(T, B)], r, [], k, new)
+        return k
+
+    def load(q, name, fn, w, ns):
+        op(q, [("n", 60)], lambda e, T, B, X: fn(e, T), [], w, sem="l" + name, lat=ns)
+    load("S", "cur", lambda e, T: [e.dma_start(T.curi[:], T.cur[:])], ["curi"], 2000)
+    load("S", "fwA", lambda e, T: [e.dma_start(T.fws[:, :2048], T.fw[:, :2048])], ["fwA"], 4500)
+    load("A", "tok", lambda e, T: [e.dma_start(T.toki[:], T.tok[:])], ["toki"], 2000)
+    load("A", "hkA", lambda e, T: [e.dma_start(T.hks[:, :2304], T.hk[:, :2304])], ["hkA"], 6000)
+    load("S", "th", lambda e, T: [e.dma_start(T.th16[8 * h:8 * h + 8, 64 * c:64 * c + 64], T.th[:, 128 * c + 64 * h:128 * c + 64 * h + 64])
+                                  for h in range(2) for c in range(2)], ["th16"], 3000)
+    load("S", "hkB", lambda e, T: [e.dma_start(T.hks[:, 2304:], T.hk[:, 2304:])], ["hkB"], 7000)
+    load("S", "bwA", lambda e, T: [e.dma_start(T.bws[:, :2304], T.bw[:, :2304])], ["bwA"], 9500)
+    load("S", "vvA", lambda e, T: [e.dma_start(T.vvs[:, :2304], T.vv[:, :2304])], ["vvA"], 12000)
+    load("S", "fwB", lambda e, T: [e.dma_start(T.fws[:, 2048:], T.fw[:, 2048:2816])], ["fwB"], 13000)
+    load("S", "bwB", lambda e, T: [e.dma_start(T.bws[:, 2304:], T.bw[:, 2304:])], ["bwB"], 14000)
+    load("S", "vvB", lambda e, T: [e.dma_start(T.vvs[:, 2304:], T.vv[:, 2304:])], ["vvB"], 15000)
+
+    IO = dict(allow_small_or_imprecise_dtypes=True)
+    G(1, lambda e, T: e.iota(T.ci[:, 0:1], [[1, 1]], 0, 1), [], ["ci0"])
+    G(768, lambda e, T: e.iota(T.num[:, :768], [[1, 768]], 0, 0, **IO), [], ["num0"])
+    for k in range(1, 4):
+        if k == 1: A(768, lambda e, T, B: e.activation(T.num[:, 768:1536], T.num[:, :768], AF.Identity, bias=768.0), ["num0"], ["num1"])
+        else: G(768, lambda e, T, k=k: e.iota(T.num[:, 768 * k:768 * k + 768], [[1, 768]], 768 * k, 0, **IO), [], ["num%d" % k])
+    NUMS = lambda n: ["num%d" % k for k in range((n + 767) // 768)]
+    r128 = lambda T: T.num[:, :128]
+    ci = lambda T, k: T.ci[:, k:k + 1]
+    cf = lambda T, k: T.cf[:, k:k + 1]
+
+    def bits(k, a, opa, b=None, opb=None):
+        if b is None: V(1, lambda e, T, B: e.tensor_scalar(ci(T, k), ci(T, 0), a, None, opa), ["ci0"], ["ci%d" % k])
+        else: V(1, lambda e, T, B: e.tensor_scalar(ci(T, k), ci(T, 0), a, b, opa, opb), ["ci0"], ["ci%d" % k])
+        V(1, lambda e, T, B: e.tensor_copy(cf(T, k), ci(T, k)), ["ci%d" % k], ["cf%d" % k])
+    AND, SHR = ALU.bitwise_and, ALU.arith_shift_right
+    bits(1, 15, AND); bits(2, 4, SHR); bits(3, 7, AND); bits(4, 4, SHR, 3, AND); bits(5, 3, SHR); bits(6, 1, AND)
+
+    def col(k, a, s1, s2, o0, o1, r):
+        sc = lambda T, s: cf(T, s[0]) if isinstance(s, list) else s
+        V(1, lambda e, T, B: e.tensor_scalar(cf(T, k), cf(T, a), sc(T, s1), sc(T, s2), *([o0, o1] if o1 is not None else [o0])), ["cf%d" % a] + ["cf%d" % j for j in r], ["cf%d" % k])
+    V(1, lambda e, T, B: e.tensor_copy(cf(T, 0), ci(T, 0)), ["ci0"], ["cf0"])
+    col(10, 1, 15.0, -2048.0, ALU.is_equal, ALU.mult, [])
+    col(8, 1, -4096.0, 63488.0, ALU.mult, ALU.add, [])
+    col(11, 8, [10], None, ALU.add, None, [10])
+    col(12, 3, 0.0, 1000.0, ALU.is_equal, ALU.mult, [])
+    col(13, 1, -1.0, [12], ALU.add, ALU.add, [12])
+    col(14, 0, -1.0, [12], ALU.add, ALU.add, [12])
+    col(15, 3, 7.0, -HB, ALU.is_equal, ALU.mult, [])
+    col(16, 1, 8.0, [2], ALU.mult, ALU.add, [2])
+    op("V", [], lambda e, T, B, X: [], [], [])
+    col(18, 6, -31.0, 1.0, ALU.mult, ALU.mult, [])
+    col(19, 1, 32.0, [18], ALU.mult, ALU.add, [18])
+    col(20, 2, 2.0, [19], ALU.mult, ALU.add, [19])
+    V(1, lambda e, T, B: e.tensor_copy(T.ofr[:, 0:1], cf(T, 20)), ["cf20"], ["ofr"])
+    V(8, lambda e, T, B: e.tensor_scalar(T.ofq[:], T.num[:, 0:8], 128.0, cf(T, 16), ALU.mult, ALU.add), ["num0", "cf16"], ["ofq"])
+    TS = lambda n, o, i, s1, s2, o0, o1, r, w: V(n, lambda e, T, B: e.tensor_scalar(o(T), i(T), s1(T) if s1 else None, s2, o0, o1), r, w)
+    r16 = lambda T: T.num[:, :16]
+    TS(16, lambda T: T.a16[:], r16, lambda T: cf(T, 1), 1.0, ALU.is_equal, ALU.mult, ["num0", "cf1"], ["a16"])
+    TS(16, lambda T: T.a16n[:], r16, lambda T: cf(T, 1), -1.0, ALU.is_equal, ALU.mult, ["num0", "cf1"], ["a16n"])
+    V(16, lambda e, T, B: e.tensor_scalar(T.selw[:], T.a16[:], cf(T, 11), None, ALU.mult), ["a16", "cf11"], ["selw"])
+    V(16, lambda e, T, B: e.tensor_copy(T.selt[:], T.a16[:]), ["a16"], ["selt"])
+    for x in range(2):
+        V(16, lambda e, T, B, x=x: e.tensor_copy(T.selt2[:, x::2], T.a16[:]), ["a16"], ["selt2%d" % x])
+    TS(128, lambda T: T.i32[:], r128, lambda T: cf(T, 0), 1.0, ALU.is_equal, ALU.mult, ["num0", "cf0"], ["i32"])
+    TS(128, lambda T: T.idf[:], r128, lambda T: cf(T, 0), 2.0 ** -13, ALU.is_equal, ALU.mult, ["num0", "cf0"], ["idf"])
+    TS(128, lambda T: T.inn[:], r128, lambda T: cf(T, 0), -PEN, ALU.is_equal, ALU.mult, ["num0", "cf0"], ["inn"])
+    for x in range(2):
+        V(64, lambda e, T, B, x=x: e.tensor_copy(T.in2[:, x::2], T.inn[:]), ["inn"], ["in2%d" % x])
+    TS(16, lambda T: T.b16[:], r16, lambda T: cf(T, 13), 1.0, ALU.is_equal, ALU.mult, ["num0", "cf13"], ["b16"])
+    V(480, lambda e, T, B: e.tensor_scalar(T.dw[:], T.num[:, :480], 0.0, None, ALU.mult), ["num0"], ["dw"])
+    op("V", [("v", 32)] * 2, lambda e, T, B, X: [e.tensor_tensor(T.dw[64 * h:64 * h + 64, 240 * h + 112:240 * h + 128], T.a16[64 * h:64 * h + 64, :], T.b16[64 * h:64 * h + 64, :], ALU.subtract)
+                                                 for h in range(2)], ["a16", "b16", "dw"], ["dw"])
+    TS(128, lambda T: T.tmp[:], r128, lambda T: cf(T, 14), PEN, ALU.is_equal, ALU.mult, ["num0", "cf14"], ["tmp"])
+    V(256, lambda e, T, B: e.tensor_tensor(T.dinv[:], T.tmp[:], T.inn[:], ALU.add), ["tmp", "inn"], ["dinv"])
+    V(128, lambda e, T, B: e.memset(T.m16[:], 1.0), [], ["m16"])
+    V(8, lambda e, T, B: e.memset(T.m16[:, 0::16], 0.0), ["m16"], ["m16"])
+    V(128, lambda e, T, B: e.memset(T.ones[:], 1.0), [], ["ones"])
+    V(64, lambda e, T, B: e.memset(T.one1[:], 1.0), [], ["one1"])
+    G(2048, lambda e, T: e.iota(T.rsel[:], [[0, 2048]], 1, 0, **IO), [], ["rsel"])
+    def zero(pool, k, n, view):
+        V(n, lambda e, T, B: e.memset(view(T), 0), [], []); ops[-1]["init"] = (pool, k)
+    for k in range(NQ):
+        if k < 2: zero("qd", k, 512, lambda T, k=k: T.qd[:, 1024 * k:1024 * k + 1024])
+        else:
+            G(1024, lambda e, T, k=k: e.iota(T.qd[:, 1024 * k:1024 * k + 1024], [[0, 1024]], 0, 0, **IO), [], []); ops[-1]["init"] = ("qd", k)
+    for k in range(NR): zero("rb", k, 256, lambda T, k=k: T.rb[:, 512 * k:512 * k + 256])
+    for k in range(2): zero("rd", k, 128, lambda T, k=k: T.rd[:, 512 * k:512 * k + 256])
+    V(NT * 64, lambda e, T, B: e.memset(T.tf[:], 0.0), [], ["ztf"])
+    V(NT * 32, lambda e, T, B: e.memset(T.ti[:], 0), [], ["zti"])
+    G(512, lambda e, T: e.iota(T.ru4[:], [[0, 16], [1, 4], [0, 8]], 0, 0, **IO), [], ["ru4"])
+    G(128, lambda e, T: e.iota(T.rum[:, :128], [[0, 2], [1, 4], [0, 16]], 0, 0, **IO), [], ["rum0"])
+    G(128, lambda e, T: e.iota(T.rum[:, 128:], [[1, 2], [0, 64]], 0, 0, **IO), [], ["rum1"])
+    V(128, lambda e, T, B: e.tensor_scalar(T.cl[0:16, :128], T.rum[0:16, 128:], T.cf[0:16, 5:6], None, ALU.is_equal), ["rum1", "cf5"], ["cl0"])
+    V(128, lambda e, T, B: e.tensor_scalar(T.cl[0:4, 128:], T.rum[0:4, :128], T.cf[0:4, 0:1], -PEN, ALU.not_equal, ALU.mult), ["rum0", "cf0"], ["cl1"])
+    TS(8, lambda T: T.g8[:], lambda T: T.num[:, :8], lambda T: cf(T, 3), -1.0, ALU.is_equal, ALU.mult, ["num0", "cf3"], ["g8"])
+    op("V", [("v", 128)] * 8, lambda e, T, B, X: [e.tensor_scalar(T.cr[0:16, h:1024:8], T.th16[0:16, :], T.g8[0:16, h:h + 1], None, ALU.mult) for h in range(8)],
+       ["g8", "th16"], ["cr"])
+    V(256, lambda e, T, B: e.tensor_scalar(T.cr[0:4, 1024:], T.ru4[0:4, :], T.cf[0:4, 0:1], None, ALU.is_equal), ["ru4", "cf0"], ["cr1"])
+    V(256, lambda e, T, B: e.tensor_scalar(T.msk[:], T.ru4[:], cf(T, 4), None, ALU.is_equal), ["ru4", "cf4"], ["msk"])
+    G(128, lambda e, T: e.iota(T.cfr[0:1, :], [[0, 8], [-1, 16]], 15, 0, **IO), [], ["cfr"])
+    V(64, lambda e, T, B: e.memset(T.cfb[0:1, 0:256:2], 0.0), [], ["cfb0"])
+    V(128, lambda e, T, B: e.tensor_scalar(T.cfb[0:1, 1:256:2], T.cfr[0:1, :], 0.0625, None, ALU.mult), ["cfr"], ["cfb"])
+    V(128, lambda e, T, B: e.tensor_scalar(T.cfb[0:1, 256:], T.cfr[0:1, :], 16384.0, 8192.0, ALU.mult, ALU.add), ["cfr"], ["crow"])
+    for c in range(NC):
+        V(8, lambda e, T, B, c=c: e.tensor_copy(T.lst[:, 24 * c + 8:24 * c + 16], T.curi[:, 8 * c:8 * c + 8]), ["curi"], ["Lin0%d" % c])
+    V(64, lambda e, T, B: e.tensor_copy(T.toku[:], T.toki[:]), ["toki"], ["toku"])
+    op("G", [("n", 3000)], lambda e, T, B, X: X["tokens"](), ["toku"], ["tokl"], sem="rtok", lat=-1)
+    for h in range(2):
+        for u in range(2):
+            G(128, lambda e, T, h=h, u=u: e.affine_select(T.pvm[:, 256 * h + 128 * u:256 * h + 128 * u + 128], T.ones[:], [[-16, 8], [1000, 2], [-1, 8]],
+                                                          ALU.is_equal, 0.0, -8 * h - 1000 * u, 1), ["ones"], ["perm%d%d" % (h, u)])
+    G(2048, lambda e, T: e.affine_select(T.rsel[:], T.rsel[:], [[-1, 16], [-16, 8], [0, 16]], ALU.is_equal, 0.0, 0, 1), ["rsel"], ["rsel"])
+    G(128, lambda e, T: e.affine_select(T.repm[0:16, :], T.ones[0:16, :], [[-1, 8], [0, 16]], ALU.is_equal, 0.0, -8, 1), ["ones"], ["repm"])
+
+    def send(name, src, dst, r, w, to, extra):
+        op("G", [("n", 600)], lambda e, T, B, X: X["send"](name, src(T), dst(T), to), r, w, sem=name, lat=-1 - extra)
+
+    def kgather(win, wk, ko):
+        k = slot("kg", NK)
+        for h in range(2):
+            gather(1024, lambda T, h=h: T.kg[:, 2048 * k + 1024 * h:2048 * k + 1024 * h + 1024], win,
+                   lambda T, h=h: T.ofk[:, 128 * ko + 64 * h:128 * ko + 64 * h + 64], wk + ["ofk%d" % ko], ["kg%d%d" % (k, h)])
+        return k
+
+    def first(T, B, k, kq, acc):
+        out = []
+        for h in range(2):
+            for b in range(16):
+                u = 64 * h + 4 * b
+                out.append((B[64 * h:64 * h + 64, 32 * b:32 * b + 32], T.kg[:, 2048 * k + 16 * u:2048 * k + 16 * u + 64],
+                            T.qd[:, 1024 * kq + 8 * u:1024 * kq + 8 * u + 32], not acc, not acc))
+        return out
+
+    def spread(src, rk):
+        kq = slot("qd", NQ)
+        op("V", [("s", 128)], lambda e, T, B, X: [e.tensor_copy(T.qd[:, 1024 * kq:1024 * kq + 1024].indirect(T.ofq[:]), src(T))], rk + ["ofq"], ["qd%d" % kq])
+        return kq
+
+    def tolist(mms, n, r, out, w):
+        ps = P(n, mms, r)
+        ky = slot("yt", NT)
+        V(32, lambda e, T, B: e.transpose(T.yt[:, 32 * ky:32 * ky + 32], B[:, :32]), [], ["yt%d" % ky], ps)
+        V(8, lambda e, T, B: e.tensor_copy(out(T), T.yt[:, 32 * ky:32 * ky + 8]), ["yt%d" % ky], w)
+
+    def read(t, c, own, kq, kr):
+        n = 2304 + 256 * t; who[0] = "o" if own else "h"
+        ab = lambda x: [x + "A"] + ([x + "B"] if t else [])
+        base = 24 * (NC * t + c) + 8 if own else 24 * (NC * (t + 1) + c)
+        Lc, Lb = (lambda T: T.lst[:, base:base + 8]), (lambda T: T.lst[:, base + 8:base + 16])
+        kc, kb = (["Lin%d%d" % (t, c)], ["Lb%d%d" % (t, c)]) if own else (["Lin%d%d" % (t + 1, c)],) * 2
+        k = slot("rd_", NT); s = slice(128 * k, 128 * k + 128)
+        ko = slot("ofk", NT)
+        gather(128, lambda T: T.dd[:, s], lambda T: T.bws[:, :n], Lb, ab("bw") + kb, ["dd%d" % k])
+        op("V", [("g", 128)], lambda e, T, B, X: [e.tensor_tensor(T.fm[:, s], T.num[:, :n].indirect(Lb(T)), T.dd[:, s], ALU.subtract)], NUMS(n) + kb + ["dd%d" % k], ["fm%d" % k])
+        V(128, lambda e, T, B: e.tensor_copy(T.ofk[:, 128 * ko:128 * ko + 128], T.fm[:, s]), ["fm%d" % k], ["ofk%d" % ko])
+        kk = kgather(lambda T: T.hks[:, :n], ab("hk"), ko)
+        op("V", [("g", 128)], lambda e, T, B, X: [e.tensor_tensor(T.inv[:, s], T.num[:, :n].indirect(Lc(T)), T.fm[:, s], ALU.is_ge)], NUMS(n) + kc + ["fm%d" % k], ["inv%d" % k])
+        ps = P(2048, lambda T, B: first(T, B, kk, kq, False), ["kg%d0" % kk, "kg%d1" % kk, "qd%d" % kq])
+        k1 = slot("s1", NS1); o1 = 512 * k1
+        V(512, lambda e, T, B: e.tensor_tensor(T.s1[:, o1:o1 + 512], B[:, :], T.msk[:], ALU.mult), ["msk"], ["s1%d" % k1], ps)
+        sv = lambda T, h, g: T.s1[64 * h:64 * h + 64, o1 + g:o1 + 512:8]
+        key = own and t + 1 < RO
+        if key:
+            def mms(T, B):
+                out = [(B[:, :256], T.inv[:, s], T.in2[:], True, False), (B[:, 1:256:2], T.dd[:, s], T.idf[:], False, False)]
+                out += [(B[64 * h:64 * h + 64, 32 * g:32 * g + 32], sv(T, h, g), T.selt2[64 * h:64 * h + 64, :], False, False) for h in range(2) for g in range(8)]
+                return out + [(B[:, :256], T.one1[0:1, :], T.cfb[0:1, :256], False, True)]
+            ps = P(1664, mms, ["inv%d" % k, "dd%d" % k, "s1%d" % k1, "in20", "in21", "idf", "one1", "cfb", "cfb0", "selt20", "selt21"])
+            sc = lambda B: B[:, 0:256:2]
+            kx = slot("ks", NT); kt = slot("tt", NT); kd = slot("rd", 2); kf = slot("ofc", 2)
+            V(128, lambda e, T, B: e.tensor_tensor_scan(T.ks[:, 128 * kx:128 * kx + 128], T.m16[:], B[:, 1:256:2], 0.0, ALU.mult, ALU.max), ["m16"], ["ks%d" % kx], ps)
+            V(8, lambda e, T, B: e.tensor_scalar(T.ti[:, 32 * kt:32 * kt + 8], T.ks[:, 128 * kx + 15:128 * kx + 128:16], 8192.0, None, ALU.mult), ["ks%d" % kx], ["tia%d" % kt])
+            V(8, lambda e, T, B: e.tensor_scalar(T.ti[:, 32 * kt + 16:32 * kt + 24], T.ti[:, 32 * kt:32 * kt + 8], 511, None, AND), ["tia%d" % kt], ["tib%d" % kt])
+            op("V", [("s", 16)], lambda e, T, B, X: [e.tensor_copy(T.rd[:, 512 * kd:512 * kd + 512].indirect(T.ofr[:, 0:1]), T.ti[:, 32 * kt + 16:32 * kt + 32])],
+               ["tib%d" % kt, "ofr"], ["rd%d" % kd])
+            tolist(lambda T, B: [m for x in range(2) for m in (
+                (B[:, 16 * x:16 * x + 16], T.rb[:, 512 * kr + x:512 * kr + 256:2], T.a16[:], True, False),
+                (B[:, 16 * x:16 * x + 16], T.rd[:, 512 * kd + x:512 * kd + 256:2], T.a16n[:], False, True))],
+                640, ["rb%d" % kr, "rd%d" % kd, "a16", "a16n"], lambda T: T.ofc[:, 8 * kf:8 * kf + 8], ["ofc%d" % kf])
+            oq = 256 * (NC * t + c)
+            gather(128, lambda T: T.qcs[:, oq + 128:oq + 256], lambda T: T.hks[:, :n], lambda T: T.ofc[:, 8 * kf:8 * kf + 8], ab("hk") + ["ofc%d" % kf], ["cs%d%d" % (t, c)])
+            send("rQ%d%d" % (t, c), lambda T: T.qcs[:, oq:oq + 256], lambda T: T.qcl[:, oq:oq + 256], ["qs%d%d" % (t, c), "cs%d%d" % (t, c)], ["ql%d%d" % (t, c)], 1, 500)
+        else:
+            def mms(T, B):
+                return [(B[:, :128], T.inv[:, s], T.inn[:], True, False)] + [
+                    (B[64 * h:64 * h + 64, 16 * g:16 * g + 16], sv(T, h, g), T.selt[64 * h:64 * h + 64, :], False, False) for h in range(2) for g in range(8)] + [
+                    (B[:, :128], T.inv[:, s], T.inn[:], False, True)]
+            ps = P(1280, mms, ["inv%d" % k, "s1%d" % k1, "inn", "selt"])
+            sc = lambda B: B[:, :128]
+        km = slot("msc", NT); om = 256 * km
+        V(128, lambda e, T, B: e.tensor_tensor_scan(T.msc[:, om:om + 128], T.m16[:], sc(B), 0.0, ALU.mult, ALU.max), ["m16"], ["mm%d" % km], ps)
+        A(128, lambda e, T, B: e.activation(T.ee[:, s], sc(B), AF.Exp, scale=0.0078125), [], ["ee%d" % k], ps)
+        V(128, lambda e, T, B: e.tensor_tensor_scan(T.msc[:, om + 128:om + 256], T.m16[:], T.ee[:, s], 0.0, ALU.mult, ALU.add), ["m16", "ee%d" % k], ["ms%d" % km])
+        ps = P(1152, lambda T, B: [m for h in range(2) for m in [(B[:, 64 * h:64 * h + 64], T.dinv[:], T.inv[:, 128 * k + 64 * h:128 * k + 64 * h + 64], True, False)] + [
+            (B[:, 64 * h:64 * h + 64], T.dw[:, 240 * h + 112 - 16 * g:240 * h + 240 - 16 * g], T.s1[:, o1 + g:o1 + 512:8], False, g == 7) for g in range(8)]],
+            ["inv%d" % k, "s1%d" % k1, "dinv", "dw"])
+        op("A", [("v", 128)] * 2, lambda e, T, B, X: [e.activation(o, B[:, :128], AF.Exp, bias=cf(T, 15), scale=0.0078125) for o in (T.hi[:, s], B[:, 128:256])],
+           ["cf15"], ["hi%d" % k], ps)
+        V(128, lambda e, T, B: e.tensor_tensor(T.lo[:, s], B[:, 128:256], T.hi[:, s], ALU.subtract), ["hi%d" % k], ["lo%d" % k], ps)
+        ps = P(1024, lambda T, B: [(B[:, 64 * h:64 * h + 64], T.pvm[:, 256 * h + 128 * u:256 * h + 128 * u + 128], T.fm[:, 128 * k + u:128 * k + 128:2], u == 0, u == 1)
+                                   for h in range(2) for u in range(2)], ["fm%d" % k, "perm00", "perm01", "perm10", "perm11"])
+        V(128, lambda e, T, B: e.tensor_copy(T.ofv[:, s], B[:, :128]), [], ["ofv%d" % k], ps)
+        kv = slot("vg", NV); kso = slot("so", NSO)
+        for h in range(2):
+            gather(1024, lambda T, h=h: T.vg[:, 2048 * kv + 1024 * h:2048 * kv + 1024 * h + 1024], lambda T: T.vvs[:, :n],
+                   lambda T, h=h: T.ofv[:, 128 * k + 64 * h:128 * k + 64 * h + 64], ab("vv") + ["ofv%d" % k], ["vg%d%d" % (kv, h)])
+            for b in range(2):
+                ps = P(1024, lambda T, B, h=h, b=b: [(B[:, i:512:8], T.rsel[:, 128 * (8 * h + i):128 * (8 * h + i) + 128], x[:, 128 * k + 64 * b:128 * k + 64 * b + 64], j == 0, j == 1)
+                                                     for i in range(8) for j, x in enumerate((T.hi, T.lo))], ["hi%d" % k, "lo%d" % k, "rsel"])
+                o = 1024 * h + 512 * b
+                V(512, lambda e, T, B, o=o: e.tensor_tensor_scan(T.so[:, 2048 * kso + o:2048 * kso + o + 512], T.vg[:, 2048 * kv + o:2048 * kv + o + 512], B[:, :], 0.0, ALU.add, ALU.mult),
+                  ["vg%d%d" % (kv, h)], ["so%d%d%d" % (kso, h, b)], ps)
+        parts = lambda T, B, more: [m for b in range(2) for m in [(B[:, 64 * b:64 * b + 64], T.i32[:], x[:, o + 64 * b:o + 64 * b + 64], True, False) for x, o in more] + [
+            (B[:, 64 * b:64 * b + 64], T.i32[:], T.so[:, 2048 * kso + 1024 * h + 512 * b + 7:2048 * kso + 1024 * h + 512 * b + 512:8], h == 0 and not more, h == 1) for h in range(2)]]
+        return km, parts, ["so%d%d%d" % (kso, h, b) for h in range(2) for b in range(2)] + ["i32"]
+
+    for t in range(RO):
+        keep = {}
+        for c in range(NC):
+            n = 2304 + 256 * t; base = 24 * (NC * t + c); oq = 256 * (NC * t + c)
+            Lc = lambda T, base=base: T.lst[:, base + 8:base + 16]
+            kl = ["Lin%d%d" % (t, c)]; who[0] = "s"
+            k = slot("fg", 2); s = slice(128 * k, 128 * k + 128); ko = slot("ofk", NT)
+            gather(128, lambda T, s=s: T.fg[:, s], lambda T, n=n: T.fws[:, :n - 256], Lc, ["fwA"] + (["fwB"] if t else []) + kl, ["fg%d" % k])
+            op("V", [("g", 128)], lambda e, T, B, X, s=s, n=n, Lc=Lc: [e.tensor_tensor(T.fr[:, s], T.num[:, :n].indirect(Lc(T)), T.fg[:, s], ALU.add)], NUMS(n) + kl + ["fg%d" % k], ["fr%d" % k])
+            V(128, lambda e, T, B, s=s, ko=ko: e.tensor_copy(T.ofk[:, 128 * ko:128 * ko + 128], T.fr[:, s]), ["fr%d" % k], ["ofk%d" % ko])
+            kk = kgather(lambda T, n=n: T.hks[:, :n], ["hkA"] + (["hkB"] if t else []), ko)
+            q = lambda T, oq=oq: T.qcs[:, oq:oq + 128]
+            if t == 0:
+                gather(128, q, lambda T: T.hks[:, :], lambda T, c=c: T.toku[:, 8 * c:8 * c + 8], ["hkA", "hkB", "toku"], ["qs0%d" % c])
+            else:
+                op("V", [("g", 128)], lambda e, T, B, X, q=q, oq=oq, o=16 * t + 8 * c: [e.tensor_tensor(q(T), T.hks[:, :].indirect(T.tokl[:, o:o + 8]), T.qcl[:, oq - 256 * NC + 128:oq - 256 * NC + 256], ALU.max)],
+                   ["hkA", "hkB", "tokl", "ql%d%d" % (t - 1, c)], ["qs%d%d" % (t, c)])
+            if t + 1 == RO:
+                send("rQ%d%d" % (t, c), q, lambda T, oq=oq: T.qcl[:, oq:oq + 128], ["qs%d%d" % (t, c)], ["ql%d%d" % (t, c)], 1, 250)
+            kq = spread(q, ["qs%d%d" % (t, c)])
+            ps = P(3072, lambda T, B, c=c, kk=kk, kq=kq: [(B[:, :], T.cl[0:16, :128], T.cr[0:16, 512 * c:512 * c + 512], True, False)] + first(T, B, kk, kq, True)
+                   + [(B[:, :], T.cl[0:4, 128:], T.cr[0:4, 1024:], False, True)],
+                   ["kg%d0" % kk, "kg%d1" % kk, "qd%d" % kq, "cl0", "cl1", "cr", "cr1"])
+            kg_ = slot("sg", 2); og = 512 * kg_
+            A(512, lambda e, T, B, og=og: e.activation(T.sg[:, og:og + 512], B[:, :], AF.Sign, bias=-0.5), [], ["sg%d" % kg_], ps)
+            ps = P(1536, lambda T, B, s=s, og=og: [(B[:, :128], T.fr[:, s], T.i32[:], True, False)] + [
+                (B[64 * h:64 * h + 64, 16 * g:16 * g + 16], T.sg[64 * h:64 * h + 64, og + g:og + 512:8], T.selw[64 * h:64 * h + 64, :], False, False)
+                for h in range(2) for g in range(8)] + [(B[:, :128], T.one1[0:1, :], T.cfb[0:1, 256:], False, True)], ["fr%d" % k, "sg%d" % kg_, "i32", "selw", "one1", "crow"])
+            kx = slot("ks", NT); kt = slot("tt", NT); kr = slot("rb", NR); oi = 32 * kt; of = 64 * kt
+            ta, tb, fa_, fb, fc = ["ti%s%d" % (x, kt) for x in "ab"] + ["tf%s%d" % (x, kt) for x in "abc"]
+            V(128, lambda e, T, B, kx=kx: e.tensor_tensor_scan(T.ks[:, 128 * kx:128 * kx + 128], T.m16[:], B[:, :128], 0.0, ALU.mult, ALU.max), ["m16"], ["ks%d" % kx], ps)
+            V(8, lambda e, T, B, kx=kx, oi=oi: e.tensor_copy(T.ti[:, oi:oi + 8], T.ks[:, 128 * kx + 15:128 * kx + 128:16]), ["ks%d" % kx, "zti", "ztf"], [ta])
+            V(8, lambda e, T, B, oi=oi: e.tensor_scalar(T.ti[:, oi + 16:oi + 24], T.ti[:, oi:oi + 8], 4095, None, AND), [ta], [tb])
+            V(8, lambda e, T, B, oi=oi, of=of: e.tensor_copy(T.tf[:, of:of + 8], T.ti[:, oi + 16:oi + 24]), [tb], [fa_])
+            V(8, lambda e, T, B, of=of: e.tensor_reduce(T.tf[:, of + 48:of + 49], T.tf[:, of:of + 8], AX.X, ALU.max), [fa_], [fc])
+            V(8, lambda e, T, B, of=of: e.tensor_scalar(T.tf[:, of + 32:of + 40], T.tf[:, of:of + 8], 96.0, T.tf[:, of + 48:of + 49], ALU.add, ALU.is_lt), [fa_, fc], [fc + "x"])
+            V(8, lambda e, T, B, of=of: e.tensor_scalar(T.tf[:, of + 16:of + 24], T.tf[:, of + 32:of + 40], T.tf[:, of + 48:of + 49], None, ALU.mult), [fc, fc + "x"], [fb])
+            op("V", [("s", 16)], lambda e, T, B, X, of=of, kr=kr: [e.tensor_tensor(T.rb[:, 512 * kr:512 * kr + 512].indirect(T.ofr[:, 0:1]), T.tf[:, of:of + 16], T.tf[:, of + 16:of + 32], ALU.max)],
+               [fa_, fb, "ofr"], ["rb%d" % kr])
+            tolist(lambda T, B, kr=kr: [(B[:, 16 * x:16 * x + 16], T.rb[:, 512 * kr + x:512 * kr + 256:2], T.a16[:], True, True) for x in range(2)],
+                   512, ["rb%d" % kr, "a16"], lambda T, base=base: T.lst[:, base + 16:base + 24], ["Lb%d%d" % (t, c)])
+            send("rL%d%d" % (t, c), lambda T, base=base: T.lst[:, base + 8:base + 24], lambda T, base=base: T.lst[:, base + 24 * NC:base + 24 * NC + 16],
+                 kl + ["Lb%d%d" % (t, c)], ["Lin%d%d" % (t + 1, c)], 1, 0)
+            keep[c] = read(t, c, True, kq, kr)
+        for c in range(NC):
+            oq = 256 * (NC * t + c); ob = 144 * (NC * t + c)
+            kq = spread(lambda T, oq=oq: T.qcl[:, oq:oq + 128], ["ql%d%d" % (t, c)])
+            km, parts, rk = read(t, c, False, kq, None)
+            A(16, lambda e, T, B, ob=ob, km=km: e.activation(T.bks[:, ob + 128:ob + 144], T.msc[:, 256 * km + 15:256 * km + 256:16], AF.Copy), ["mm%d" % km, "ms%d" % km], ["bm%d%d" % (t, c)])
+            ps = P(1024, lambda T, B, parts=parts: parts(T, B, []), rk)
+            A(128, lambda e, T, B, ob=ob: e.activation(T.bks[:, ob:ob + 128], B[:, :128], AF.Copy), [], ["ba%d%d" % (t, c)], ps)
+            send("rB%d%d" % (t, c), lambda T, ob=ob: T.bks[:, ob:ob + 144], lambda T, ob=ob: T.bkl[:, ob:ob + 144], ["bm%d%d" % (t, c), "ba%d%d" % (t, c)], ["bl%d%d" % (t, c)], -1, 600)
+        for c in range(NC):
+            km, parts, rk = keep[c]
+            ob = 144 * (NC * t + c); oy = 256 * t + 128 * c; k = slot("xx", 2); ox = 48 * k; om = 256 * km; bl = "bl%d%d" % (t, c)
+            V(16, lambda e, T, B, ox=ox, om=om, ob=ob: e.tensor_tensor(T.xx[:, ox + 8:ox + 16], T.msc[:, om + 15:om + 128:16], T.bkl[:, ob + 128:ob + 136], ALU.max), ["mm%d" % km, bl], ["xm%d" % k])
+            V(16, lambda e, T, B, ox=ox, om=om, ob=ob: e.tensor_tensor(T.xx[:, ox + 16:ox + 24], T.msc[:, om + 143:om + 256:16], T.bkl[:, ob + 136:ob + 144], ALU.add), ["ms%d" % km, bl], ["xt%d" % k])
+            A(8, lambda e, T, B, ox=ox: e.activation(T.xx[:, ox + 32:ox + 40], T.xx[:, ox + 8:ox + 16], AF.Exp, scale=-0.0078125), ["xm%d" % k], ["xf%d" % k])
+            V(16, lambda e, T, B, ox=ox: e.tensor_tensor(T.xx[:, ox:ox + 8], T.xx[:, ox + 16:ox + 24], T.xx[:, ox + 32:ox + 40], ALU.mult), ["xt%d" % k, "xf%d" % k], ["xs%d" % k])
+            ps = P(512, lambda T, B, ox=ox: [(B[0:16, :128], T.xx[:, ox:ox + 16], T.i32[:], True, True)], ["xm%d" % k, "xs%d" % k, "i32"])
+            A(128, lambda e, T, B, oy=oy: e.activation(T.mss[0:16, oy:oy + 128], B[0:16, :128], AF.Copy), [], ["mo%d%d" % (t, c)], ps)
+            ps = P(512, lambda T, B, oy=oy: [(B[:, :128], T.repm[0:16, :], T.mss[0:16, oy:oy + 128], True, True)], ["mo%d%d" % (t, c), "repm"])
+            A(128, lambda e, T, B, k=k: e.activation(T.fa[:, 128 * k:128 * k + 128], B[:, :128], AF.Exp, bias=HB, scale=-0.0078125), [], ["fa%d" % k], ps)
+            ps = P(1536, lambda T, B, ob=ob, parts=parts: parts(T, B, [(T.bkl, ob)]), rk + [bl])
+            V(128, lambda e, T, B, k=k, oy=oy: e.tensor_tensor(T.yas[:, oy:oy + 128], B[:, :128], T.fa[:, 128 * k:128 * k + 128], ALU.mult), ["fa%d" % k], ["yo%d%d" % (t, c)], ps)
+            op("S", [("n", 60)], lambda e, T, B, X, oy=oy: [e.dma_start(T.ya[:, oy:oy + 128], T.yas[:, oy:oy + 128])], ["yo%d%d" % (t, c)], [], sem="stored", lat=2500)
+            ops[-1]["due"] = RO - 1 - t
+        if t >= RO - 2:
+            lo_, hi_ = (0, 768) if t == RO - 2 else (768, 1024)
+            op("S", [("n", 120)], lambda e, T, B, X, a=lo_, b=hi_: [e.dma_start(T.ys[:, a:b], T.mss[0:8, a:b]), e.dma_start(T.ym[:, a:b], T.mss[8:16, a:b])],
+               ["mo%d%d" % (x, c) for x in range(lo_ // 256, hi_ // 256) for c in range(NC)], [], sem="stored", lat=2200)
+    lastw, readers, acc = {}, {}, {}
+    for i, o in enumerate(ops):
+        d = set()
+        for k in o["r"]:
+            if k in lastw: d.add(lastw[k])
+        for k in o["w"]:
+            if k in lastw: d.add(lastw[k])
+            d.update(readers.get(k, []))
+        if o["ps"] is not None:
+            d.update(acc.get(o["ps"], [])); acc.setdefault(o["ps"], []).append(i)
+        for k in o["r"]: readers.setdefault(k, []).append(i)
+        for k in o["w"]: lastw[k] = i; readers[k] = []
+        d.discard(i); o["dep"] = sorted(d)
+        o["tiles"] = sorted(set(tile_of(k) for k in o["r"] + o["w"] if tile_of(k)) | ({("ps", o["ps"])} if o["ps"] is not None else set()))
+    return ops
+
+
+def after(o, M):
+    if o["sem"] is None: return M["hop"]
+    return o["lat"] if o["lat"] >= 0 else M["net"] - o["lat"]
+
+
+def plan(ops, M, seed, look=0.5, noise=0.03, onv=(), per=32000, off=20000, infl=12000, moves=()):
+    n = len(ops); rng = np.random.default_rng(seed)
+    succ = [[] for _ in ops]
+    for i, o in enumerate(ops):
+        for d in o["dep"]: succ[d].append(i)
+    du = [[dur(a[1], M) for a in o["alts"]] for o in ops]
+    pr = [0.0] * n
+    for i in range(n - 1, -1, -1):
+        o = ops[i]
+        pr[i] = du[i][0] + after(o, M) + max([pr[j] for j in succ[i]], default=o.get("due", 0) * per - off if o.get("due") else 0.0)
+        if o["sem"] and o["sem"][:2] == "rQ": pr[i] += infl
+    for i, o in enumerate(ops):
+        if "init" in o: pr[i] = 600 + [pr[j] for j, x in enumerate(ops) if o["init"] in x["tiles"]][0]
+    pr = [p + noise * 20000 * rng.random() for p in pr]
+    pick = [0 if len(o["alts"]) == 1 else (1 if o["role"] in onv else 0) for o in ops]
+    for i, m, d in moves:
+        if not m: pick[i] = 1 - pick[i]
+        for j in range(i, min(n, i + m)): pr[j] += 1000.0 * d
+    users = {}
+    for i, o in enumerate(ops):
+        for k in o["tiles"]: users.setdefault(k, []).append(i)
+    last = {p: [[] for _ in range(m)] for p, m in POOLS.items()}
+    held = {p: [0] * m for p, m in POOLS.items()}
+    live = {p: np.zeros(n + 1, int) for p in POOLS}
+    for k, u in users.items(): live[k[0]][u[0]:u[-1] + 1] += 1
+    for i, o in enumerate(ops):
+        if "init" in o: held[o["init"][0]][o["init"][1]] = 1; live[o["init"][0]][:i + 1] += 1
+    cur = 0
+    free = {e: 0.0 for e in "VAPGS"}; left = [len(o["dep"]) for o in ops]; avail = [0.0] * n; fin = [0.0] * n
+    where = {}; prev = {}; since = {}; order = []; extra = {}; placed = 0
+    ready = [i for i in range(n) if not left[i]]
+    while ready:
+        cand = []; spot = {}; most = {}
+        while placed >> cur & 1: cur += 1
+        for p in POOLS:
+            most[p] = np.maximum.accumulate(live[p][cur:])
+            fr = [(max([fin[j] for j in last[p][x]], default=-1e3), x) for x in range(POOLS[p]) if not held[p][x]]
+            spot[p] = (len(fr),) + min(fr) if fr else (0, 0, 0)
+        for i in ready:
+            o = ops[i]; r = avail[i]; ok = True
+            for k in o["tiles"]:
+                if k in where: r = max(r, since[k])
+                elif not spot[k[0]][0] or (users[k][0] > cur and most[k[0]][users[k][0] - 1 - cur] >= POOLS[k[0]]): ok = False
+                else: r = max(r, spot[k[0]][1] + M["hop"])
+            if ok: cand.append((max(r, free[o["alts"][pick[i]][0]]), i))
+        if not cand: return None
+        t0 = min(c[0] for c in cand)
+        now = max((c for c in cand if c[0] <= t0 + 1.0), key=lambda c: pr[c[1]])
+        eng = ops[now[1]]["alts"][pick[now[1]]][0]
+        soon = [c for c in cand if ops[c[1]]["alts"][pick[c[1]]][0] == eng and c[0] < t0 + look * du[now[1]][0] and pr[c[1]] > pr[now[1]] + 2000]
+        if soon: now = max(soon, key=lambda c: pr[c[1]] - 4 * (c[0] - t0))
+        st, i = now; o = ops[i]; x = pick[i]; e = o["alts"][x][0]
+        fin[i] = free[e] = st + du[i][x]; extra[i] = []
+        if "init" in o: held[o["init"][0]][o["init"][1]] = 0; last[o["init"][0]][o["init"][1]] = [i]; live[o["init"][0]][:i + 1] -= 1
+        for k in o["tiles"]:
+            p = k[0]
+            if k not in where:
+                b = spot[p][2]; where[k] = b; prev[k] = last[p][b]; since[k] = spot[p][1] + M["hop"]
+                last[p][b] = users[k]; held[p][b] = len(users[k])
+                live[p][:users[k][0]] += 1
+            held[p][where[k]] -= 1; extra[i] += prev[k]
+            if not held[p][where[k]]: live[p][:users[k][-1] + 1] -= 1
+        order.append((i, x)); ready.remove(i); placed |= 1 << i
+        for j in succ[i]:
+            avail[j] = max(avail[j], fin[i] + after(o, M)); left[j] -= 1
+            if not left[j]: ready.append(j)
+    return order, where, extra, max(fin[i] + after(ops[i], M) for i in range(n))
+
+
+def place(ops, order, M):
+    users = {}
+    for i, o in enumerate(ops):
+        for k in o["tiles"]: users.setdefault(k, []).append(i)
+    last = {p: [[] for _ in range(m)] for p, m in POOLS.items()}; held = {p: [0] * m for p, m in POOLS.items()}
+    for o in ops:
+        if "init" in o: held[o["init"][0]][o["init"][1]] = 1
+    free = {e: 0.0 for e in "VAPGS"}; done = {}; where = {}; prev = {}; extra = {}
+    for i, x in order:
+        o = ops[i]; e, cost, _ = o["alts"][x]; extra[i] = []
+        if "init" in o: held[o["init"][0]][o["init"][1]] = 0; last[o["init"][0]][o["init"][1]] = [i]
+        for k in o["tiles"]:
+            p = k[0]
+            if k not in where:
+                b = min((max([done[j] for j in last[p][y]], default=0.0), y) for y in range(POOLS[p]) if not held[p][y])[1]
+                where[k] = b; prev[k] = last[p][b]; last[p][b] = users[k]; held[p][b] = len(users[k])
+            held[p][where[k]] -= 1; extra[i] += prev[k]
+        free[e] = max([free[e]] + [done[d] for d in o["dep"] + extra[i]]) + dur(cost, M); done[i] = free[e] + after(o, M)
+    return order, where, extra, max(done.values())
+
+
+def replay(ops, sched, M):
+    order, _, extra, _ = sched
+    free = {e: 0.0 for e in "VAPGS"}; done = {}; busy = {e: 0.0 for e in "VAPGS"}
+    for i, x in order:
+        o = ops[i]; e, cost, _ = o["alts"][x]
+        st = max([free[e]] + [done[d] for d in o["dep"] + extra.get(i, [])])
+        d = dur(cost, M); free[e] = st + d; busy[e] += d; done[i] = free[e] + after(o, M)
+    return max(done.values()), busy
+
+
+PLAN = (65, 0.0, 0.0, ("ovg1", "hvg1", "hdd", "odd", "ocs"), 26000, 17000, 14000,
+        [(397, 0, 0), (76, 19, -8), (157, 24, 2), (130, 20, -2), (344, 21, -4), (124, 6, -4), (320, 4, 8), (191, 19, 2), (692, 9, 8), (751, 0, 0), (866, 14, 1), (576, 13, -1), (162, 2, 2), (822, 9, -2), (847, 1, 8), (532, 16, -2), (877, 4, -1), (369, 6, 8)])
+ORDER = """1 2 6 4 3 7 5 9 12 13 10 8 11 72 71 66 60 70 63 15 77 75 73 90 61 21 92 17 65 14 19 18 76 62 20 25 91 37 158 100 22 30 27 31 44 43 82 32 78 79 29 26 159 87 38 160 83 28 67 86 -163 81 164 101 162 84 68 80 161 64 46 102 103 23 93 39 40 16 52 51 165 74 33 50 41 42 34 89 53 55 35 48 56 24 54 166 -105 47 167 36 57 106 49 58 168 104 107 45 169 170 171 172 173 174 175 88 176 59 85 177 178 179 108 109 180 181 110 69 182 111 183 112 185 113 114 115 116 117 118 119 120 184 -122 123 124 127 186 187 -249 -360 188 201 250 121 94 189 96 190 95 97 98 361 191 254 192 362 251 125 126 128 -302 -217 193 129 130 194 218 195 -196 197 99 303 131 232 304 132 233 133 219 134 135 364 -239 146 363 136 140 220 137 204 198 147 -138 264 265 222 205 253 306 365 366 367 368 252 139 143 -305 -211 248 221 369 216 370 307 371 372 373 308 255 223 266 374 256 375 261 376 377 153 -206 378 379 224 309 229 262 310 230 311 380 -271 -382 263 381 234 267 383 312 384 269 386 313 272 268 274 270 257 314 385 273 225 315 387 316 275 277 317 258 259 318 226 319 231 320 -451 227 260 321 322 452 388 199 202 203 278 456 144 237 240 389 390 324 207 -562 325 235 238 323 326 391 242 453 276 392 241 393 279 563 148 394 236 243 395 466 396 -504 328 327 245 397 145 330 398 141 246 208 467 200 291 564 228 505 212 209 329 292 399 506 331 213 244 566 332 -473 333 406 210 214 293 247 334 507 419 142 151 294 335 215 149 336 508 565 567 420 154 568 454 337 155 403 295 338 424 156 152 421 569 407 281 339 280 296 282 157 150 283 -422 340 341 284 570 285 455 450 342 288 -413 286 297 287 298 423 408 571 572 289 573 509 299 574 418 348 468 300 575 434 457 290 425 435 576 510 577 511 349 512 301 578 400 579 458 463 426 580 -441 436 513 459 464 431 432 -355 514 465 515 401 343 350 404 581 460 516 471 582 517 433 518 583 -584 519 585 469 427 437 520 586 521 522 470 461 588 462 523 472 524 474 475 525 -526 478 476 442 444 439 477 527 402 587 528 479 440 445 438 530 443 345 480 346 590 589 591 428 405 608 447 531 592 411 409 609 344 448 429 347 -653 593 430 594 412 595 529 532 -707 654 596 597 410 481 533 414 534 757 598 446 758 351 416 449 353 599 -621 759 493 610 535 415 536 708 494 600 537 495 601 417 538 496 354 761 760 356 539 540 550 497 357 541 498 501 499 352 482 542 709 622 483 543 551 484 485 358 605 500 502 658 486 359 655 762 547 668 503 652 710 487 711 488 636 763 764 490 489 669 765 656 657 -557 491 766 712 637 713 714 623 715 492 620 -675 -643 659 716 660 767 768 625 717 839 624 769 718 770 626 771 719 602 661 627 665 772 720 670 666 544 773 721 774 662 722 638 663 775 776 723 628 724 777 633 667 725 -615 726 671 673 634 727 778 779 603 545 552 672 629 -780 635 781 728 807 676 630 729 606 677 782 664 631 674 730 548 784 644 678 632 679 646 639 641 647 645 680 607 840 642 640 681 -808 841 648 731 682 795 618 842 649 809 813 845 604 810 611 783 650 549 683 745 616 613 844 553 612 555 619 786 843 614 696 695 697 651 556 732 846 560 746 546 617 698 684 847 554 558 685 559 812 699 686 811 700 687 733 787 855 848 849 735 823 824 796 814 852 688 561 689 856 815 850 857 -802 820 701 690 691 702 706 821 853 734 703 -862 785 854 692 851 816 817 818 693 694 858 860 822 704 792 867 833 865 828 -830 705 861 825 797 859 866 863 826 831 864 868 869 752 736 827 829 832 788 834 737 819 836 789 870 742 738 793 794 798 739 835 837 838 790 743 791 740 747 799 741 744 805 806 800 801 803 748 755 750 882 804 753 884 749 883 871 873 885 890 886 887 872 756 874 875 876 893 751 754 888 877 889 891 892 878 879 880 881"""
+CACHE = {}
+
+
+def rank_program(g, core, T, topo):
+    rank = T.rank_of(core)
+    if rank is None:
+        return
+    if "ops" not in CACHE:
+        CACHE["ops"] = build(); order = [(abs(int(v)) - 1, int(int(v) < 0)) for v in ORDER.split()]
+        CACHE["plan"] = place(CACHE["ops"], order, REF) if order else plan(CACHE["ops"], REF, *PLAN)
+        CACHE["calls"] = build(CACHE["plan"][1])
+    ops = CACHE["ops"]; order, where, extra, _ = CACHE["plan"]
+    N = len(T.cores); peer = lambda k: T.cores[(rank + k) % N]
+    sent = [0]; arrive = {}
+
+    def send(name, src, dst, to):
+        rid, pid, _ = topo.addr(peer(to))
+        g.remote_dma(dst, src, T.sem[name], T.sem.sent, pid, rid, topo.mask(core, peer(to)))
+        sent[0] += len(topo.engines(core, peer(to))); arrive[name] = len(topo.engines(peer(-to), core))
+        return []
+
+    def share(src, dst, t):
+        e = topo.engines(src, dst); h = len(e) // 2; q = h // 2
+        return (e[:h], e[h:h + q], e[h + q:])[t - 1]
+
+    def tokens():
+        tr = []
+        for t in range(1, RO):
+            rid, pid, _ = topo.addr(peer(t)); e = share(core, peer(t), t)
+            tr.append(RemoteDMATransfer(dst_ids=[DstId(rid=rid, pnc=pid)], dma_engine_mask=sum(1 << x for x in e), remote_sem=T.sem.rtok,
+                                        src=T.toku[:, 16 * t:16 * t + 16], dst=T.tokl[:, 16 * t:16 * t + 16]))
+            sent[0] += len(e)
+        g.remote_dma_fused(tr, local_sem=T.sem.sent)
+        arrive["rtok"] = sum(len(share(peer(-t), core, t)) for t in range(1, RO))
+        return []
+
+    X = {"send": send, "tokens": tokens}
+    Q = {"V": g.vector, "A": g.scalar, "P": g.tensor, "G": g, "S": g.sync}
+    count = {}; mark = {}; waited = {e: {} for e in Q}
+    for i, x in order:
+        o = ops[i]; e, _, fn = CACHE["calls"][i]["alts"][x]
+        need = {}
+        for d in o["dep"] + extra.get(i, []):
+            s, v = mark[d]; need[s] = max(need.get(s, 0), v)
+        for s, v in need.items():
+            if waited[e].get(s, 0) < v:
+                Q[e].wait_ge(T.sem[s], v); waited[e][s] = v
+        B = T["pb%d" % where[("ps", o["ps"])]] if o["ps"] is not None else None
+        ins = fn(Q[e], T, B, X)
+        s = o["sem"] or "c" + e
+        if o["sem"] and e == "G":
+            count[s] = arrive[s]
+        for c in ins:
+            step = 16 if o["sem"] else 1
+            c.then_inc(T.sem[s], step); count[s] = count.get(s, 0) + step
+        mark[i] = (s, count.get(s, 0))
+    count["sent"] = sent[0]
+    for s, v in count.items():
+        if waited["G"].get(s, 0) < v: g.wait_ge(T.sem[s], v)

@@ -1,39 +1,41 @@
 import numpy as np
 from concourse.bass import DstId, RemoteDMATransfer
-from concourse.mybir import AluOpType as ALU, AxisListType as AX, ActivationFunctionType as AF
+from concourse.mybir import AluOpType as ALU, ActivationFunctionType as AF
 
 W, RO, NC = 3072, 4, 2
-NK, NV, NSO, NQ, NS1, NR, NT = 5, 4, 6, 5, 4, 3, 6
+POOLS = {"kg": 5, "vg": 4, "so": 6, "qd": 2, "qh": 2, "sg": 2, "s1": 4, "rb": 2, "fr": 2, "rd": 6, "ofk": 6, "ks": 4, "msc": 6, "tt": 2, "cy": 6, "yt": 2,
+         "xx": 2, "ps": 8}
 PEN, HB = 4096.0, 28.0
+OFS = 1024
 F32, BF, F16, I32, U16 = "float32", "bfloat16", "float16", "int32", "uint16"
 SB = lambda n, d: ("sbuf", [128, n], d)
+TILES = {"kg": ("kg", 2048, BF), "vg": ("vg", 2048, BF), "so": ("so", 2048, F32), "qd": ("qd", 1024, BF), "qh": ("qh", 1024, F16), "sg": ("sg", 256, BF), "s1": ("s1", 256, F16),
+         "rb": ("rb", 512, F32), "fr": ("fr", 128, F16), "fm": ("rd", 128, F16), "inv": ("rd", 128, BF), "ee": ("rd", 128, F32), "hi": ("rd", 128, BF),
+         "lo": ("rd", 128, BF), "ofv": ("rd", 128, U16), "ofk": ("ofk", 128, U16), "ks": ("ks", 128, F32), "msc": ("msc", 256, F32),
+         "tf": ("tt", 64, F32), "mi": ("cy", 8, I32), "fq": ("cy", 8, BF), "ofc": ("cy", 8, U16), "yt": ("yt", 32, F32),
+         "zt": ("xx", 128, F32), "xx": ("xx", 16, F32), "fa": ("xx", 128, F32)}
 SCRATCH = {
-    "hks": SB(W, BF), "vvs": SB(W, BF), "fws": SB(2816, BF), "bws": SB(W, BF), "num": SB(W, F32),
-    "curi": SB(16, I32), "toki": SB(64, I32), "toku": SB(64, U16), "tokl": SB(64, U16), "th16": SB(128, I32),
-    "lst": SB(5 * NC * 24, U16), "qcs": SB(RO * NC * 256, BF), "qcl": SB(RO * NC * 256, BF),
+    "hks": SB(W, BF), "vvs": SB(W, BF), "fws": SB(2816, BF), "bws": SB(W, BF), "nnum": SB(W, F32),
+    "curi": SB(16, I32), "toki": SB(64, I32), "toku": SB(64, U16), "tokl": SB(64, U16), "thi": SB(256, I32), "thq": SB(256, F16), "thl": SB(256, BF),
+    "lsl": SB((RO + 1) * NC * 8, U16), "lso": SB(RO * NC * 8, U16), "nq": SB((RO + 1) * NC * 640, F16),
+    "crs": SB(RO * NC * 128, BF), "crl": SB(RO * NC * 128, BF),
     "bks": SB(RO * NC * 144, F32), "bkl": SB(RO * NC * 144, F32), "yas": SB(1024, F32), "mss": SB(1024, F32),
-    "kg": SB(NK * 2048, BF), "vg": SB(NV * 2048, BF), "so": SB(NSO * 2048, F32), "qd": SB(NQ * 1024, BF),
-    "sg": SB(2 * 512, BF), "s1": SB(NS1 * 512, F16), "rb": SB(NR * 512, F32), "rd": SB(2 * 512, BF),
-    "fg": SB(2 * 128, F32), "fr": SB(2 * 128, F32), "fm": SB(NT * 128, F32), "dd": SB(NT * 128, BF),
-    "inv": SB(NT * 128, BF), "ofk": SB(NT * 128, U16), "ofv": SB(NT * 128, U16), "ofc": SB(2 * 8, U16),
-    "ks": SB(NT * 128, F32), "ee": SB(NT * 128, F32), "msc": SB(NT * 256, F32), "hi": SB(NT * 128, BF),
-    "lo": SB(NT * 128, BF), "fa": SB(2 * 128, F32), "yt": SB(NT * 32, F32),
-    "ti": SB(NT * 32, I32), "tf": SB(NT * 64, F32), "xx": SB(2 * 48, F32),
-    "ci": SB(16, I32), "cf": SB(32, F32), "r128": SB(128, F32), "ones": SB(128, F32), "i32": SB(128, F32),
-    "idf": SB(128, BF), "inn": SB(128, BF), "in2": SB(256, BF), "a16": SB(16, F32), "a16n": SB(16, BF),
-    "selt": SB(16, F16), "selt2": SB(32, F16), "selw": SB(16, BF), "b16": SB(16, F32), "dw": SB(480, F16),
-    "dinv": SB(128, BF), "rsel": SB(2048, BF), "pvm": SB(512, F32), "ru4": SB(512, BF), "msk": SB(512, BF),
-    "rum": SB(256, F32), "cl": SB(256, F16), "cr": SB(1536, F16), "g8": SB(8, F32), "m16": SB(128, F32),
-    "ofq": SB(8, U16), "ofr": SB(2, U16), "rq": SB(8, I32), "repm": SB(128, F32), "cfr": SB(128, F32),
-    "cfb": SB(384, BF), "one1": SB(128, BF), "tmp": SB(128, BF),
+    "ci": SB(16, I32), "cf": SB(32, F32), "rr": SB(160, F32), "ones": SB(512, BF), "i32": SB(128, F32), "idh": SB(128, BF),
+    "inn": SB(128, BF), "inp": SB(128, BF), "a16": SB(16, F32), "a16p": SB(16, BF), "b16p": SB(16, BF), "selw": SB(64, BF),
+    "zw": SB(320, BF), "yh": SB(288, BF), "dq": SB(192, BF), "cb": SB(8, F16), "sel0": SB(128, F32), "rsel": SB(2048, BF),
+    "m16": SB(272, F32), "rk": SB(272, F32), "c9": SB(16, F32), "zz": SB(512, BF), "ofq": SB(8, U16), "ofr": SB(2, U16),
 }
+for _k, (_p, _n, _d) in TILES.items():
+    SCRATCH[_k] = SB(POOLS[_p] * _n, _d)
 for _b in range(8):
     SCRATCH["pb%d" % _b] = ("psum", [128, 512], F32)
 LOADS = ["cur", "tok", "fwA", "hkA", "th", "hkB", "bwA", "vvA", "fwB", "bwB", "vvB"]
-SEMAPHORES = (["cV", "cA", "cP", "cG", "sent", "stored", "rtok"] + ["l" + n for n in LOADS]
-              + ["r%s%d%d" % (k, t, c) for k in "LQB" for t in range(RO) for c in range(NC)])
+BYDMA = [k + "%d%d" % (t, c) for k in "oh" for t in range(RO) for c in range(NC) if k == "h"]
+WHOLE = ()
+SEMAPHORES = (["cV", "cA", "cP", "cG", "sent", "stored", "rtok"] + ["l" + n for n in LOADS] + ["d" + n for n in BYDMA]
+              + ["r%s%d%d" % (k, t, c) for k in "LNB" for t in range(RO) for c in range(NC)] + ["rC%d%d" % (t, c) for t in range(RO - 1) for c in range(NC)])
 
-REF = {"c": 1.0, "p": 0.5, "g": 1.56, "s": 3.8, "hop": 150.0, "net": 3000.0, "o": 30.0}
+REF = {"c": 1.0, "p": 0.6, "g": 1.56, "s": 3.8, "hop": 200.0, "net": 4000.0, "o": 30.0}
 
 
 def dur(cost, M):
@@ -47,60 +49,48 @@ def dur(cost, M):
     return tot
 
 
-POOLS = {"kg": NK, "vg": NV, "so": NSO, "qd": NQ, "sg": 2, "s1": NS1, "rb": NR, "rd": 2, "fg": 2, "rd_": NT, "ofk": NT, "ofc": 2,
-         "ks": NT, "msc": NT, "yt": NT, "tt": NT, "xx": 2, "ps": 8}
-OF = {"kg": ("kg", 1), "vg": ("vg", 1), "so": ("so", 2), "fr": ("fg", 0), "mm": ("msc", 0), "ms": ("msc", 0)}
-OF.update({k: (k, 0) for k in ("qd", "sg", "s1", "rb", "rd", "fg", "ofk", "ofc", "ks", "yt")})
-OF.update({k: ("rd_", 0) for k in ("fm", "dd", "inv", "ee", "hi", "lo", "ofv")})
-OF.update({k: ("tt", 0) for k in ("tia", "tib", "tfa", "tfb", "tfc")})
-OF.update({k: ("xx", 0) for k in ("xm", "xt", "xf", "xs", "fa")})
+STAGES = [("o", 0), ("o", 0), ("o", -1), ("h", 1), ("o", 1), ("h", 2), ("b", 3)]
 
 
-def tile_of(key):
-    for p in OF:
-        d = key[len(p):].rstrip("x")
-        if key.startswith(p) and d.isdigit(): return OF[p][0], int(d[:len(d) - OF[p][1]])
-    return None
-
-
-def build(where=None):
+def build(where=None, stages=STAGES):
     ops, ring, who = [], {}, ["s"]
 
-    def op(eng, cost, fn, r, w, ps=None, new=False, sem=None, lat=0.0, alt=None):
-        ops.append({"alts": [(eng, cost, fn)] + (alt or []), "r": r, "w": w, "ps": ps, "new": new, "sem": sem, "lat": lat})
+    def op(eng, cost, fn, r, w, ps=None, sem=None, lat=0.0, alt=None):
+        ops.append({"alts": [(eng, cost, fn)] + (alt or []), "r": r, "w": w, "ps": ps, "sem": sem, "lat": lat})
 
-    def slot(name, n):
-        k = ring.get(name, 0); ring[name] = k + 1
-        return k if where is None else where[(name, k)]
+    def tiles(*names):
+        p = TILES[names[0]][0]; k = ring.get(p, 0); ring[p] = k + 1
+        x = k if where is None else where[(p, k)]
+        return [((p, k, s), lambda T, a=0, b=None, st=1, s=s, n=TILES[s][1], rows=slice(None): T[s][rows, n * x + a:n * x + (n if b is None else b):st]) for s in names]
 
-    def tile():
+    def bank():
         k = ring.get("ps", 0); ring["ps"] = k + 1
         return k
 
     V = lambda n, fn, r, w, ps=None: op("V", [("v", n)], lambda e, T, B, X: [fn(e, T, B)], r, w, ps)
     A = lambda n, fn, r, w, ps=None: op("A", [("v", n)], lambda e, T, B, X: [fn(e, T, B)], r, w, ps)
     G = lambda n, fn, r, w: op("G", [("n", 170 + 2.0 * n)], lambda e, T, B, X: [fn(e, T)], r, w)
+    VG = lambda n, fn, r, w, kind="g": op("V", [(kind, n)], lambda e, T, B, X: [fn(e, T)], r, w)
 
-    def gather(n, out, win, off, r, w):
+    def gather(n, out, win, off, r, w, role):
         op("A", [("g", n)], lambda e, T, B, X: [e.activation(out(T), win(T).indirect(off(T)), AF.Copy)], r, w,
            alt=[("V", [("g", n)], lambda e, T, B, X: [e.tensor_copy(out(T), win(T).indirect(off(T)))])])
-        ops[-1]["role"] = who[0] + w[0][:2] + (w[0][-1] if n > 128 else "")
+        ops[-1]["role"] = who[0] + role
 
-    def P(n, mms, r, new=True, ps=None):
-        k = tile() if ps is None else ps
-        op("P", [("p", n)], lambda e, T, B, X: [e.matmul(*m) for m in mms(T, B)], r, [], k, new)
+    def P(n, mms, r, ps=None):
+        k = bank() if ps is None else ps
+        op("P", [("p", n)], lambda e, T, B, X: [e.matmul(*m) for m in mms(T, B)], r, [], k)
         return k
 
-    def load(q, name, fn, w, ns):
-        op(q, [("n", 60)], lambda e, T, B, X: fn(e, T), [], w, sem="l" + name, lat=ns)
+    def load(q, name, fn, w, ns, n=1):
+        op(q, [("n", 60 * n)], lambda e, T, B, X: fn(e, T), [], w, sem="l" + name, lat=ns)
     load("S", "cur", lambda e, T: [e.dma_start(T.curi[:], T.cur[:])], ["curi"], 2000)
     load("S", "fwA", lambda e, T: [e.dma_start(T.fws[:, :2048], T.fw[:, :2048])], ["fwA"], 4500)
     load("A", "tok", lambda e, T: [e.dma_start(T.toki[:], T.tok[:])], ["toki"], 2000)
     load("A", "hkA", lambda e, T: [e.dma_start(T.hks[:, :2304], T.hk[:, :2304])], ["hkA"], 6000)
-    load("S", "th", lambda e, T: [e.dma_start(T.th16[8 * h:8 * h + 8, 64 * c:64 * c + 64], T.th[:, 128 * c + 64 * h:128 * c + 64 * h + 64])
-                                  for h in range(2) for c in range(2)], ["th16"], 3000)
     load("S", "hkB", lambda e, T: [e.dma_start(T.hks[:, 2304:], T.hk[:, 2304:])], ["hkB"], 7000)
     load("S", "bwA", lambda e, T: [e.dma_start(T.bws[:, :2304], T.bw[:, :2304])], ["bwA"], 9500)
+    load("S", "th", lambda e, T: [e.dma_start(T.thi[x:x + 1, 128 * h:128 * h + 128], T.th[h::2, 32 * x:32 * x + 32]) for x in range(8) for h in range(2)], ["thi"], 3000, 16)
     load("S", "vvA", lambda e, T: [e.dma_start(T.vvs[:, :2304], T.vv[:, :2304])], ["vvA"], 12000)
     load("S", "fwB", lambda e, T: [e.dma_start(T.fws[:, 2048:], T.fw[:, 2048:2816])], ["fwB"], 13000)
     load("S", "bwB", lambda e, T: [e.dma_start(T.bws[:, 2304:], T.bw[:, 2304:])], ["bwB"], 14000)
@@ -108,272 +98,252 @@ def build(where=None):
 
     IO = dict(allow_small_or_imprecise_dtypes=True)
     G(1, lambda e, T: e.iota(T.ci[:, 0:1], [[1, 1]], 0, 1), [], ["ci0"])
-    G(768, lambda e, T: e.iota(T.num[:, :768], [[1, 768]], 0, 0, **IO), [], ["num0"])
-    for k in range(1, 4):
-        if k == 1: A(768, lambda e, T, B: e.activation(T.num[:, 768:1536], T.num[:, :768], AF.Identity, bias=768.0), ["num0"], ["num1"])
-        else: G(768, lambda e, T, k=k: e.iota(T.num[:, 768 * k:768 * k + 768], [[1, 768]], 768 * k, 0, **IO), [], ["num%d" % k])
-    NUMS = lambda n: ["num%d" % k for k in range((n + 767) // 768)]
-    r128 = lambda T: T.num[:, :128]
+    G(512, lambda e, T: e.iota(T.nnum[:, :512], [[-1, 512]], OFS, 0, **IO), [], ["num0"])
+    A(512, lambda e, T, B: e.activation(T.nnum[:, 512:1024], T.nnum[:, :512], AF.Identity, bias=-512.0), ["num0"], ["num1"])
+    A(1024, lambda e, T, B: e.activation(T.nnum[:, 1024:2048], T.nnum[:, :1024], AF.Identity, bias=-1024.0), ["num0", "num1"], ["num2"])
+    G(160, lambda e, T: e.iota(T.rr[:], [[1, 160]], 0, 0, **IO), [], ["rr"])
+    G(1024, lambda e, T: e.iota(T.nnum[:, 2048:], [[-1, 1024]], OFS - 2048, 0, **IO), [], ["num3"])
     ci = lambda T, k: T.ci[:, k:k + 1]
     cf = lambda T, k: T.cf[:, k:k + 1]
+    AND, SHR, EQ, MUL, ADD = ALU.bitwise_and, ALU.arith_shift_right, ALU.is_equal, ALU.mult, ALU.add
 
-    def bits(k, a, opa, b=None, opb=None):
-        if b is None: V(1, lambda e, T, B: e.tensor_scalar(ci(T, k), ci(T, 0), a, None, opa), ["ci0"], ["ci%d" % k])
-        else: V(1, lambda e, T, B: e.tensor_scalar(ci(T, k), ci(T, 0), a, b, opa, opb), ["ci0"], ["ci%d" % k])
-        V(1, lambda e, T, B: e.tensor_copy(cf(T, k), ci(T, k)), ["ci%d" % k], ["cf%d" % k])
-    AND, SHR = ALU.bitwise_and, ALU.arith_shift_right
-    bits(1, 15, AND); bits(2, 4, SHR); bits(3, 7, AND); bits(4, 4, SHR, 3, AND); bits(5, 3, SHR); bits(6, 1, AND)
+    BITS = ((0, 15), (4, 7), (0, 7), (4, 1), (5, 3), (3, 1), (0, 1))
+    op("V", [("v", 1)] * 7, lambda e, T, B, X: [e.tensor_scalar(ci(T, k + 1), ci(T, 0), a, b, SHR, AND) for k, (a, b) in enumerate(BITS)], ["ci0"], ["ci1"])
+    V(8, lambda e, T, B: e.tensor_copy(T.cf[:, 0:8], T.ci[:, 0:8]), ["ci0", "ci1"], ["cf%d" % k for k in range(8)])
 
-    def col(k, a, s1, s2, o0, o1, r):
-        sc = lambda T, s: cf(T, s[0]) if isinstance(s, list) else s
-        V(1, lambda e, T, B: e.tensor_scalar(cf(T, k), cf(T, a), sc(T, s1), sc(T, s2), *([o0, o1] if o1 is not None else [o0])), ["cf%d" % a] + ["cf%d" % j for j in r], ["cf%d" % k])
-    V(1, lambda e, T, B: e.tensor_copy(cf(T, 0), ci(T, 0)), ["ci0"], ["cf0"])
-    col(10, 1, 15.0, -2048.0, ALU.is_equal, ALU.mult, [])
-    col(8, 1, -4096.0, 63488.0, ALU.mult, ALU.add, [])
-    col(11, 8, [10], None, ALU.add, None, [10])
-    col(12, 3, 0.0, 1000.0, ALU.is_equal, ALU.mult, [])
-    col(13, 1, -1.0, [12], ALU.add, ALU.add, [12])
-    col(14, 0, -1.0, [12], ALU.add, ALU.add, [12])
-    col(15, 3, 7.0, -HB, ALU.is_equal, ALU.mult, [])
-    col(16, 1, 8.0, [2], ALU.mult, ALU.add, [2])
-    op("V", [], lambda e, T, B, X: [], [], [])
-    col(18, 6, -31.0, 1.0, ALU.mult, ALU.mult, [])
-    col(19, 1, 32.0, [18], ALU.mult, ALU.add, [18])
-    col(20, 2, 2.0, [19], ALU.mult, ALU.add, [19])
+    def col(k, a, s1, s2, o0, o1):
+        sc = lambda T: cf(T, s2[0]) if isinstance(s2, list) else s2
+        r = ["cf%d" % j for j in [a] + (s2 if isinstance(s2, list) else [])]
+        if o0 == MUL: A(1, lambda e, T, B: e.activation(cf(T, k), cf(T, a), AF.Identity, bias=sc(T), scale=s1), r, ["cf%d" % k])
+        else: V(1, lambda e, T, B: e.tensor_scalar(cf(T, k), cf(T, a), s1, sc(T), o0, o1), r, ["cf%d" % k])
+    col(8, 1, -4096.0, 17 * 4096.0 + OFS, MUL, ADD)
+    col(9, 1, 15.0, -0.5, EQ, ADD)
+    col(10, 4, 1000.0, [1], MUL, ADD)
+    col(11, 5, 16.0, [10], MUL, ADD)
+    col(12, 3, 0.0, 1000.0, EQ, MUL)
+    col(26, 12, 1.0, -1.0, MUL, ADD)
+    col(13, 10, 1.0, [26], MUL, ADD)
+    col(14, 0, 1.0, [26], MUL, ADD)
+    col(15, 3, 7.0, -HB, EQ, MUL)
+    col(16, 4, 4.0, [5], MUL, ADD)
+    col(17, 1, 8.0, [16], MUL, ADD)
+    col(18, 7, -31.0, 0.0, MUL, ADD)
+    col(19, 1, 32.0, [18], MUL, ADD)
+    col(20, 2, 2.0, [19], MUL, ADD)
+    col(21, 4, 1000.0, [0], MUL, ADD); col(22, 4, -1000.0, [0], MUL, ADD)
+    col(23, 6, 1000.0, [0], MUL, ADD); col(24, 6, -1000.0, [0], MUL, ADD)
+    col(25, 1, -0.5, -15 / 32, MUL, ADD)
     V(1, lambda e, T, B: e.tensor_copy(T.ofr[:, 0:1], cf(T, 20)), ["cf20"], ["ofr"])
-    V(8, lambda e, T, B: e.tensor_scalar(T.ofq[:], T.num[:, 0:8], 128.0, cf(T, 16), ALU.mult, ALU.add), ["num0", "cf16"], ["ofq"])
-    TS = lambda n, o, i, s1, s2, o0, o1, r, w: V(n, lambda e, T, B: e.tensor_scalar(o(T), i(T), s1(T) if s1 else None, s2, o0, o1), r, w)
-    r16 = lambda T: T.num[:, :16]
-    TS(16, lambda T: T.a16[:], r16, lambda T: cf(T, 1), 1.0, ALU.is_equal, ALU.mult, ["num0", "cf1"], ["a16"])
-    TS(16, lambda T: T.a16n[:], r16, lambda T: cf(T, 1), -1.0, ALU.is_equal, ALU.mult, ["num0", "cf1"], ["a16n"])
-    V(16, lambda e, T, B: e.tensor_scalar(T.selw[:], T.a16[:], cf(T, 11), None, ALU.mult), ["a16", "cf11"], ["selw"])
-    V(16, lambda e, T, B: e.tensor_copy(T.selt[:], T.a16[:]), ["a16"], ["selt"])
-    for x in range(2):
-        V(16, lambda e, T, B, x=x: e.tensor_copy(T.selt2[:, x::2], T.a16[:]), ["a16"], ["selt2%d" % x])
-    TS(128, lambda T: T.i32[:], r128, lambda T: cf(T, 0), 1.0, ALU.is_equal, ALU.mult, ["num0", "cf0"], ["i32"])
-    TS(128, lambda T: T.idf[:], r128, lambda T: cf(T, 0), 2.0 ** -13, ALU.is_equal, ALU.mult, ["num0", "cf0"], ["idf"])
-    TS(128, lambda T: T.inn[:], r128, lambda T: cf(T, 0), -PEN, ALU.is_equal, ALU.mult, ["num0", "cf0"], ["inn"])
-    for x in range(2):
-        V(64, lambda e, T, B, x=x: e.tensor_copy(T.in2[:, x::2], T.inn[:]), ["inn"], ["in2%d" % x])
-    TS(16, lambda T: T.b16[:], r16, lambda T: cf(T, 13), 1.0, ALU.is_equal, ALU.mult, ["num0", "cf13"], ["b16"])
-    V(480, lambda e, T, B: e.tensor_scalar(T.dw[:], T.num[:, :480], 0.0, None, ALU.mult), ["num0"], ["dw"])
-    op("V", [("v", 32)] * 2, lambda e, T, B, X: [e.tensor_tensor(T.dw[64 * h:64 * h + 64, 240 * h + 112:240 * h + 128], T.a16[64 * h:64 * h + 64, :], T.b16[64 * h:64 * h + 64, :], ALU.subtract)
-                                                 for h in range(2)], ["a16", "b16", "dw"], ["dw"])
-    TS(128, lambda T: T.tmp[:], r128, lambda T: cf(T, 14), PEN, ALU.is_equal, ALU.mult, ["num0", "cf14"], ["tmp"])
-    V(256, lambda e, T, B: e.tensor_tensor(T.dinv[:], T.tmp[:], T.inn[:], ALU.add), ["tmp", "inn"], ["dinv"])
-    V(128, lambda e, T, B: e.memset(T.m16[:], 1.0), [], ["m16"])
-    V(8, lambda e, T, B: e.memset(T.m16[:, 0::16], 0.0), ["m16"], ["m16"])
-    V(128, lambda e, T, B: e.memset(T.ones[:], 1.0), [], ["ones"])
-    V(64, lambda e, T, B: e.memset(T.one1[:], 1.0), [], ["one1"])
-    G(2048, lambda e, T: e.iota(T.rsel[:], [[0, 2048]], 1, 0, **IO), [], ["rsel"])
-    def zero(pool, k, n, view):
-        V(n, lambda e, T, B: e.memset(view(T), 0), [], []); ops[-1]["init"] = (pool, k)
-    for k in range(NQ):
-        if k < 2: zero("qd", k, 512, lambda T, k=k: T.qd[:, 1024 * k:1024 * k + 1024])
+    V(8, lambda e, T, B: e.tensor_scalar(T.ofq[:], T.rr[:, 0:8], 128.0, cf(T, 17), MUL, ADD), ["rr", "cf17"], ["ofq"])
+    V(8, lambda e, T, B: e.tensor_scalar(T.cb[:], T.rr[:, 0:8], -8.0, cf(T, 25), MUL, ADD), ["rr", "cf25"], ["cb"])
+
+    def mark(name, a, b, k, val, shift=0.0, key=None):
+        src = lambda T: T.rr[:, :b - a]
+        if shift:
+            V(b - a, lambda e, T, B: e.tensor_scalar(T[name][:, a:b], src(T), shift, cf(T, k), ADD, EQ), ["rr", "cf%d" % k], [key or name])
         else:
-            G(1024, lambda e, T, k=k: e.iota(T.qd[:, 1024 * k:1024 * k + 1024], [[0, 1024]], 0, 0, **IO), [], []); ops[-1]["init"] = ("qd", k)
-    for k in range(NR): zero("rb", k, 256, lambda T, k=k: T.rb[:, 512 * k:512 * k + 256])
-    for k in range(2): zero("rd", k, 128, lambda T, k=k: T.rd[:, 512 * k:512 * k + 256])
-    V(NT * 64, lambda e, T, B: e.memset(T.tf[:], 0.0), [], ["ztf"])
-    V(NT * 32, lambda e, T, B: e.memset(T.ti[:], 0), [], ["zti"])
-    G(512, lambda e, T: e.iota(T.ru4[:], [[0, 16], [1, 4], [0, 8]], 0, 0, **IO), [], ["ru4"])
-    G(128, lambda e, T: e.iota(T.rum[:, :128], [[0, 2], [1, 4], [0, 16]], 0, 0, **IO), [], ["rum0"])
-    G(128, lambda e, T: e.iota(T.rum[:, 128:], [[1, 2], [0, 64]], 0, 0, **IO), [], ["rum1"])
-    V(128, lambda e, T, B: e.tensor_scalar(T.cl[0:16, :128], T.rum[0:16, 128:], T.cf[0:16, 5:6], None, ALU.is_equal), ["rum1", "cf5"], ["cl0"])
-    V(128, lambda e, T, B: e.tensor_scalar(T.cl[0:4, 128:], T.rum[0:4, :128], T.cf[0:4, 0:1], -PEN, ALU.not_equal, ALU.mult), ["rum0", "cf0"], ["cl1"])
-    TS(8, lambda T: T.g8[:], lambda T: T.num[:, :8], lambda T: cf(T, 3), -1.0, ALU.is_equal, ALU.mult, ["num0", "cf3"], ["g8"])
-    op("V", [("v", 128)] * 8, lambda e, T, B, X: [e.tensor_scalar(T.cr[0:16, h:1024:8], T.th16[0:16, :], T.g8[0:16, h:h + 1], None, ALU.mult) for h in range(8)],
-       ["g8", "th16"], ["cr"])
-    V(256, lambda e, T, B: e.tensor_scalar(T.cr[0:4, 1024:], T.ru4[0:4, :], T.cf[0:4, 0:1], None, ALU.is_equal), ["ru4", "cf0"], ["cr1"])
-    V(256, lambda e, T, B: e.tensor_scalar(T.msk[:], T.ru4[:], cf(T, 4), None, ALU.is_equal), ["ru4", "cf4"], ["msk"])
-    G(128, lambda e, T: e.iota(T.cfr[0:1, :], [[0, 8], [-1, 16]], 15, 0, **IO), [], ["cfr"])
-    V(64, lambda e, T, B: e.memset(T.cfb[0:1, 0:256:2], 0.0), [], ["cfb0"])
-    V(128, lambda e, T, B: e.tensor_scalar(T.cfb[0:1, 1:256:2], T.cfr[0:1, :], 0.0625, None, ALU.mult), ["cfr"], ["cfb"])
-    V(128, lambda e, T, B: e.tensor_scalar(T.cfb[0:1, 256:], T.cfr[0:1, :], 16384.0, 8192.0, ALU.mult, ALU.add), ["cfr"], ["crow"])
+            V(b - a, lambda e, T, B: e.tensor_scalar(T[name][:, a:b], src(T), cf(T, k), cf(T, val[0]) if isinstance(val, list) else val, EQ, MUL),
+              ["rr", "cf%d" % k] + (["cf%d" % val[0]] if isinstance(val, list) else []), [key or name])
+    mark("a16", 0, 16, 1, 1.0); mark("selw", 0, 64, 11, [8])
+    mark("inn", 0, 128, 0, -PEN); mark("inp", 0, 128, 14, PEN); mark("a16p", 0, 16, 10, 1.0); mark("b16p", 0, 16, 13, 1.0)
+    mark("zw", 0, 160, 21, 1.0, -16.0, "zw0"); mark("zw", 160, 320, 22, 1.0, -1016.0, "zw1")
+    mark("yh", 0, 144, 23, 1.0, -8.0, "yh0"); mark("yh", 144, 288, 24, 1.0, -1008.0, "yh1")
+    V(256, lambda e, T, B: e.memset(T.zz[:], 0.0), [], ["zz"])
+    fill = lambda n, view, val, r, w: A(n, lambda e, T, B: e.activation(view(T), T.zz[:, :n], AF.Identity, bias=val), ["zz"] + r, w)
+    fill(192, lambda T: T.dq[:], 0.0, [], ["dq"])
+    op("V", [("v", 32)] * 4, lambda e, T, B, X: [e.tensor_tensor(T.dq[32 * x:32 * x + 32, 48 * x + 16:48 * x + 32], T.a16p[32 * x:32 * x + 32, :], T.b16p[32 * x:32 * x + 32, :], ALU.subtract)
+                                                 for x in range(4)], ["a16p", "b16p", "dq"], ["dq"])
+    for name, val, first in (("m16", 1.0, 0.0), ("rk", 1 / 32, -1e6)):
+        fill(272, lambda T, name=name: T[name][:], val, [], [name])
+        fill(17, lambda T, name=name: T[name][:, 0::16], first, [name], [name])
+    fill(8, lambda T: T.c9[:, :8], 0.0, [], ["c9"]); fill(1, lambda T: T.c9[:, 8:9], -96.0, [], ["c9x"])
+    A(512, lambda e, T, B: e.activation(T.ones[:], T.zz[:], AF.Exp), ["zz"], ["ones"])
+    G(256, lambda e, T: e.affine_select(T.thl[0:8, :], T.m16[0:8, 1:257], [[1, 8], [0, 32]], EQ, 0.0, 0, -1), ["m16"], ["thl"])
+    V(256, lambda e, T, B: e.tensor_scalar(T.thq[0:8, :], T.thi[0:8, :], -1.0, None, MUL), ["thi"], ["thq"])
+    for name in ("idh", "i32"):
+        G(128, lambda e, T, name=name: e.affine_select(T[name][:], T.ones[:, :128], [[-1, 128]], EQ, 0.0, 0, 1), ["ones"], [name])
+
+    def init(pool, k): ops[-1]["init"] = (pool, k)
+    for k in range(8):
+        op("P", [("p", 512)], lambda e, T, B, X, k=k: [e.matmul(T["pb%d" % k][:, :], T.zz[0:1, :128], T.zz[0:1, :], True, True)], ["zz"], []); init("ps", k)
+    for k in range(POOLS["qd"]):
+        if k < 2: V(512, lambda e, T, B, k=k: e.memset(T.qd[:, 1024 * k:1024 * k + 1024], 0.0), [], [])
+        else: G(1024, lambda e, T, k=k: e.iota(T.qd[:, 1024 * k:1024 * k + 1024], [[0, 1024]], 0, 0, **IO), [], [])
+        init("qd", k)
+    for k in range(POOLS["qh"]):
+        op("V", [("v", 256)] * 2, lambda e, T, B, X, k=k: [e.tensor_copy(T.qh[:, 1024 * k + a:1024 * k + a + 512], T.zz[:]) for a in (0, 512)], ["zz"], []); init("qh", k)
+    for pool, name, n in (("rb", "rb", 256), ("tt", "tf", 64), ("xx", "zt", 128)):
+        for k in range(POOLS[pool]):
+            fill(n, lambda T, o=TILES[name][1] * k, name=name, n=n: T[name][:, o:o + n], 0.0, [], []); init(pool, k)
+    V(16, lambda e, T, B: e.tensor_copy(T.lsl[:, :16], T.curi[:]), ["curi"], ["Lc00", "Lc01"])
     for c in range(NC):
-        V(8, lambda e, T, B, c=c: e.tensor_copy(T.lst[:, 24 * c + 8:24 * c + 16], T.curi[:, 8 * c:8 * c + 8]), ["curi"], ["Lin0%d" % c])
+        VG(128, lambda e, T, c=c: e.tensor_copy(T.nq[:, 640 * c + 256:640 * c + 384], T.nnum[:, :2048].indirect(T.lsl[:, 8 * c:8 * c + 8])), ["num0", "num1", "num2", "Lc0%d" % c], ["nc0%d" % c])
     V(64, lambda e, T, B: e.tensor_copy(T.toku[:], T.toki[:]), ["toki"], ["toku"])
     op("G", [("n", 3000)], lambda e, T, B, X: X["tokens"](), ["toku"], ["tokl"], sem="rtok", lat=-1)
-    for h in range(2):
-        for u in range(2):
-            G(128, lambda e, T, h=h, u=u: e.affine_select(T.pvm[:, 256 * h + 128 * u:256 * h + 128 * u + 128], T.ones[:], [[-16, 8], [1000, 2], [-1, 8]],
-                                                          ALU.is_equal, 0.0, -8 * h - 1000 * u, 1), ["ones"], ["perm%d%d" % (h, u)])
-    G(2048, lambda e, T: e.affine_select(T.rsel[:], T.rsel[:], [[-1, 16], [-16, 8], [0, 16]], ALU.is_equal, 0.0, 0, 1), ["rsel"], ["rsel"])
-    G(128, lambda e, T: e.affine_select(T.repm[0:16, :], T.ones[0:16, :], [[-1, 8], [0, 16]], ALU.is_equal, 0.0, -8, 1), ["ones"], ["repm"])
+    for k in range(4):
+        G(512, lambda e, T, k=k: e.affine_select(T.rsel[:, 512 * k:512 * k + 512], T.ones[:], [[-1, 4], [-16, 8], [0, 16]], EQ, 0.0, -4 * k, 1), ["ones"], ["rsel%d" % k])
+    G(128, lambda e, T: e.affine_select(T.sel0[:], T.ones[:, :128], [[16, 8], [0, 16]], EQ, 0.0, 0, -1), ["ones"], ["sel0"])
 
     def send(name, src, dst, r, w, to, extra):
         op("G", [("n", 600)], lambda e, T, B, X: X["send"](name, src(T), dst(T), to), r, w, sem=name, lat=-1 - extra)
 
-    def kgather(win, wk, ko):
-        k = slot("kg", NK)
+    def halves(name, win, wk, off, ok):
+        (k, v), = tiles(name)
+        if who[0] + name in WHOLE:
+            gather(2048, v, win, off, wk + [ok], [k + (0,), k + (1,)], name + "0")
+            return [k + (0,), k + (1,)], v
         for h in range(2):
-            gather(1024, lambda T, h=h: T.kg[:, 2048 * k + 1024 * h:2048 * k + 1024 * h + 1024], win,
-                   lambda T, h=h: T.ofk[:, 128 * ko + 64 * h:128 * ko + 64 * h + 64], wk + ["ofk%d" % ko], ["kg%d%d" % (k, h)])
-        return k
+            gather(1024, lambda T, h=h: v(T, 1024 * h, 1024 * h + 1024), win, lambda T, h=h: off(T, 64 * h, 64 * h + 64), wk + [ok], [k + (h,)], name + str(h))
+        return [k + (0,), k + (1,)], v
 
-    def first(T, B, k, kq, acc):
-        out = []
-        for h in range(2):
-            for b in range(16):
-                u = 64 * h + 4 * b
-                out.append((B[64 * h:64 * h + 64, 32 * b:32 * b + 32], T.kg[:, 2048 * k + 16 * u:2048 * k + 16 * u + 64],
-                            T.qd[:, 1024 * kq + 8 * u:1024 * kq + 8 * u + 32], not acc, not acc))
-        return out
+    def scores(T, B, kg, qd, alone):
+        return [(B[32 * (u // 32):32 * (u // 32) + 16, u % 32:256:32], kg(T, 16 * u, 16 * u + 16), qd(T, u), alone, alone) for u in range(128)]
 
-    def spread(src, rk):
-        kq = slot("qd", NQ)
-        op("V", [("s", 128)], lambda e, T, B, X: [e.tensor_copy(T.qd[:, 1024 * kq:1024 * kq + 1024].indirect(T.ofq[:]), src(T))], rk + ["ofq"], ["qd%d" % kq])
-        return kq
+    def spread(name, src, rk):
+        if name in BYDMA:
+            (k, v), = tiles("qh")
+            op("S", [("n", 800)], lambda e, T, B, X: [e.dma_start(v(T, 128 * (4 * (h % 2) + h // 2), 128 * (4 * (h % 2) + h // 2) + 128, rows=slice(16 * h, 16 * h + 16)),
+                                                                  T.nq[16 * h:16 * h + 16, src:src + 128]) for h in range(8)], rk, [k], sem="d" + name, lat=2000)
+            return k, lambda T, u: v(T, u, 1024, 128)
+        (k, v), = tiles("qd")
+        VG(128, lambda e, T: e.tensor_copy(v(T).indirect(T.ofq[:]), T.nq[:, src:src + 128]), rk + ["ofq"], [k], "s")
+        return k, lambda T, u: v(T, 8 * u, 8 * u + 8)
 
-    def tolist(mms, n, r, out, w):
-        ps = P(n, mms, r)
-        ky = slot("yt", NT)
-        V(32, lambda e, T, B: e.transpose(T.yt[:, 32 * ky:32 * ky + 32], B[:, :32]), [], ["yt%d" % ky], ps)
-        V(8, lambda e, T, B: e.tensor_copy(out(T), T.yt[:, 32 * ky:32 * ky + 8]), ["yt%d" % ky], w)
-
-    def read(t, c, own, kq, kr):
-        n = 2304 + 256 * t; who[0] = "o" if own else "h"
-        ab = lambda x: [x + "A"] + ([x + "B"] if t else [])
-        base = 24 * (NC * t + c) + 8 if own else 24 * (NC * (t + 1) + c)
-        Lc, Lb = (lambda T: T.lst[:, base:base + 8]), (lambda T: T.lst[:, base + 8:base + 16])
-        kc, kb = (["Lin%d%d" % (t, c)], ["Lb%d%d" % (t, c)]) if own else (["Lin%d%d" % (t + 1, c)],) * 2
-        k = slot("rd_", NT); s = slice(128 * k, 128 * k + 128)
-        ko = slot("ofk", NT)
-        gather(128, lambda T: T.dd[:, s], lambda T: T.bws[:, :n], Lb, ab("bw") + kb, ["dd%d" % k])
-        op("V", [("g", 128)], lambda e, T, B, X: [e.tensor_tensor(T.fm[:, s], T.num[:, :n].indirect(Lb(T)), T.dd[:, s], ALU.subtract)], NUMS(n) + kb + ["dd%d" % k], ["fm%d" % k])
-        V(128, lambda e, T, B: e.tensor_copy(T.ofk[:, 128 * ko:128 * ko + 128], T.fm[:, s]), ["fm%d" % k], ["ofk%d" % ko])
-        kk = kgather(lambda T: T.hks[:, :n], ab("hk"), ko)
-        op("V", [("g", 128)], lambda e, T, B, X: [e.tensor_tensor(T.inv[:, s], T.num[:, :n].indirect(Lc(T)), T.fm[:, s], ALU.is_ge)], NUMS(n) + kc + ["fm%d" % k], ["inv%d" % k])
-        ps = P(2048, lambda T, B: first(T, B, kk, kq, False), ["kg%d0" % kk, "kg%d1" % kk, "qd%d" % kq])
-        k1 = slot("s1", NS1); o1 = 512 * k1
-        V(512, lambda e, T, B: e.tensor_tensor(T.s1[:, o1:o1 + 512], B[:, :], T.msk[:], ALU.mult), ["msk"], ["s1%d" % k1], ps)
-        sv = lambda T, h, g: T.s1[64 * h:64 * h + 64, o1 + g:o1 + 512:8]
-        key = own and t + 1 < RO
-        if key:
-            def mms(T, B):
-                out = [(B[:, :256], T.inv[:, s], T.in2[:], True, False), (B[:, 1:256:2], T.dd[:, s], T.idf[:], False, False)]
-                out += [(B[64 * h:64 * h + 64, 32 * g:32 * g + 32], sv(T, h, g), T.selt2[64 * h:64 * h + 64, :], False, False) for h in range(2) for g in range(8)]
-                return out + [(B[:, :256], T.one1[0:1, :], T.cfb[0:1, :256], False, True)]
-            ps = P(1664, mms, ["inv%d" % k, "dd%d" % k, "s1%d" % k1, "in20", "in21", "idf", "one1", "cfb", "cfb0", "selt20", "selt21"])
-            sc = lambda B: B[:, 0:256:2]
-            kx = slot("ks", NT); kt = slot("tt", NT); kd = slot("rd", 2); kf = slot("ofc", 2)
-            V(128, lambda e, T, B: e.tensor_tensor_scan(T.ks[:, 128 * kx:128 * kx + 128], T.m16[:], B[:, 1:256:2], 0.0, ALU.mult, ALU.max), ["m16"], ["ks%d" % kx], ps)
-            V(8, lambda e, T, B: e.tensor_scalar(T.ti[:, 32 * kt:32 * kt + 8], T.ks[:, 128 * kx + 15:128 * kx + 128:16], 8192.0, None, ALU.mult), ["ks%d" % kx], ["tia%d" % kt])
-            V(8, lambda e, T, B: e.tensor_scalar(T.ti[:, 32 * kt + 16:32 * kt + 24], T.ti[:, 32 * kt:32 * kt + 8], 511, None, AND), ["tia%d" % kt], ["tib%d" % kt])
-            op("V", [("s", 16)], lambda e, T, B, X: [e.tensor_copy(T.rd[:, 512 * kd:512 * kd + 512].indirect(T.ofr[:, 0:1]), T.ti[:, 32 * kt + 16:32 * kt + 32])],
-               ["tib%d" % kt, "ofr"], ["rd%d" % kd])
-            tolist(lambda T, B: [m for x in range(2) for m in (
-                (B[:, 16 * x:16 * x + 16], T.rb[:, 512 * kr + x:512 * kr + 256:2], T.a16[:], True, False),
-                (B[:, 16 * x:16 * x + 16], T.rd[:, 512 * kd + x:512 * kd + 256:2], T.a16n[:], False, True))],
-                640, ["rb%d" % kr, "rd%d" % kd, "a16", "a16n"], lambda T: T.ofc[:, 8 * kf:8 * kf + 8], ["ofc%d" % kf])
-            oq = 256 * (NC * t + c)
-            gather(128, lambda T: T.qcs[:, oq + 128:oq + 256], lambda T: T.hks[:, :n], lambda T: T.ofc[:, 8 * kf:8 * kf + 8], ab("hk") + ["ofc%d" % kf], ["cs%d%d" % (t, c)])
-            send("rQ%d%d" % (t, c), lambda T: T.qcs[:, oq:oq + 256], lambda T: T.qcl[:, oq:oq + 256], ["qs%d%d" % (t, c), "cs%d%d" % (t, c)], ["ql%d%d" % (t, c)], 1, 500)
+    def read(t, c, own, kq, qd):
+        n = 2304 + 256 * t; who[0] = "o" if own else "h"; tc = "%d%d" % (t, c); x = NC * t + c
+        ab = lambda s: [s + "A"] + ([s + "B"] if t else [])
+        if own:
+            Lb, kl = (lambda T: T.lso[:, 8 * x:8 * x + 8]), "Lb" + tc
+            ob, kb, oc, kc = 640 * x, "nb" + tc, 640 * x + 256, "nc" + tc
         else:
-            def mms(T, B):
-                return [(B[:, :128], T.inv[:, s], T.inn[:], True, False)] + [
-                    (B[64 * h:64 * h + 64, 16 * g:16 * g + 16], sv(T, h, g), T.selt[64 * h:64 * h + 64, :], False, False) for h in range(2) for g in range(8)] + [
-                    (B[:, :128], T.inv[:, s], T.inn[:], False, True)]
-            ps = P(1280, mms, ["inv%d" % k, "s1%d" % k1, "inn", "selt"])
-            sc = lambda B: B[:, :128]
-        km = slot("msc", NT); om = 256 * km
-        V(128, lambda e, T, B: e.tensor_tensor_scan(T.msc[:, om:om + 128], T.m16[:], sc(B), 0.0, ALU.mult, ALU.max), ["m16"], ["mm%d" % km], ps)
-        A(128, lambda e, T, B: e.activation(T.ee[:, s], sc(B), AF.Exp, scale=0.0078125), [], ["ee%d" % k], ps)
-        V(128, lambda e, T, B: e.tensor_tensor_scan(T.msc[:, om + 128:om + 256], T.m16[:], T.ee[:, s], 0.0, ALU.mult, ALU.add), ["m16", "ee%d" % k], ["ms%d" % km])
-        ps = P(1152, lambda T, B: [m for h in range(2) for m in [(B[:, 64 * h:64 * h + 64], T.dinv[:], T.inv[:, 128 * k + 64 * h:128 * k + 64 * h + 64], True, False)] + [
-            (B[:, 64 * h:64 * h + 64], T.dw[:, 240 * h + 112 - 16 * g:240 * h + 240 - 16 * g], T.s1[:, o1 + g:o1 + 512:8], False, g == 7) for g in range(8)]],
-            ["inv%d" % k, "s1%d" % k1, "dinv", "dw"])
-        op("A", [("v", 128)] * 2, lambda e, T, B, X: [e.activation(o, B[:, :128], AF.Exp, bias=cf(T, 15), scale=0.0078125) for o in (T.hi[:, s], B[:, 128:256])],
-           ["cf15"], ["hi%d" % k], ps)
-        V(128, lambda e, T, B: e.tensor_tensor(T.lo[:, s], B[:, 128:256], T.hi[:, s], ALU.subtract), ["hi%d" % k], ["lo%d" % k], ps)
-        ps = P(1024, lambda T, B: [(B[:, 64 * h:64 * h + 64], T.pvm[:, 256 * h + 128 * u:256 * h + 128 * u + 128], T.fm[:, 128 * k + u:128 * k + 128:2], u == 0, u == 1)
-                                   for h in range(2) for u in range(2)], ["fm%d" % k, "perm00", "perm01", "perm10", "perm11"])
-        V(128, lambda e, T, B: e.tensor_copy(T.ofv[:, s], B[:, :128]), [], ["ofv%d" % k], ps)
-        kv = slot("vg", NV); kso = slot("so", NSO)
+            Lb, kl = (lambda T: T.lsl[:, 8 * (x + NC):8 * (x + NC) + 8]), "Lc%d%d" % (t + 1, c)
+            ob, kb, oc, kc = 640 * (x + NC) + 256, "nc%d%d" % (t + 1, c), 640 * (x + NC) + 512, "hq" + tc
+        (kfm, fm), (kin, inv), (kee, ee), (khi, hi), (klo, lo), (kov, ofv) = tiles("fm", "inv", "ee", "hi", "lo", "ofv")
+        (kok, ofk), = tiles("ofk")
+        VG(128, lambda e, T: e.tensor_tensor(fm(T), T.bws[:, :n].indirect(Lb(T)), T.nq[:, ob:ob + 128], ADD), ab("bw") + [kl, kb], [kfm])
+        V(64, lambda e, T, B: e.tensor_scalar(ofk(T), fm(T), -1.0, float(OFS), MUL, ADD), [kfm], [kok])
+        kk, kg = halves("kg", lambda T: T.hks[:, :n], ab("hk"), ofk, kok)
+        V(128, lambda e, T, B: e.tensor_tensor(inv(T), fm(T), T.nq[:, oc:oc + 128], ALU.is_ge), [kfm, kc], [kin])
+        ps = P(1024, lambda T, B: scores(T, B, kg, qd, True)[:64], [kk[0], kq])
+        P(1024, lambda T, B: scores(T, B, kg, qd, True)[64:], [kk[1], kq], ps)
+        (k1, s1), = tiles("s1")
+        V(256, lambda e, T, B: e.tensor_scalar(s1(T), B[:, :256], 2048.0, -2048.0, ALU.min, ALU.max), [], [k1], ps)
+        ps = P(768, lambda T, B: [(B[:, :128], s1(T, 0, 128), T.zw[:, 16:144], True, False)] + [
+            (B[32 * a:32 * a + 32, 32 * b:32 * b + 32], inv(T, 32 * b, 32 * b + 32), T.inn[:, 32 * a:32 * a + 32], False, False) for a in range(4) for b in range(4)] + [
+            (B[:, :128], s1(T, 128, 256), T.zw[:, 0:128], False, True)], [k1, kin, "zw0", "inn"])
+        (km, msc), = tiles("msc")
+        if own and t + 1 < RO:
+            (kx, ks), = tiles("ks"); (kmi, mi), (kfq, fq), (kof, ofc) = tiles("mi", "fq", "ofc")
+            V(128, lambda e, T, B: e.tensor_tensor_scan(ks(T), T.rk[:, :128], B[:, :128], 0.0, ADD, ALU.max), ["rk"], [kx], ps)
+            V(8, lambda e, T, B: e.tensor_copy(mi(T), ks(T, 15, 128, 16)), [kx], [kmi])
+            V(16, lambda e, T, B: e.tensor_tensor(fq(T), ks(T, 15, 128, 16), mi(T), ALU.subtract), [kx, kmi], [kfq])
+            p2 = P(384, lambda T, B: [m for b in range(2) for m in [(B[:, b:8:2], T.idh[:], T.cb[:, b:8:2], True, False)] + [
+                (B[:, b:8:2], T.zw[:, 160 * b + 16 - 16 * (h - b):160 * b + 144 - 16 * (h - b)], fq(T, h, 8, 2), False, h == 1) for h in range(2)]], [kfq, "idh", "cb", "zw0", "zw1"])
+            V(8, lambda e, T, B: e.tensor_scalar(ofc(T), B[:, :8], -32.0, None, MUL), [], [kof], p2)
+            gather(128, lambda T: T.crs[:, 128 * x:128 * x + 128], kg, ofc, kk + [kof], ["cs" + tc], "cs")
+            send("rC" + tc, lambda T: T.crs[:, 128 * x:128 * x + 128], lambda T: T.crl[:, 128 * x:128 * x + 128], ["cs" + tc], ["cl" + tc], 1, 250)
+            kmx, mx = kmi, mi
+        else:
+            V(128, lambda e, T, B: e.tensor_tensor_scan(msc(T, 0, 128), T.m16[:, :128], B[:, :128], 0.0, MUL, ALU.max), ["m16"], [km + (0,)], ps)
+            kmx, mx = km + (0,), lambda T: msc(T, 15, 128, 16)
+        A(128, lambda e, T, B: e.activation(ee(T), B[:, :128], AF.Exp, scale=0.0078125), [], [kee], ps)
+        V(128, lambda e, T, B: e.tensor_tensor_scan(msc(T, 128, 256), T.m16[:, :128], ee(T), 0.0, MUL, ADD), ["m16", kee], [km + (1,)])
+        yield
+        who[0] = "o" if own else "h"
+        ps = P(1280, lambda T, B: [(B[:, :128], T.inn[:], inv(T), True, False)] + [
+            (B[32 * a:32 * a + 32, 32 * b:32 * b + 32], T.dq[:, 48 * b + 16 - 16 * h:48 * b + 48 - 16 * h], s1(T, 128 * h + 32 * a, 128 * h + 32 * a + 32), False, False)
+            for a in range(4) for h in range(2) for b in range(4)] + [(B[:, :128], T.inp[:], inv(T), False, True)], [kin, k1, "inn", "inp", "dq"])
+        op("A", [("v", 128)] * 2, lambda e, T, B, X: [e.activation(o, B[:, :128], AF.Exp, bias=cf(T, 15), scale=0.0078125) for o in (hi(T), B[:, 128:256])], ["cf15"], [khi], ps)
+        V(128, lambda e, T, B: e.tensor_tensor(lo(T), B[:, 128:256], hi(T), ALU.subtract), [khi], [klo], ps)
+        ps = P(256, lambda T, B: [(B[:, 64 * h:64 * h + 64], T.yh[:, 144 * h + 8 - 8 * (u - h):144 * h + 136 - 8 * (u - h)], fm(T, u, 128, 2), u == 0, u == 1)
+                                  for h in range(2) for u in range(2)], [kfm, "yh0", "yh1"])
+        V(128, lambda e, T, B: e.tensor_scalar(ofv(T), B[:, :128], -1.0, float(OFS), MUL, ADD), [], [kov], ps)
+        kv, vg = halves("vg", lambda T: T.vvs[:, :n], ab("vv"), ofv, kov)
+        (kso, so), = tiles("so")
         for h in range(2):
-            gather(1024, lambda T, h=h: T.vg[:, 2048 * kv + 1024 * h:2048 * kv + 1024 * h + 1024], lambda T: T.vvs[:, :n],
-                   lambda T, h=h: T.ofv[:, 128 * k + 64 * h:128 * k + 64 * h + 64], ab("vv") + ["ofv%d" % k], ["vg%d%d" % (kv, h)])
             for b in range(2):
-                ps = P(1024, lambda T, B, h=h, b=b: [(B[:, i:512:8], T.rsel[:, 128 * (8 * h + i):128 * (8 * h + i) + 128], x[:, 128 * k + 64 * b:128 * k + 64 * b + 64], j == 0, j == 1)
-                                                     for i in range(8) for j, x in enumerate((T.hi, T.lo))], ["hi%d" % k, "lo%d" % k, "rsel"])
+                ps = P(1024, lambda T, B, h=h, b=b: [(B[:, i:512:8], T.rsel[:, 128 * (8 * h + i):128 * (8 * h + i) + 128], y(T, 64 * b, 64 * b + 64), j == 0, j == 1)
+                                                     for i in range(8) for j, y in enumerate((hi, lo))], [khi, klo, "rsel%d" % (2 * h), "rsel%d" % (2 * h + 1)])
                 o = 1024 * h + 512 * b
-                V(512, lambda e, T, B, o=o: e.tensor_tensor_scan(T.so[:, 2048 * kso + o:2048 * kso + o + 512], T.vg[:, 2048 * kv + o:2048 * kv + o + 512], B[:, :], 0.0, ALU.add, ALU.mult),
-                  ["vg%d%d" % (kv, h)], ["so%d%d%d" % (kso, h, b)], ps)
-        parts = lambda T, B, more: [m for b in range(2) for m in [(B[:, 64 * b:64 * b + 64], T.i32[:], x[:, o + 64 * b:o + 64 * b + 64], True, False) for x, o in more] + [
-            (B[:, 64 * b:64 * b + 64], T.i32[:], T.so[:, 2048 * kso + 1024 * h + 512 * b + 7:2048 * kso + 1024 * h + 512 * b + 512:8], h == 0 and not more, h == 1) for h in range(2)]]
-        return km, parts, ["so%d%d%d" % (kso, h, b) for h in range(2) for b in range(2)] + ["i32"]
+                V(512, lambda e, T, B, o=o: e.tensor_tensor_scan(so(T, o, o + 512), vg(T, o, o + 512), B[:, :], 0.0, ADD, MUL), [kv[h]], [kso + (h, b)], ps)
+        return kmx, mx, km + (1,), msc, so, [kso + (h, b) for h in range(2) for b in range(2)]
 
+    keep, run = {}, {}
     for t in range(RO):
-        keep = {}
         for c in range(NC):
-            n = 2304 + 256 * t; base = 24 * (NC * t + c); oq = 256 * (NC * t + c)
-            Lc = lambda T, base=base: T.lst[:, base + 8:base + 16]
-            kl = ["Lin%d%d" % (t, c)]; who[0] = "s"
-            k = slot("fg", 2); s = slice(128 * k, 128 * k + 128); ko = slot("ofk", NT)
-            gather(128, lambda T, s=s: T.fg[:, s], lambda T, n=n: T.fws[:, :n - 256], Lc, ["fwA"] + (["fwB"] if t else []) + kl, ["fg%d" % k])
-            op("V", [("g", 128)], lambda e, T, B, X, s=s, n=n, Lc=Lc: [e.tensor_tensor(T.fr[:, s], T.num[:, :n].indirect(Lc(T)), T.fg[:, s], ALU.add)], NUMS(n) + kl + ["fg%d" % k], ["fr%d" % k])
-            V(128, lambda e, T, B, s=s, ko=ko: e.tensor_copy(T.ofk[:, 128 * ko:128 * ko + 128], T.fr[:, s]), ["fr%d" % k], ["ofk%d" % ko])
-            kk = kgather(lambda T, n=n: T.hks[:, :n], ["hkA"] + (["hkB"] if t else []), ko)
-            q = lambda T, oq=oq: T.qcs[:, oq:oq + 128]
-            if t == 0:
-                gather(128, q, lambda T: T.hks[:, :], lambda T, c=c: T.toku[:, 8 * c:8 * c + 8], ["hkA", "hkB", "toku"], ["qs0%d" % c])
-            else:
-                op("V", [("g", 128)], lambda e, T, B, X, q=q, oq=oq, o=16 * t + 8 * c: [e.tensor_tensor(q(T), T.hks[:, :].indirect(T.tokl[:, o:o + 8]), T.qcl[:, oq - 256 * NC + 128:oq - 256 * NC + 256], ALU.max)],
-                   ["hkA", "hkB", "tokl", "ql%d%d" % (t - 1, c)], ["qs%d%d" % (t, c)])
-            if t + 1 == RO:
-                send("rQ%d%d" % (t, c), q, lambda T, oq=oq: T.qcl[:, oq:oq + 128], ["qs%d%d" % (t, c)], ["ql%d%d" % (t, c)], 1, 250)
-            kq = spread(q, ["qs%d%d" % (t, c)])
-            ps = P(3072, lambda T, B, c=c, kk=kk, kq=kq: [(B[:, :], T.cl[0:16, :128], T.cr[0:16, 512 * c:512 * c + 512], True, False)] + first(T, B, kk, kq, True)
-                   + [(B[:, :], T.cl[0:4, 128:], T.cr[0:4, 1024:], False, True)],
-                   ["kg%d0" % kk, "kg%d1" % kk, "qd%d" % kq, "cl0", "cl1", "cr", "cr1"])
-            kg_ = slot("sg", 2); og = 512 * kg_
-            A(512, lambda e, T, B, og=og: e.activation(T.sg[:, og:og + 512], B[:, :], AF.Sign, bias=-0.5), [], ["sg%d" % kg_], ps)
-            ps = P(1536, lambda T, B, s=s, og=og: [(B[:, :128], T.fr[:, s], T.i32[:], True, False)] + [
-                (B[64 * h:64 * h + 64, 16 * g:16 * g + 16], T.sg[64 * h:64 * h + 64, og + g:og + 512:8], T.selw[64 * h:64 * h + 64, :], False, False)
-                for h in range(2) for g in range(8)] + [(B[:, :128], T.one1[0:1, :], T.cfb[0:1, 256:], False, True)], ["fr%d" % k, "sg%d" % kg_, "i32", "selw", "one1", "crow"])
-            kx = slot("ks", NT); kt = slot("tt", NT); kr = slot("rb", NR); oi = 32 * kt; of = 64 * kt
-            ta, tb, fa_, fb, fc = ["ti%s%d" % (x, kt) for x in "ab"] + ["tf%s%d" % (x, kt) for x in "abc"]
-            V(128, lambda e, T, B, kx=kx: e.tensor_tensor_scan(T.ks[:, 128 * kx:128 * kx + 128], T.m16[:], B[:, :128], 0.0, ALU.mult, ALU.max), ["m16"], ["ks%d" % kx], ps)
-            V(8, lambda e, T, B, kx=kx, oi=oi: e.tensor_copy(T.ti[:, oi:oi + 8], T.ks[:, 128 * kx + 15:128 * kx + 128:16]), ["ks%d" % kx, "zti", "ztf"], [ta])
-            V(8, lambda e, T, B, oi=oi: e.tensor_scalar(T.ti[:, oi + 16:oi + 24], T.ti[:, oi:oi + 8], 4095, None, AND), [ta], [tb])
-            V(8, lambda e, T, B, oi=oi, of=of: e.tensor_copy(T.tf[:, of:of + 8], T.ti[:, oi + 16:oi + 24]), [tb], [fa_])
-            V(8, lambda e, T, B, of=of: e.tensor_reduce(T.tf[:, of + 48:of + 49], T.tf[:, of:of + 8], AX.X, ALU.max), [fa_], [fc])
-            V(8, lambda e, T, B, of=of: e.tensor_scalar(T.tf[:, of + 32:of + 40], T.tf[:, of:of + 8], 96.0, T.tf[:, of + 48:of + 49], ALU.add, ALU.is_lt), [fa_, fc], [fc + "x"])
-            V(8, lambda e, T, B, of=of: e.tensor_scalar(T.tf[:, of + 16:of + 24], T.tf[:, of + 32:of + 40], T.tf[:, of + 48:of + 49], None, ALU.mult), [fc, fc + "x"], [fb])
-            op("V", [("s", 16)], lambda e, T, B, X, of=of, kr=kr: [e.tensor_tensor(T.rb[:, 512 * kr:512 * kr + 512].indirect(T.ofr[:, 0:1]), T.tf[:, of:of + 16], T.tf[:, of + 16:of + 32], ALU.max)],
-               [fa_, fb, "ofr"], ["rb%d" % kr])
-            tolist(lambda T, B, kr=kr: [(B[:, 16 * x:16 * x + 16], T.rb[:, 512 * kr + x:512 * kr + 256:2], T.a16[:], True, True) for x in range(2)],
-                   512, ["rb%d" % kr, "a16"], lambda T, base=base: T.lst[:, base + 16:base + 24], ["Lb%d%d" % (t, c)])
-            send("rL%d%d" % (t, c), lambda T, base=base: T.lst[:, base + 8:base + 24], lambda T, base=base: T.lst[:, base + 24 * NC:base + 24 * NC + 16],
-                 kl + ["Lb%d%d" % (t, c)], ["Lin%d%d" % (t + 1, c)], 1, 0)
-            keep[c] = read(t, c, True, kq, kr)
+            def scan(t=t, c=c):
+                n = 2304 + 256 * t; x = NC * t + c; tc = "%d%d" % (t, c); on = 640 * x; who[0] = "s"
+                (kf, fr), = tiles("fr"); (kok, ofk), = tiles("ofk")
+                VG(128, lambda e, T: e.tensor_tensor(fr(T), T.fws[:, :n - 256].indirect(T.lsl[:, 8 * x:8 * x + 8]), T.nq[:, on + 256:on + 384], ALU.subtract),
+                   ["fwA"] + (["fwB"] if t else []) + ["Lc" + tc, "nc" + tc], [kf])
+                V(64, lambda e, T, B: e.tensor_scalar(ofk(T), fr(T), float(OFS), None, ADD), [kf], [kok])
+                kk, kg = halves("kg", lambda T: T.hks[:, :n], ["hkA"] + (["hkB"] if t else []), ofk, kok)
+                yield
+                q = lambda T: T.nq[:, on + 128:on + 256]
+                if t == 0: VG(128, lambda e, T: e.tensor_copy(q(T), T.hks[:, :].indirect(T.toku[:, 8 * c:8 * c + 8])), ["hkA", "hkB", "toku"], ["qq" + tc])
+                else: VG(128, lambda e, T: e.tensor_tensor(q(T), T.hks[:, :].indirect(T.tokl[:, 8 * x:8 * x + 8]), T.crl[:, 128 * (x - NC):128 * (x - NC) + 128], ALU.max),
+                         ["hkA", "hkB", "tokl", "cl%d%d" % (t - 1, c)], ["qq" + tc])
+                kq, qd = spread("o" + tc, on + 128, ["qq" + tc])
+                ps = P(1024 + 256, lambda T, B: [(B[:, :256], T.thl[0:8, 128 * c:128 * c + 128], T.thq[0:8, :], True, False)] + scores(T, B, kg, qd, False)[:64], [kk[0], kq, "thl", "thq"])
+                P(1024 + 64, lambda T, B: scores(T, B, kg, qd, False)[64:] + [(B[:, :CLOSE], T.zz[0:1, :128], T.zz[0:1, :CLOSE], False, True)], [kk[1], kq, "zz"], ps)
+                (ksg, sg), = tiles("sg")
+                A(256, lambda e, T, B: e.activation(sg(T), B[:, :256], AF.Sign, bias=cf(T, 9)), ["cf9"], [ksg], ps)
+                ps = P(1024 + 128 + 64, lambda T, B: [(B[:, :128], fr(T), T.idh[:], True, False)] + [
+                    (B[32 * a:32 * a + 32, 32 * (h % 4) + 16 * (h // 4):32 * (h % 4) + 16 * (h // 4) + 16], sg(T, 32 * h, 32 * h + 32), T.selw[:, 16 * a:16 * a + 16], False, False)
+                    for a in range(4) for h in range(8)] + [(B[:, :min(CLOSE, 128)], T.zz[0:1, :128], T.zz[0:1, :min(CLOSE, 128)], False, True)], [kf, ksg, "idh", "selw", "zz"])
+                (kx, ks), = tiles("ks"); (kt, tf), = tiles("tf"); (kr, rb), = tiles("rb"); (ky, yt), = tiles("yt")
+                V(128, lambda e, T, B: e.tensor_tensor_scan(ks(T), T.m16[:, :128], B[:, :128], 0.0, MUL, ALU.max), ["m16"], [kx], ps)
+                V(8, lambda e, T, B: e.tensor_scalar(tf(T, 48, 56), ks(T, 15, 128, 16), 2.0 ** 35 - 2048, -2.0 ** 35, ADD, ADD), [kx], [kt + (0,)])
+                V(16, lambda e, T, B: e.tensor_tensor(tf(T, 0, 8), ks(T, 15, 128, 16), tf(T, 48, 56), ALU.subtract), [kx, kt + (0,)], [kt + (1,)])
+                V(9, lambda e, T, B: e.tensor_tensor_scan(tf(T, 32, 41), T.c9[:, :9], tf(T, 0, 9), 0.0, ADD, ALU.max), ["c9", "c9x", kt + (1,)], [kt + (2,)])
+                V(8, lambda e, T, B: e.tensor_scalar(tf(T, 16, 24), tf(T, 0, 8), tf(T, 40, 41), tf(T, 39, 40), ALU.is_lt, MUL), [kt + (1,), kt + (2,)], [kt + (3,)])
+                VG(16, lambda e, T: e.tensor_tensor(rb(T).indirect(T.ofr[:, 0:1]), tf(T, 0, 16), tf(T, 16, 32), ALU.max), [kt + (1,), kt + (3,), "ofr"], [kr], "s")
+                ps = P(512, lambda T, B: [(B[:, 16 * y:16 * y + 16], rb(T, y, 256, 2), T.a16[:], True, True) for y in range(2)], [kr, "a16"])
+                V(32, lambda e, T, B: e.transpose(yt(T), B[:, :32]), [], [ky], ps)
+                V(8, lambda e, T, B: e.tensor_copy(T.lso[:, 8 * x:8 * x + 8], yt(T, 0, 8)), [ky], ["Lb" + tc])
+                send("rL" + tc, lambda T: T.lso[:, 8 * x:8 * x + 8], lambda T: T.lsl[:, 8 * (x + NC):8 * (x + NC) + 8], ["Lb" + tc], ["Lc%d%d" % (t + 1, c)], 1, 0)
+                VG(128, lambda e, T: e.tensor_copy(T.nq[:, on:on + 128], T.nnum[:, :n].indirect(T.lso[:, 8 * x:8 * x + 8])), ["num0", "num1", "num2", "num3", "Lb" + tc], ["nb" + tc])
+                send("rN" + tc, lambda T: T.nq[:, on:on + 384], lambda T: T.nq[:, on + 640 * NC + 256:on + 640 * NC + 640], ["nb" + tc, "qq" + tc, "nc" + tc],
+                     ["nc%d%d" % (t + 1, c), "hq" + tc], 1, 700)
+                yield
+                keep[x] = yield from read(t, c, True, kq, qd)
+            run["o", NC * t + c] = scan()
         for c in range(NC):
-            oq = 256 * (NC * t + c); ob = 144 * (NC * t + c)
-            kq = spread(lambda T, oq=oq: T.qcl[:, oq:oq + 128], ["ql%d%d" % (t, c)])
-            km, parts, rk = read(t, c, False, kq, None)
-            A(16, lambda e, T, B, ob=ob, km=km: e.activation(T.bks[:, ob + 128:ob + 144], T.msc[:, 256 * km + 15:256 * km + 256:16], AF.Copy), ["mm%d" % km, "ms%d" % km], ["bm%d%d" % (t, c)])
-            ps = P(1024, lambda T, B, parts=parts: parts(T, B, []), rk)
-            A(128, lambda e, T, B, ob=ob: e.activation(T.bks[:, ob:ob + 128], B[:, :128], AF.Copy), [], ["ba%d%d" % (t, c)], ps)
-            send("rB%d%d" % (t, c), lambda T, ob=ob: T.bks[:, ob:ob + 144], lambda T, ob=ob: T.bkl[:, ob:ob + 144], ["bm%d%d" % (t, c), "ba%d%d" % (t, c)], ["bl%d%d" % (t, c)], -1, 600)
+            def helper(t=t, c=c):
+                x = NC * t + c; tc = "%d%d" % (t, c); ob = 144 * x; oq = 640 * (x + NC) + 384
+                kq, qd = spread("h" + tc, oq, ["hq" + tc])
+                kmx, mx, ksm, msc, so, kso = yield from read(t, c, False, kq, qd)
+                A(16, lambda e, T, B: e.activation(T.bks[:, ob + 128:ob + 144], msc(T, 15, 256, 16), AF.Copy), [kmx, ksm], ["bm" + tc])
+                V(256, lambda e, T, B: e.tensor_tensor(T.bks[:, ob:ob + 128], so(T, 7, 1024, 8), so(T, 1031, 2048, 8), ADD), kso, ["ba" + tc])
+                send("rB" + tc, lambda T: T.bks[:, ob:ob + 144], lambda T: T.bkl[:, ob:ob + 144], ["bm" + tc, "ba" + tc], ["bl" + tc], -1, 600)
+            run["h", NC * t + c] = helper()
         for c in range(NC):
-            km, parts, rk = keep[c]
-            ob = 144 * (NC * t + c); oy = 256 * t + 128 * c; k = slot("xx", 2); ox = 48 * k; om = 256 * km; bl = "bl%d%d" % (t, c)
-            V(16, lambda e, T, B, ox=ox, om=om, ob=ob: e.tensor_tensor(T.xx[:, ox + 8:ox + 16], T.msc[:, om + 15:om + 128:16], T.bkl[:, ob + 128:ob + 136], ALU.max), ["mm%d" % km, bl], ["xm%d" % k])
-            V(16, lambda e, T, B, ox=ox, om=om, ob=ob: e.tensor_tensor(T.xx[:, ox + 16:ox + 24], T.msc[:, om + 143:om + 256:16], T.bkl[:, ob + 136:ob + 144], ALU.add), ["ms%d" % km, bl], ["xt%d" % k])
-            A(8, lambda e, T, B, ox=ox: e.activation(T.xx[:, ox + 32:ox + 40], T.xx[:, ox + 8:ox + 16], AF.Exp, scale=-0.0078125), ["xm%d" % k], ["xf%d" % k])
-            V(16, lambda e, T, B, ox=ox: e.tensor_tensor(T.xx[:, ox:ox + 8], T.xx[:, ox + 16:ox + 24], T.xx[:, ox + 32:ox + 40], ALU.mult), ["xt%d" % k, "xf%d" % k], ["xs%d" % k])
-            ps = P(512, lambda T, B, ox=ox: [(B[0:16, :128], T.xx[:, ox:ox + 16], T.i32[:], True, True)], ["xm%d" % k, "xs%d" % k, "i32"])
-            A(128, lambda e, T, B, oy=oy: e.activation(T.mss[0:16, oy:oy + 128], B[0:16, :128], AF.Copy), [], ["mo%d%d" % (t, c)], ps)
-            ps = P(512, lambda T, B, oy=oy: [(B[:, :128], T.repm[0:16, :], T.mss[0:16, oy:oy + 128], True, True)], ["mo%d%d" % (t, c), "repm"])
-            A(128, lambda e, T, B, k=k: e.activation(T.fa[:, 128 * k:128 * k + 128], B[:, :128], AF.Exp, bias=HB, scale=-0.0078125), [], ["fa%d" % k], ps)
-            ps = P(1536, lambda T, B, ob=ob, parts=parts: parts(T, B, [(T.bkl, ob)]), rk + [bl])
-            V(128, lambda e, T, B, k=k, oy=oy: e.tensor_tensor(T.yas[:, oy:oy + 128], B[:, :128], T.fa[:, 128 * k:128 * k + 128], ALU.mult), ["fa%d" % k], ["yo%d%d" % (t, c)], ps)
-            op("S", [("n", 60)], lambda e, T, B, X, oy=oy: [e.dma_start(T.ya[:, oy:oy + 128], T.yas[:, oy:oy + 128])], ["yo%d%d" % (t, c)], [], sem="stored", lat=2500)
-            ops[-1]["due"] = RO - 1 - t
-        if t >= RO - 2:
-            lo_, hi_ = (0, 768) if t == RO - 2 else (768, 1024)
-            op("S", [("n", 120)], lambda e, T, B, X, a=lo_, b=hi_: [e.dma_start(T.ys[:, a:b], T.mss[0:8, a:b]), e.dma_start(T.ym[:, a:b], T.mss[8:16, a:b])],
-               ["mo%d%d" % (x, c) for x in range(lo_ // 256, hi_ // 256) for c in range(NC)], [], sem="stored", lat=2200)
+            def both(t=t, c=c):
+                kmx, mx, ksm, msc, so, kso = keep[NC * t + c]
+                tc = "%d%d" % (t, c); ob = 144 * (NC * t + c); oy = 256 * t + 128 * c; bl = "bl" + tc
+                (kz, zt), (kx, xx), (kf, fa) = tiles("zt", "xx", "fa")
+                V(16, lambda e, T, B: e.tensor_tensor(zt(T, 0, 128, 16), mx(T), T.bkl[:, ob + 128:ob + 136], ALU.max), [kmx, bl], [kz + (0,)])
+                V(16, lambda e, T, B: e.tensor_tensor(xx(T, 0, 8), msc(T, 143, 256, 16), T.bkl[:, ob + 136:ob + 144], ADD), [ksm, bl], [kx + (0,)])
+                A(8, lambda e, T, B: e.activation(xx(T, 8, 16), zt(T, 0, 128, 16), AF.Exp, scale=-0.0078125), [kz + (0,)], [kx + (1,)])
+                V(16, lambda e, T, B: e.tensor_tensor(zt(T, 1, 128, 16), xx(T, 0, 8), xx(T, 8, 16), MUL), [kx + (0,), kx + (1,)], [kz + (1,)])
+                V(128, lambda e, T, B: e.transpose(T.mss[:, oy:oy + 128], zt(T)), [kz + (0,), kz + (1,)], ["mo" + tc])
+                ps = P(512, lambda T, B: [(B[:, :128], T.sel0[:], T.mss[:, oy:oy + 128], True, True)], ["mo" + tc, "sel0"])
+                A(128, lambda e, T, B: e.activation(fa(T), B[:, :128], AF.Exp, bias=HB, scale=-0.0078125), [], [kf], ps)
+                ps = P(1536, lambda T, B: [(B[:, :128], T.i32[:], y, j == 0, j == 2) for j, y in enumerate((so(T, 7, 1024, 8), so(T, 1031, 2048, 8), T.bkl[:, ob:ob + 128]))],
+                       kso + [bl, "i32"])
+                V(128, lambda e, T, B: e.tensor_tensor(T.yas[:, oy:oy + 128], B[:, :128], fa(T), MUL), [kf], ["yo" + tc], ps)
+                op("S", [("n", 60)], lambda e, T, B, X: [e.dma_start(T.ya[:, oy:oy + 128], T.yas[:, oy:oy + 128])], ["yo" + tc], [], sem="stored", lat=2500)
+                if t >= RO - 2 and c == NC - 1:
+                    a, b = (0, 768) if t == RO - 2 else (768, 1024)
+                    op("S", [("n", 120)], lambda e, T, B, X: [e.dma_start(T.ym[:, a:b], T.mss[0::16, a:b]), e.dma_start(T.ys[:, a:b], T.mss[1::16, a:b])],
+                       ["mo%d%d" % (y, z) for y in range(a // 256, b // 256) for z in range(NC)], [], sem="stored", lat=2200)
+                yield
+            run["b", NC * t + c] = both()
+    for k in range(-NC, RO * NC + 8):
+        for name, lag in stages:
+            if 0 <= k - lag < RO * NC:
+                first = len(ops); next(run[name, k - lag], None)
+                for o in ops[first:]: o["turn"] = k
     lastw, readers, acc = {}, {}, {}
     for i, o in enumerate(ops):
         d = set()
@@ -387,7 +357,7 @@ def build(where=None):
         for k in o["r"]: readers.setdefault(k, []).append(i)
         for k in o["w"]: lastw[k] = i; readers[k] = []
         d.discard(i); o["dep"] = sorted(d)
-        o["tiles"] = sorted(set(tile_of(k) for k in o["r"] + o["w"] if tile_of(k)) | ({("ps", o["ps"])} if o["ps"] is not None else set()))
+        o["tiles"] = sorted(set(k[:2] for k in o["r"] + o["w"] if isinstance(k, tuple)) | ({("ps", o["ps"])} if o["ps"] is not None else set()))
     return ops
 
 
@@ -396,27 +366,30 @@ def after(o, M):
     return o["lat"] if o["lat"] >= 0 else M["net"] - o["lat"]
 
 
-def plan(ops, M, seed, look=0.5, noise=0.03, onv=(), per=32000, off=20000, infl=12000, moves=()):
-    n = len(ops); rng = np.random.default_rng(seed)
+def plan(ops, M, onv=(), per=0.0, look=0.5, sticky=0.0):
+    n = len(ops)
     succ = [[] for _ in ops]
     for i, o in enumerate(ops):
         for d in o["dep"]: succ[d].append(i)
-    du = [[dur(a[1], M) for a in o["alts"]] for o in ops]
+    pick = [0 if len(o["alts"]) == 1 else int(o["role"] in onv) for o in ops]
+    seen = {}
+    for i, o in enumerate(ops):
+        if len(o["alts"]) > 1:
+            k = seen.get(o["role"], 0); seen[o["role"]] = k + 1
+            pick[i] = int(str(k) in onv.get(o["role"], ""))
+    du = [dur(o["alts"][pick[i]][1], M) for i, o in enumerate(ops)]
     pr = [0.0] * n
     for i in range(n - 1, -1, -1):
         o = ops[i]
-        pr[i] = du[i][0] + after(o, M) + max([pr[j] for j in succ[i]], default=o.get("due", 0) * per - off if o.get("due") else 0.0)
-        if o["sem"] and o["sem"][:2] == "rQ": pr[i] += infl
-    for i, o in enumerate(ops):
-        if "init" in o: pr[i] = 600 + [pr[j] for j, x in enumerate(ops) if o["init"] in x["tiles"]][0]
-    pr = [p + noise * 20000 * rng.random() for p in pr]
-    pick = [0 if len(o["alts"]) == 1 else (1 if o["role"] in onv else 0) for o in ops]
-    for i, m, d in moves:
-        if not m: pick[i] = 1 - pick[i]
-        for j in range(i, min(n, i + m)): pr[j] += 1000.0 * d
+        pr[i] = du[i] + after(o, M) + max([pr[j] for j in succ[i]], default=-o.get("turn", 0) * per)
     users = {}
     for i, o in enumerate(ops):
         for k in o["tiles"]: users.setdefault(k, []).append(i)
+    for i, o in enumerate(ops):
+        if "init" in o: pr[i] = 600 + pr[users[o["init"]][0]]
+    for i, o in enumerate(ops):
+        if o["sem"] in ["l" + k for k in LOADS]: pr[i] = 1e9 - i
+    for i in range(n - 1, -1, -1): pr[i] = max([pr[i]] + [du[i] + after(ops[i], M) + pr[j] for j in succ[i]])
     last = {p: [[] for _ in range(m)] for p, m in POOLS.items()}
     held = {p: [0] * m for p, m in POOLS.items()}
     live = {p: np.zeros(n + 1, int) for p in POOLS}
@@ -425,30 +398,30 @@ def plan(ops, M, seed, look=0.5, noise=0.03, onv=(), per=32000, off=20000, infl=
         if "init" in o: held[o["init"][0]][o["init"][1]] = 1; live[o["init"][0]][:i + 1] += 1
     cur = 0
     free = {e: 0.0 for e in "VAPGS"}; left = [len(o["dep"]) for o in ops]; avail = [0.0] * n; fin = [0.0] * n
-    where = {}; prev = {}; since = {}; order = []; extra = {}; placed = 0
+    where = {}; prev = {}; since = {}; order = []; extra = {}; placed = [False] * (n + 1)
     ready = [i for i in range(n) if not left[i]]
     while ready:
         cand = []; spot = {}; most = {}
-        while placed >> cur & 1: cur += 1
-        for p in POOLS:
-            most[p] = np.maximum.accumulate(live[p][cur:])
-            fr = [(max([fin[j] for j in last[p][x]], default=-1e3), x) for x in range(POOLS[p]) if not held[p][x]]
-            spot[p] = (len(fr),) + min(fr) if fr else (0, 0, 0)
+        while placed[cur]: cur += 1
         for i in ready:
             o = ops[i]; r = avail[i]; ok = True
             for k in o["tiles"]:
-                if k in where: r = max(r, since[k])
-                elif not spot[k[0]][0] or (users[k][0] > cur and most[k[0]][users[k][0] - 1 - cur] >= POOLS[k[0]]): ok = False
-                else: r = max(r, spot[k[0]][1] + M["hop"])
+                p = k[0]
+                if k in where: r = max(r, since[k]); continue
+                if p not in spot:
+                    most[p] = np.maximum.accumulate(live[p][cur:])
+                    fr = [(max([fin[j] for j in last[p][x]], default=-1e3), x) for x in range(POOLS[p]) if not held[p][x]]
+                    spot[p] = (len(fr),) + min(fr) if fr else (0, 0, 0)
+                if not spot[p][0] or (users[k][0] > cur and most[p][users[k][0] - 1 - cur] >= POOLS[p]): ok = False
+                else: r = max(r, spot[p][1] + M["hop"])
             if ok: cand.append((max(r, free[o["alts"][pick[i]][0]]), i))
-        if not cand: return None
         t0 = min(c[0] for c in cand)
         now = max((c for c in cand if c[0] <= t0 + 1.0), key=lambda c: pr[c[1]])
         eng = ops[now[1]]["alts"][pick[now[1]]][0]
-        soon = [c for c in cand if ops[c[1]]["alts"][pick[c[1]]][0] == eng and c[0] < t0 + look * du[now[1]][0] and pr[c[1]] > pr[now[1]] + 2000]
+        soon = [c for c in cand if ops[c[1]]["alts"][pick[c[1]]][0] == eng and c[0] < t0 + look * du[now[1]] and pr[c[1]] > pr[now[1]] + sticky]
         if soon: now = max(soon, key=lambda c: pr[c[1]] - 4 * (c[0] - t0))
         st, i = now; o = ops[i]; x = pick[i]; e = o["alts"][x][0]
-        fin[i] = free[e] = st + du[i][x]; extra[i] = []
+        fin[i] = free[e] = st + du[i]; extra[i] = []
         if "init" in o: held[o["init"][0]][o["init"][1]] = 0; last[o["init"][0]][o["init"][1]] = [i]; live[o["init"][0]][:i + 1] -= 1
         for k in o["tiles"]:
             p = k[0]
@@ -458,36 +431,14 @@ def plan(ops, M, seed, look=0.5, noise=0.03, onv=(), per=32000, off=20000, infl=
                 live[p][:users[k][0]] += 1
             held[p][where[k]] -= 1; extra[i] += prev[k]
             if not held[p][where[k]]: live[p][:users[k][-1] + 1] -= 1
-        order.append((i, x)); ready.remove(i); placed |= 1 << i
+        order.append((i, x)); ready.remove(i); placed[i] = True
         for j in succ[i]:
             avail[j] = max(avail[j], fin[i] + after(o, M)); left[j] -= 1
             if not left[j]: ready.append(j)
-    return order, where, extra, max(fin[i] + after(ops[i], M) for i in range(n))
+    return order, where, extra
 
 
-def place(ops, order, M):
-    users = {}
-    for i, o in enumerate(ops):
-        for k in o["tiles"]: users.setdefault(k, []).append(i)
-    last = {p: [[] for _ in range(m)] for p, m in POOLS.items()}; held = {p: [0] * m for p, m in POOLS.items()}
-    for o in ops:
-        if "init" in o: held[o["init"][0]][o["init"][1]] = 1
-    free = {e: 0.0 for e in "VAPGS"}; done = {}; where = {}; prev = {}; extra = {}
-    for i, x in order:
-        o = ops[i]; e, cost, _ = o["alts"][x]; extra[i] = []
-        if "init" in o: held[o["init"][0]][o["init"][1]] = 0; last[o["init"][0]][o["init"][1]] = [i]
-        for k in o["tiles"]:
-            p = k[0]
-            if k not in where:
-                b = min((max([done[j] for j in last[p][y]], default=0.0), y) for y in range(POOLS[p]) if not held[p][y])[1]
-                where[k] = b; prev[k] = last[p][b]; last[p][b] = users[k]; held[p][b] = len(users[k])
-            held[p][where[k]] -= 1; extra[i] += prev[k]
-        free[e] = max([free[e]] + [done[d] for d in o["dep"] + extra[i]]) + dur(cost, M); done[i] = free[e] + after(o, M)
-    return order, where, extra, max(done.values())
-
-
-def replay(ops, sched, M):
-    order, _, extra, _ = sched
+def replay(ops, order, extra, M):
     free = {e: 0.0 for e in "VAPGS"}; done = {}; busy = {e: 0.0 for e in "VAPGS"}
     for i, x in order:
         o = ops[i]; e, cost, _ = o["alts"][x]
@@ -496,21 +447,23 @@ def replay(ops, sched, M):
     return max(done.values()), busy
 
 
-PLAN = (65, 0.0, 0.0, ("ovg1", "hvg1", "hdd", "odd", "ocs"), 26000, 17000, 14000,
-        [(397, 0, 0), (76, 19, -8), (157, 24, 2), (130, 20, -2), (344, 21, -4), (124, 6, -4), (320, 4, 8), (191, 19, 2), (692, 9, 8), (751, 0, 0), (866, 14, 1), (576, 13, -1), (162, 2, 2), (822, 9, -2), (847, 1, 8), (532, 16, -2), (877, 4, -1), (369, 6, 8)])
-ORDER = """1 2 6 4 3 7 5 9 12 13 10 8 11 72 71 66 60 70 63 15 77 75 73 90 61 21 92 17 65 14 19 18 76 62 20 25 91 37 158 100 22 30 27 31 44 43 82 32 78 79 29 26 159 87 38 160 83 28 67 86 -163 81 164 101 162 84 68 80 161 64 46 102 103 23 93 39 40 16 52 51 165 74 33 50 41 42 34 89 53 55 35 48 56 24 54 166 -105 47 167 36 57 106 49 58 168 104 107 45 169 170 171 172 173 174 175 88 176 59 85 177 178 179 108 109 180 181 110 69 182 111 183 112 185 113 114 115 116 117 118 119 120 184 -122 123 124 127 186 187 -249 -360 188 201 250 121 94 189 96 190 95 97 98 361 191 254 192 362 251 125 126 128 -302 -217 193 129 130 194 218 195 -196 197 99 303 131 232 304 132 233 133 219 134 135 364 -239 146 363 136 140 220 137 204 198 147 -138 264 265 222 205 253 306 365 366 367 368 252 139 143 -305 -211 248 221 369 216 370 307 371 372 373 308 255 223 266 374 256 375 261 376 377 153 -206 378 379 224 309 229 262 310 230 311 380 -271 -382 263 381 234 267 383 312 384 269 386 313 272 268 274 270 257 314 385 273 225 315 387 316 275 277 317 258 259 318 226 319 231 320 -451 227 260 321 322 452 388 199 202 203 278 456 144 237 240 389 390 324 207 -562 325 235 238 323 326 391 242 453 276 392 241 393 279 563 148 394 236 243 395 466 396 -504 328 327 245 397 145 330 398 141 246 208 467 200 291 564 228 505 212 209 329 292 399 506 331 213 244 566 332 -473 333 406 210 214 293 247 334 507 419 142 151 294 335 215 149 336 508 565 567 420 154 568 454 337 155 403 295 338 424 156 152 421 569 407 281 339 280 296 282 157 150 283 -422 340 341 284 570 285 455 450 342 288 -413 286 297 287 298 423 408 571 572 289 573 509 299 574 418 348 468 300 575 434 457 290 425 435 576 510 577 511 349 512 301 578 400 579 458 463 426 580 -441 436 513 459 464 431 432 -355 514 465 515 401 343 350 404 581 460 516 471 582 517 433 518 583 -584 519 585 469 427 437 520 586 521 522 470 461 588 462 523 472 524 474 475 525 -526 478 476 442 444 439 477 527 402 587 528 479 440 445 438 530 443 345 480 346 590 589 591 428 405 608 447 531 592 411 409 609 344 448 429 347 -653 593 430 594 412 595 529 532 -707 654 596 597 410 481 533 414 534 757 598 446 758 351 416 449 353 599 -621 759 493 610 535 415 536 708 494 600 537 495 601 417 538 496 354 761 760 356 539 540 550 497 357 541 498 501 499 352 482 542 709 622 483 543 551 484 485 358 605 500 502 658 486 359 655 762 547 668 503 652 710 487 711 488 636 763 764 490 489 669 765 656 657 -557 491 766 712 637 713 714 623 715 492 620 -675 -643 659 716 660 767 768 625 717 839 624 769 718 770 626 771 719 602 661 627 665 772 720 670 666 544 773 721 774 662 722 638 663 775 776 723 628 724 777 633 667 725 -615 726 671 673 634 727 778 779 603 545 552 672 629 -780 635 781 728 807 676 630 729 606 677 782 664 631 674 730 548 784 644 678 632 679 646 639 641 647 645 680 607 840 642 640 681 -808 841 648 731 682 795 618 842 649 809 813 845 604 810 611 783 650 549 683 745 616 613 844 553 612 555 619 786 843 614 696 695 697 651 556 732 846 560 746 546 617 698 684 847 554 558 685 559 812 699 686 811 700 687 733 787 855 848 849 735 823 824 796 814 852 688 561 689 856 815 850 857 -802 820 701 690 691 702 706 821 853 734 703 -862 785 854 692 851 816 817 818 693 694 858 860 822 704 792 867 833 865 828 -830 705 861 825 797 859 866 863 826 831 864 868 869 752 736 827 829 832 788 834 737 819 836 789 870 742 738 793 794 798 739 835 837 838 790 743 791 740 747 799 741 744 805 806 800 801 803 748 755 750 882 804 753 884 749 883 871 873 885 890 886 887 872 756 874 875 876 893 751 754 888 877 889 891 892 878 879 880 881"""
+CLOSE = 8
+PLAN = ({"skg1": "1", "okg1": "01234567", "hkg1": "0", "ovg0": "26", "ovg1": "135", "hvg1": "0246"}, 8000.0, 0.3, 2000.0)
 CACHE = {}
+
+
+def schedule():
+    if "s" not in CACHE:
+        ops = build(); order, where, extra = plan(ops, REF, *PLAN)
+        CACHE["s"] = (ops, order, where, extra, build(where))
+    return CACHE["s"]
 
 
 def rank_program(g, core, T, topo):
     rank = T.rank_of(core)
     if rank is None:
         return
-    if "ops" not in CACHE:
-        CACHE["ops"] = build(); order = [(abs(int(v)) - 1, int(int(v) < 0)) for v in ORDER.split()]
-        CACHE["plan"] = place(CACHE["ops"], order, REF) if order else plan(CACHE["ops"], REF, *PLAN)
-        CACHE["calls"] = build(CACHE["plan"][1])
-    ops = CACHE["ops"]; order, where, extra, _ = CACHE["plan"]
+    ops, order, where, extra, calls = schedule()
     N = len(T.cores); peer = lambda k: T.cores[(rank + k) % N]
     sent = [0]; arrive = {}
 
@@ -539,7 +492,7 @@ def rank_program(g, core, T, topo):
     Q = {"V": g.vector, "A": g.scalar, "P": g.tensor, "G": g, "S": g.sync}
     count = {}; mark = {}; waited = {e: {} for e in Q}
     for i, x in order:
-        o = ops[i]; e, _, fn = CACHE["calls"][i]["alts"][x]
+        o = ops[i]; e, _, fn = calls[i]["alts"][x]
         need = {}
         for d in o["dep"] + extra.get(i, []):
             s, v = mark[d]; need[s] = max(need.get(s, 0), v)

@@ -11,14 +11,14 @@ F32, BF, F16, I32, U16 = "float32", "bfloat16", "float16", "int32", "uint16"
 SB = lambda n, d: ("sbuf", [128, n], d)
 TILES = {"kg": ("kg", 2048, BF), "vg": ("vg", 2048, BF), "so": ("so", 2048, F32), "qd": ("qd", 1024, BF), "qh": ("qh", 1024, F16), "sg": ("sg", 256, BF), "s1": ("s1", 256, F16),
          "rb": ("rb", 512, F32), "fr": ("fr", 128, F16), "fm": ("rd", 128, F16), "inv": ("rd", 128, BF), "ee": ("rd", 128, F32), "hi": ("rd", 128, BF),
-         "lo": ("rd", 128, BF), "ofv": ("rd", 128, U16), "ofk": ("ofk", 128, U16), "ks": ("ks", 128, F32), "msc": ("msc", 256, F32),
+         "lo": ("rd", 128, BF), "ofv": ("rd", 128, U16), "ofk": ("ofk", 128, U16), "ivt": ("ofk", 128, BF), "ks": ("ks", 128, F32), "msc": ("msc", 256, F32),
          "tf": ("tt", 64, F32), "mi": ("cy", 8, I32), "fq": ("cy", 8, BF), "ofc": ("cy", 8, U16), "yt": ("yt", 32, F32),
          "zt": ("xx", 128, F32), "xx": ("xx", 16, F32), "fa": ("xx", 128, F32)}
 SCRATCH = {
     "hks": SB(W, BF), "vvs": SB(W, BF), "fws": SB(2816, BF), "bws": SB(W, BF), "nnum": SB(W, F32),
     "curi": SB(16, I32), "toki": SB(64, I32), "toku": SB(64, U16), "tokl": SB(64, U16), "thi": SB(256, I32), "thq": SB(256, F16), "thl": SB(256, BF),
     "lsl": SB((RO + 1) * NC * 8, U16), "lso": SB(RO * NC * 8, U16), "nq": SB((RO + 1) * NC * 640, F16),
-    "crs": SB(RO * NC * 128, BF), "crl": SB(RO * NC * 128, BF),
+    "crs": SB((RO - 1) * 256, F16), "tks": SB((RO - 1) * 256, BF), "tkl": SB((RO - 1) * 256, BF),
     "bks": SB(RO * NC * 144, F32), "bkl": SB(RO * NC * 144, F32), "yas": SB(1024, F32), "mss": SB(1024, F32),
     "ci": SB(16, I32), "cf": SB(32, F32), "rr": SB(160, F32), "ones": SB(512, BF), "i32": SB(128, F32), "idh": SB(128, BF),
     "inn": SB(128, BF), "inp": SB(128, BF), "a16": SB(16, F32), "a16p": SB(16, BF), "b16p": SB(16, BF), "selw": SB(64, BF),
@@ -27,15 +27,18 @@ SCRATCH = {
 }
 for _k, (_p, _n, _d) in TILES.items():
     SCRATCH[_k] = SB(POOLS[_p] * _n, _d)
-for _b in range(8):
-    SCRATCH["pb%d" % _b] = ("psum", [128, 512], F32)
+for _b in range(POOLS["ps"]):
+    SCRATCH["ps%d" % _b] = ("psum", [128, 512], F32)
 LOADS = ["cur", "tok", "fwA", "hkA", "th", "hkB", "bwA", "vvA", "fwB", "bwB", "vvB"]
 BYDMA = [k + "%d%d" % (t, c) for k in "oh" for t in range(RO) for c in range(NC) if k == "h"]
-WHOLE = ()
-SEMAPHORES = (["cV", "cA", "cP", "cG", "sent", "stored", "rtok"] + ["l" + n for n in LOADS] + ["d" + n for n in BYDMA]
+EARLY = ("31",)
+TURN = True
+SEMAPHORES = (["cV", "cA", "cP", "cG", "sent", "stored", "rtok", "rkey"] + ["l" + n for n in LOADS] + ["d" + n for n in BYDMA] + ["rM" + n for n in EARLY]
               + ["r%s%d%d" % (k, t, c) for k in "LNB" for t in range(RO) for c in range(NC)] + ["rC%d%d" % (t, c) for t in range(RO - 1) for c in range(NC)])
 
-REF = {"c": 1.0, "p": 0.6, "g": 1.56, "s": 3.8, "hop": 200.0, "net": 4000.0, "o": 30.0}
+REF = {"c": 0.9, "p": 0.52, "g": 1.56, "s": 3.8, "hop": 180.0, "net": 4000.0, "o": 10.0}
+
+CHECK = [REF, dict(REF, g=1.1, p=0.45, hop=120.0), dict(REF, g=2.0, p=0.45, hop=120.0, net=3000.0)]
 
 
 def dur(cost, M):
@@ -63,9 +66,9 @@ def build(where=None, stages=STAGES):
         x = k if where is None else where[(p, k)]
         return [((p, k, s), lambda T, a=0, b=None, st=1, s=s, n=TILES[s][1], rows=slice(None): T[s][rows, n * x + a:n * x + (n if b is None else b):st]) for s in names]
 
-    def bank():
-        k = ring.get("ps", 0); ring["ps"] = k + 1
-        return k
+    def bank(p):
+        k = ring.get(p, 0); ring[p] = k + 1
+        return p, k
 
     V = lambda n, fn, r, w, ps=None: op("V", [("v", n)], lambda e, T, B, X: [fn(e, T, B)], r, w, ps)
     A = lambda n, fn, r, w, ps=None: op("A", [("v", n)], lambda e, T, B, X: [fn(e, T, B)], r, w, ps)
@@ -77,18 +80,18 @@ def build(where=None, stages=STAGES):
            alt=[("V", [("g", n)], lambda e, T, B, X: [e.tensor_copy(out(T), win(T).indirect(off(T)))])])
         ops[-1]["role"] = who[0] + role
 
-    def P(n, mms, r, ps=None):
-        k = bank() if ps is None else ps
+    def P(n, mms, r, ps=None, pool="ps"):
+        k = bank(pool) if ps is None else ps
         op("P", [("p", n)], lambda e, T, B, X: [e.matmul(*m) for m in mms(T, B)], r, [], k)
         return k
 
     def load(q, name, fn, w, ns, n=1):
         op(q, [("n", 60 * n)], lambda e, T, B, X: fn(e, T), [], w, sem="l" + name, lat=ns)
     load("S", "cur", lambda e, T: [e.dma_start(T.curi[:], T.cur[:])], ["curi"], 2000)
-    load("S", "fwA", lambda e, T: [e.dma_start(T.fws[:, :2048], T.fw[:, :2048])], ["fwA"], 4500)
+    load("S", "hkB", lambda e, T: [e.dma_start(T.hks[:, 2304:], T.hk[:, 2304:])], ["hkB"], 3000)
     load("A", "tok", lambda e, T: [e.dma_start(T.toki[:], T.tok[:])], ["toki"], 2000)
-    load("A", "hkA", lambda e, T: [e.dma_start(T.hks[:, :2304], T.hk[:, :2304])], ["hkA"], 6000)
-    load("S", "hkB", lambda e, T: [e.dma_start(T.hks[:, 2304:], T.hk[:, 2304:])], ["hkB"], 7000)
+    load("A", "hkA", lambda e, T: [e.dma_start(T.hks[:, :2304], T.hk[:, :2304])], ["hkA"], 6500)
+    load("S", "fwA", lambda e, T: [e.dma_start(T.fws[:, :2048], T.fw[:, :2048])], ["fwA"], 6000)
     load("S", "bwA", lambda e, T: [e.dma_start(T.bws[:, :2304], T.bw[:, :2304])], ["bwA"], 9500)
     load("S", "th", lambda e, T: [e.dma_start(T.thi[x:x + 1, 128 * h:128 * h + 128], T.th[h::2, 32 * x:32 * x + 32]) for x in range(8) for h in range(2)], ["thi"], 3000, 16)
     load("S", "vvA", lambda e, T: [e.dma_start(T.vvs[:, :2304], T.vv[:, :2304])], ["vvA"], 12000)
@@ -164,8 +167,8 @@ def build(where=None, stages=STAGES):
         G(128, lambda e, T, name=name: e.affine_select(T[name][:], T.ones[:, :128], [[-1, 128]], EQ, 0.0, 0, 1), ["ones"], [name])
 
     def init(pool, k): ops[-1]["init"] = (pool, k)
-    for k in range(8):
-        op("P", [("p", 512)], lambda e, T, B, X, k=k: [e.matmul(T["pb%d" % k][:, :], T.zz[0:1, :128], T.zz[0:1, :], True, True)], ["zz"], []); init("ps", k)
+    for k in range(POOLS["ps"]):
+        op("P", [("p", 256)], lambda e, T, B, X, k=k: [e.matmul(T["ps%d" % k][:, :256], T.zz[0:1, :128], T.zz[0:1, :256], True, True)], ["zz"], []); init("ps", k)
     for k in range(POOLS["qd"]):
         if k < 2: V(512, lambda e, T, B, k=k: e.memset(T.qd[:, 1024 * k:1024 * k + 1024], 0.0), [], [])
         else: G(1024, lambda e, T, k=k: e.iota(T.qd[:, 1024 * k:1024 * k + 1024], [[0, 1024]], 0, 0, **IO), [], [])
@@ -187,13 +190,15 @@ def build(where=None, stages=STAGES):
     def send(name, src, dst, r, w, to, extra):
         op("G", [("n", 600)], lambda e, T, B, X: X["send"](name, src(T), dst(T), to), r, w, sem=name, lat=-1 - extra)
 
+    gather(768, lambda T: T.tks[:], lambda T: T.hks[:, :], lambda T: T.tokl[:, 16:64], ["hkA", "hkB", "tokl"], ["tks"], "tk")
+    send("rkey", lambda T: T.tks[:], lambda T: T.tkl[:], ["tks"], ["tkl"], -1, 2000)
+
     def halves(name, win, wk, off, ok):
         (k, v), = tiles(name)
-        if who[0] + name in WHOLE:
-            gather(2048, v, win, off, wk + [ok], [k + (0,), k + (1,)], name + "0")
-            return [k + (0,), k + (1,)], v
         for h in range(2):
             gather(1024, lambda T, h=h: v(T, 1024 * h, 1024 * h + 1024), win, lambda T, h=h: off(T, 64 * h, 64 * h + 64), wk + [ok], [k + (h,)], name + str(h))
+        ops[-2]["alts"].append(("A", [("g", 2048)], lambda e, T, B, X: [e.activation(v(T), win(T).indirect(off(T)), AF.Copy)]))
+        ops[-1]["alts"].append(("A", [], lambda e, T, B, X: []))
         return [k + (0,), k + (1,)], v
 
     def scores(T, B, kg, qd, alone):
@@ -219,7 +224,7 @@ def build(where=None, stages=STAGES):
             Lb, kl = (lambda T: T.lsl[:, 8 * (x + NC):8 * (x + NC) + 8]), "Lc%d%d" % (t + 1, c)
             ob, kb, oc, kc = 640 * (x + NC) + 256, "nc%d%d" % (t + 1, c), 640 * (x + NC) + 512, "hq" + tc
         (kfm, fm), (kin, inv), (kee, ee), (khi, hi), (klo, lo), (kov, ofv) = tiles("fm", "inv", "ee", "hi", "lo", "ofv")
-        (kok, ofk), = tiles("ofk")
+        (kok, ofk), (kit, ivt) = tiles("ofk", "ivt")
         VG(128, lambda e, T: e.tensor_tensor(fm(T), T.bws[:, :n].indirect(Lb(T)), T.nq[:, ob:ob + 128], ADD), ab("bw") + [kl, kb], [kfm])
         V(64, lambda e, T, B: e.tensor_scalar(ofk(T), fm(T), -1.0, float(OFS), MUL, ADD), [kfm], [kok])
         kk, kg = halves("kg", lambda T: T.hks[:, :n], ab("hk"), ofk, kok)
@@ -228,9 +233,14 @@ def build(where=None, stages=STAGES):
         P(1024, lambda T, B: scores(T, B, kg, qd, True)[64:], [kk[1], kq], ps)
         (k1, s1), = tiles("s1")
         V(256, lambda e, T, B: e.tensor_scalar(s1(T), B[:, :256], 2048.0, -2048.0, ALU.min, ALU.max), [], [k1], ps)
-        ps = P(768, lambda T, B: [(B[:, :128], s1(T, 0, 128), T.zw[:, 16:144], True, False)] + [
-            (B[32 * a:32 * a + 32, 32 * b:32 * b + 32], inv(T, 32 * b, 32 * b + 32), T.inn[:, 32 * a:32 * a + 32], False, False) for a in range(4) for b in range(4)] + [
-            (B[:, :128], s1(T, 128, 256), T.zw[:, 0:128], False, True)], [k1, kin, "zw0", "inn"])
+        if TURN:
+            V(64, lambda e, T, B: e.transpose(ivt(T), inv(T)), [kin], [kit])
+            ps = P(384, lambda T, B: [(B[:, :128], T.inn[:], ivt(T), True, False), (B[:, :128], s1(T, 0, 128), T.zw[:, 16:144], False, False),
+                                      (B[:, :128], s1(T, 128, 256), T.zw[:, 0:128], False, True)], [k1, kit, "zw0", "inn"])
+        else:
+            ps = P(768, lambda T, B: [(B[:, :128], s1(T, 0, 128), T.zw[:, 16:144], True, False)] + [
+                (B[32 * a:32 * a + 32, 32 * b:32 * b + 32], inv(T, 32 * b, 32 * b + 32), T.inn[:, 32 * a:32 * a + 32], False, False) for a in range(4) for b in range(4)] + [
+                (B[:, :128], s1(T, 128, 256), T.zw[:, 0:128], False, True)], [k1, kin, "zw0", "inn"])
         (km, msc), = tiles("msc")
         if own and t + 1 < RO:
             (kx, ks), = tiles("ks"); (kmi, mi), (kfq, fq), (kof, ofc) = tiles("mi", "fq", "ofc")
@@ -240,8 +250,8 @@ def build(where=None, stages=STAGES):
             p2 = P(384, lambda T, B: [m for b in range(2) for m in [(B[:, b:8:2], T.idh[:], T.cb[:, b:8:2], True, False)] + [
                 (B[:, b:8:2], T.zw[:, 160 * b + 16 - 16 * (h - b):160 * b + 144 - 16 * (h - b)], fq(T, h, 8, 2), False, h == 1) for h in range(2)]], [kfq, "idh", "cb", "zw0", "zw1"])
             V(8, lambda e, T, B: e.tensor_scalar(ofc(T), B[:, :8], -32.0, None, MUL), [], [kof], p2)
-            gather(128, lambda T: T.crs[:, 128 * x:128 * x + 128], kg, ofc, kk + [kof], ["cs" + tc], "cs")
-            send("rC" + tc, lambda T: T.crs[:, 128 * x:128 * x + 128], lambda T: T.crl[:, 128 * x:128 * x + 128], ["cs" + tc], ["cl" + tc], 1, 250)
+            VG(128, lambda e, T: e.tensor_tensor(T.crs[:, 128 * x:128 * x + 128], kg(T).indirect(ofc(T)), T.tkl[:, 128 * x:128 * x + 128], ALU.max), kk + [kof, "tkl"], ["cs" + tc])
+            send("rC" + tc, lambda T: T.crs[:, 128 * x:128 * x + 128], lambda T: T.nq[:, 640 * (x + NC) + 128:640 * (x + NC) + 256], ["cs" + tc], ["qq%d%d" % (t + 1, c)], 1, 250)
             kmx, mx = kmi, mi
         else:
             V(128, lambda e, T, B: e.tensor_tensor_scan(msc(T, 0, 128), T.m16[:, :128], B[:, :128], 0.0, MUL, ALU.max), ["m16"], [km + (0,)], ps)
@@ -281,8 +291,6 @@ def build(where=None, stages=STAGES):
                 yield
                 q = lambda T: T.nq[:, on + 128:on + 256]
                 if t == 0: VG(128, lambda e, T: e.tensor_copy(q(T), T.hks[:, :].indirect(T.toku[:, 8 * c:8 * c + 8])), ["hkA", "hkB", "toku"], ["qq" + tc])
-                else: VG(128, lambda e, T: e.tensor_tensor(q(T), T.hks[:, :].indirect(T.tokl[:, 8 * x:8 * x + 8]), T.crl[:, 128 * (x - NC):128 * (x - NC) + 128], ALU.max),
-                         ["hkA", "hkB", "tokl", "cl%d%d" % (t - 1, c)], ["qq" + tc])
                 kq, qd = spread("o" + tc, on + 128, ["qq" + tc])
                 ps = P(1024 + 256, lambda T, B: [(B[:, :256], T.thl[0:8, 128 * c:128 * c + 128], T.thq[0:8, :], True, False)] + scores(T, B, kg, qd, False)[:64], [kk[0], kq, "thl", "thq"])
                 P(1024 + 64, lambda T, B: scores(T, B, kg, qd, False)[64:] + [(B[:, :CLOSE], T.zz[0:1, :128], T.zz[0:1, :CLOSE], False, True)], [kk[1], kq, "zz"], ps)
@@ -315,15 +323,18 @@ def build(where=None, stages=STAGES):
                 kmx, mx, ksm, msc, so, kso = yield from read(t, c, False, kq, qd)
                 A(16, lambda e, T, B: e.activation(T.bks[:, ob + 128:ob + 144], msc(T, 15, 256, 16), AF.Copy), [kmx, ksm], ["bm" + tc])
                 V(256, lambda e, T, B: e.tensor_tensor(T.bks[:, ob:ob + 128], so(T, 7, 1024, 8), so(T, 1031, 2048, 8), ADD), kso, ["ba" + tc])
-                send("rB" + tc, lambda T: T.bks[:, ob:ob + 144], lambda T: T.bkl[:, ob:ob + 144], ["bm" + tc, "ba" + tc], ["bl" + tc], -1, 600)
+                if tc in EARLY:
+                    send("rM" + tc, lambda T: T.bks[:, ob + 128:ob + 144], lambda T: T.bkl[:, ob + 128:ob + 144], ["bm" + tc], ["bn" + tc], -1, 0)
+                    send("rB" + tc, lambda T: T.bks[:, ob:ob + 128], lambda T: T.bkl[:, ob:ob + 128], ["ba" + tc], ["bl" + tc], -1, 550)
+                else: send("rB" + tc, lambda T: T.bks[:, ob:ob + 144], lambda T: T.bkl[:, ob:ob + 144], ["bm" + tc, "ba" + tc], ["bl" + tc, "bn" + tc], -1, 600)
             run["h", NC * t + c] = helper()
         for c in range(NC):
             def both(t=t, c=c):
                 kmx, mx, ksm, msc, so, kso = keep[NC * t + c]
                 tc = "%d%d" % (t, c); ob = 144 * (NC * t + c); oy = 256 * t + 128 * c; bl = "bl" + tc
                 (kz, zt), (kx, xx), (kf, fa) = tiles("zt", "xx", "fa")
-                V(16, lambda e, T, B: e.tensor_tensor(zt(T, 0, 128, 16), mx(T), T.bkl[:, ob + 128:ob + 136], ALU.max), [kmx, bl], [kz + (0,)])
-                V(16, lambda e, T, B: e.tensor_tensor(xx(T, 0, 8), msc(T, 143, 256, 16), T.bkl[:, ob + 136:ob + 144], ADD), [ksm, bl], [kx + (0,)])
+                V(16, lambda e, T, B: e.tensor_tensor(zt(T, 0, 128, 16), mx(T), T.bkl[:, ob + 128:ob + 136], ALU.max), [kmx, "bn" + tc], [kz + (0,)])
+                V(16, lambda e, T, B: e.tensor_tensor(xx(T, 0, 8), msc(T, 143, 256, 16), T.bkl[:, ob + 136:ob + 144], ADD), [ksm, "bn" + tc], [kx + (0,)])
                 A(8, lambda e, T, B: e.activation(xx(T, 8, 16), zt(T, 0, 128, 16), AF.Exp, scale=-0.0078125), [kz + (0,)], [kx + (1,)])
                 V(16, lambda e, T, B: e.tensor_tensor(zt(T, 1, 128, 16), xx(T, 0, 8), xx(T, 8, 16), MUL), [kx + (0,), kx + (1,)], [kz + (1,)])
                 V(128, lambda e, T, B: e.transpose(T.mss[:, oy:oy + 128], zt(T)), [kz + (0,), kz + (1,)], ["mo" + tc])
@@ -340,10 +351,10 @@ def build(where=None, stages=STAGES):
                 yield
             run["b", NC * t + c] = both()
     for k in range(-NC, RO * NC + 8):
-        for name, lag in stages:
+        for j, (name, lag) in enumerate(stages):
             if 0 <= k - lag < RO * NC:
                 first = len(ops); next(run[name, k - lag], None)
-                for o in ops[first:]: o["turn"] = k
+                for o in ops[first:]: o["turn"] = k; o["stage"] = j
     lastw, readers, acc = {}, {}, {}
     for i, o in enumerate(ops):
         d = set()
@@ -357,7 +368,7 @@ def build(where=None, stages=STAGES):
         for k in o["r"]: readers.setdefault(k, []).append(i)
         for k in o["w"]: lastw[k] = i; readers[k] = []
         d.discard(i); o["dep"] = sorted(d)
-        o["tiles"] = sorted(set(k[:2] for k in o["r"] + o["w"] if isinstance(k, tuple)) | ({("ps", o["ps"])} if o["ps"] is not None else set()))
+        o["tiles"] = sorted(set(k[:2] for k in o["r"] + o["w"] if isinstance(k, tuple)) | ({o["ps"]} if o["ps"] is not None else set()))
     return ops
 
 
@@ -366,22 +377,18 @@ def after(o, M):
     return o["lat"] if o["lat"] >= 0 else M["net"] - o["lat"]
 
 
-def plan(ops, M, onv=(), per=0.0, look=0.5, sticky=0.0):
+def plan(ops, M, per, look, sticky, idle, marg, slack=1e9, cap=99, lead=99, ahead=(0,) * 7):
     n = len(ops)
     succ = [[] for _ in ops]
     for i, o in enumerate(ops):
         for d in o["dep"]: succ[d].append(i)
-    pick = [0 if len(o["alts"]) == 1 else int(o["role"] in onv) for o in ops]
-    seen = {}
-    for i, o in enumerate(ops):
-        if len(o["alts"]) > 1:
-            k = seen.get(o["role"], 0); seen[o["role"]] = k + 1
-            pick[i] = int(str(k) in onv.get(o["role"], ""))
+    pick = [0] * n
     du = [dur(o["alts"][pick[i]][1], M) for i, o in enumerate(ops)]
     pr = [0.0] * n
     for i in range(n - 1, -1, -1):
         o = ops[i]
         pr[i] = du[i] + after(o, M) + max([pr[j] for j in succ[i]], default=-o.get("turn", 0) * per)
+    pr = [p + (1000.0 * ahead[o["stage"]] if "stage" in o else 0.0) for p, o in zip(pr, ops)]
     users = {}
     for i, o in enumerate(ops):
         for k in o["tiles"]: users.setdefault(k, []).append(i)
@@ -401,7 +408,7 @@ def plan(ops, M, onv=(), per=0.0, look=0.5, sticky=0.0):
     where = {}; prev = {}; since = {}; order = []; extra = {}; placed = [False] * (n + 1)
     ready = [i for i in range(n) if not left[i]]
     while ready:
-        cand = []; spot = {}; most = {}
+        cand = []; spot = {}; most = {}; rdy = {}
         while placed[cur]: cur += 1
         for i in ready:
             o = ops[i]; r = avail[i]; ok = True
@@ -414,7 +421,14 @@ def plan(ops, M, onv=(), per=0.0, look=0.5, sticky=0.0):
                     spot[p] = (len(fr),) + min(fr) if fr else (0, 0, 0)
                 if not spot[p][0] or (users[k][0] > cur and most[p][users[k][0] - 1 - cur] >= POOLS[p]): ok = False
                 else: r = max(r, spot[p][1] + M["hop"])
-            if ok: cand.append((max(r, free[o["alts"][pick[i]][0]]), i))
+            if ok: cand.append((max(r, free[o["alts"][pick[i]][0]]), i)); rdy[i] = r
+        flex = [c for c in cand if len(ops[c[1]]["alts"]) > 1 and not pick[c[1]] and du[c[1]] > 500 and max(rdy[c[1]], free["V"]) + marg < c[0]]
+        if flex:
+            tv = min(max(rdy[c[1]], free["V"]) for c in flex)
+            c = max((c for c in flex if max(rdy[c[1]], free["V"]) <= tv + 1), key=lambda c: pr[c[1]])
+            nv = min([y[0] for y in cand if ops[y[1]]["alts"][pick[y[1]]][0] == "V" and pr[y[1]] > pr[c[1]] - slack], default=1e12)
+            if tv <= min(y[0] for y in cand) and nv > tv + idle and sum(pick) < min(cap, lead + cap * ops[c[1]].get("turn", 0) / 8):
+                pick[c[1]] = 1; cand.remove(c); cand.append((tv, c[1]))
         t0 = min(c[0] for c in cand)
         now = max((c for c in cand if c[0] <= t0 + 1.0), key=lambda c: pr[c[1]])
         eng = ops[now[1]]["alts"][pick[now[1]]][0]
@@ -438,6 +452,60 @@ def plan(ops, M, onv=(), per=0.0, look=0.5, sticky=0.0):
     return order, where, extra
 
 
+def justify(ops, order, extra, M):
+    n = len(ops); pick = dict(order); dep = [ops[i]["dep"] + extra[i] for i in range(n)]; succ = [[] for _ in ops]
+    for i in range(n):
+        for d in dep[i]: succ[d].append(i)
+    du = [dur(o["alts"][pick[i]][1], M) for i, o in enumerate(ops)]; af = [after(o, M) for o in ops]
+
+    def lay(seq, forward):
+        busy = {e: [] for e in "VAPGS"}; st = {}
+        for i in seq:
+            t = max([st[j] + du[j] + af[j] for j in dep[i]], default=0.0) if forward else max([st[j] + du[j] for j in succ[i]], default=0.0) + af[i]
+            q = busy[ops[i]["alts"][pick[i]][0]]; k = 0
+            while k < len(q) and t + du[i] > q[k][0] + 1e-6: t = max(t, q[k][1]); k += 1
+            q.insert(k, (t, t + du[i])); st[i] = t
+        return st
+    seq = [i for i, x in order]; st = lay(seq, True)
+    seq = sorted(seq[::-1], key=lambda i: -st[i] - du[i]); st = lay(seq, False)
+    seq = sorted(seq[::-1], key=lambda i: (0, i) if i < len(LOADS) else (1, -st[i] - du[i])); st = lay(seq, True)
+    return [(i, pick[i]) for i in sorted(seq, key=lambda i: st[i])]
+
+
+def place(ops, order, M):
+    users = {}
+    for i, o in enumerate(ops):
+        for k in o["tiles"]: users.setdefault(k, []).append(i)
+    last = {p: [[] for _ in range(m)] for p, m in POOLS.items()}; held = {p: [0] * m for p, m in POOLS.items()}
+    for o in ops:
+        if "init" in o: held[o["init"][0]][o["init"][1]] = 1
+    free = {e: 0.0 for e in "VAPGS"}; done = {}; where = {}; prev = {}; extra = {}
+    for i, x in order:
+        o = ops[i]; e, cost, _ = o["alts"][x]; extra[i] = []
+        if "init" in o: held[o["init"][0]][o["init"][1]] = 0; last[o["init"][0]][o["init"][1]] = [i]
+        for k in o["tiles"]:
+            p = k[0]
+            if k not in where:
+                b = min((max([done[j] for j in last[p][y]], default=0.0), y) for y in range(POOLS[p]) if not held[p][y])[1]
+                where[k] = b; prev[k] = last[p][b]; last[p][b] = users[k]; held[p][b] = len(users[k])
+            held[p][where[k]] -= 1; extra[i] += prev[k]
+        free[e] = max([free[e]] + [done[d] for d in o["dep"] + extra[i]]) + dur(cost, M); done[i] = free[e] + after(o, M)
+    return where, extra
+
+
+def join(ops, order, extra):
+    total = lambda q: sum(replay(ops, q, extra, M)[0] for M in CHECK)
+    best = total(order)
+    for i, o in enumerate(ops[:-1]):
+        pick = dict(order)
+        if len(o["alts"]) == 3 and o["alts"][2][1] and pick[i] == pick[i + 1] == 0:
+            at = min(k for k, (j, x) in enumerate(order) if j in (i, i + 1))
+            q = order[:at] + [(i, 2), (i + 1, 2)] + [y for y in order[at:] if y[0] not in (i, i + 1)]
+            s = total(q)
+            if s < best: best, order = s, q
+    return order
+
+
 def replay(ops, order, extra, M):
     free = {e: 0.0 for e in "VAPGS"}; done = {}; busy = {e: 0.0 for e in "VAPGS"}
     for i, x in order:
@@ -448,13 +516,14 @@ def replay(ops, order, extra, M):
 
 
 CLOSE = 8
-PLAN = ({"skg1": "1", "okg1": "01234567", "hkg1": "0", "ovg0": "26", "ovg1": "135", "hvg1": "0246"}, 8000.0, 0.3, 2000.0)
+PLAN = (6000.0, 0.15, 500.0, 170.0, 250.0, 1e9, 20, 99, (-2, 2, 4, -2, -4, 0, -6))
 CACHE = {}
 
 
 def schedule():
     if "s" not in CACHE:
         ops = build(); order, where, extra = plan(ops, REF, *PLAN)
+        order = justify(ops, order, extra, REF); where, extra = place(ops, order, REF); order = join(ops, order, extra)
         CACHE["s"] = (ops, order, where, extra, build(where))
     return CACHE["s"]
 
@@ -499,7 +568,7 @@ def rank_program(g, core, T, topo):
         for s, v in need.items():
             if waited[e].get(s, 0) < v:
                 Q[e].wait_ge(T.sem[s], v); waited[e][s] = v
-        B = T["pb%d" % where[("ps", o["ps"])]] if o["ps"] is not None else None
+        B = T[o["ps"][0] + str(where[o["ps"]])] if o["ps"] is not None else None
         ins = fn(Q[e], T, B, X)
         s = o["sem"] or "c" + e
         if o["sem"] and e == "G":

@@ -1,44 +1,52 @@
+import math
 import numpy as np
 from concourse.bass import DstId, RemoteDMATransfer
 from concourse.mybir import AluOpType as ALU, ActivationFunctionType as AF
 
 W, RO, NC = 3072, 4, 2
-POOLS = {"kg": 5, "vg": 4, "so": 6, "qd": 2, "qh": 2, "sg": 2, "s1": 4, "rb": 2, "fr": 2, "rd": 6, "ofk": 6, "ks": 4, "msc": 6, "tt": 2, "cy": 6, "yt": 2,
-         "xx": 2, "ps": 8}
-PEN, HB = 4096.0, 28.0
+RINGS = {"kg": {"s": 3, "o": 2, "h": 2}, "vg": {"O": 2, "H": 2}, "vt": {"O": 2, "H": 2}, "wx": {"OH": 3}, "hl": {"o": 8, "h": 4}, "wc": {"O": 2, "H": 2},
+         "sel": {"O": 3, "H": 2}, "qd": {"s": 2}, "qh": {"h": 2}, "sg": {"s": 2}, "s1": {"o": 2, "h": 2}, "rb": {"s": 2}, "fr": {"s": 3}, "rd": {"o": 2, "h": 2},
+         "ofk": {"s": 2, "o": 8, "h": 4}, "ks": {"s": 2, "o": 2}, "msc": {"o": 2, "h": 4}, "tt": {"s": 2}, "cy": {"o": 6}, "xx": {"b": 2},
+         "ps": {"so": 3, "h": 1, "b": 1}, "pa": {"OH": 3}}
+POOLS = {p: sum(r.values()) for p, r in RINGS.items()}
+PEN, BIG = 4096.0, 2.0 ** 40
 OFS = 1024
 F32, BF, F16, I32, U16 = "float32", "bfloat16", "float16", "int32", "uint16"
-SB = lambda n, d: ("sbuf", [128, n], d)
-TILES = {"kg": ("kg", 2048, BF), "vg": ("vg", 2048, BF), "so": ("so", 2048, F32), "qd": ("qd", 1024, BF), "qh": ("qh", 1024, F16), "sg": ("sg", 256, BF), "s1": ("s1", 256, F16),
-         "rb": ("rb", 512, F32), "fr": ("fr", 128, F16), "fm": ("rd", 128, F16), "inv": ("rd", 128, BF), "ee": ("rd", 128, F32), "hi": ("rd", 128, BF),
-         "lo": ("rd", 128, BF), "ofv": ("rd", 128, U16), "ofk": ("ofk", 128, U16), "ivt": ("ofk", 128, BF), "ks": ("ks", 128, F32), "msc": ("msc", 256, F32),
-         "tf": ("tt", 64, F32), "mi": ("cy", 8, I32), "fq": ("cy", 8, BF), "ofc": ("cy", 8, U16), "yt": ("yt", 32, F32),
-         "zt": ("xx", 128, F32), "xx": ("xx", 16, F32), "fa": ("xx", 128, F32)}
+SB = lambda n, d: ("sbuf", [128] + (n if isinstance(n, list) else [n]), d)
+TILES = {"kg": ("kg", 2048, BF), "vg": ("vg", 2048, BF), "vt": ("vt", 2048, BF), "wx": ("wx", [8, 8, 32], BF), "hl": ("hl", [4, 4, 16], BF),
+         "wc": ("wc", 256, BF), "sel": ("sel", 512, F32), "qd": ("qd", 1024, BF), "qh": ("qh", 1024, F16), "sg": ("sg", 256, BF), "s1": ("s1", 256, F16),
+         "rb": ("rb", 128, F32), "fr": ("fr", 128, F16), "fm": ("rd", 128, F16), "inv": ("rd", 128, BF), "ivt": ("rd", 128, BF),
+         "ofk": ("ofk", 128, U16), "ks": ("ks", 128, F32), "msc": ("msc", 256, F32),
+         "tf": ("tt", 64, F32), "mi": ("cy", 8, I32), "fq": ("cy", 8, BF), "ofc": ("cy", 8, U16),
+         "zt": ("xx", 256, F32), "xx": ("xx", 32, F32), "fa": ("xx", 256, F32)}
 SCRATCH = {
     "hks": SB(W, BF), "vvs": SB(W, BF), "fws": SB(2816, BF), "bws": SB(W, BF), "nnum": SB(W, F32),
-    "curi": SB(16, I32), "toki": SB(64, I32), "toku": SB(64, U16), "tokl": SB(64, U16), "thi": SB(256, I32), "thq": SB(256, F16), "thl": SB(256, BF),
+    "curi": SB(16, I32), "toki": SB(64, I32), "toku": SB(64, U16), "tokl": SB(64, U16), "thi": SB([8, 32], I32), "thq": SB(256, F16), "thl": SB(256, BF),
     "lsl": SB((RO + 1) * NC * 8, U16), "lso": SB(RO * NC * 8, U16), "nq": SB((RO + 1) * NC * 640, F16),
     "crs": SB((RO - 1) * 256, F16), "tks": SB((RO - 1) * 256, BF), "tkl": SB((RO - 1) * 256, BF),
-    "bks": SB(RO * NC * 144, F32), "bkl": SB(RO * NC * 144, F32), "yas": SB(1024, F32), "mss": SB(1024, F32),
-    "ci": SB(16, I32), "cf": SB(32, F32), "rr": SB(160, F32), "ones": SB(512, BF), "i32": SB(128, F32), "idh": SB(128, BF),
-    "inn": SB(128, BF), "inp": SB(128, BF), "a16": SB(16, F32), "a16p": SB(16, BF), "b16p": SB(16, BF), "selw": SB(64, BF),
-    "zw": SB(320, BF), "yh": SB(288, BF), "dq": SB(192, BF), "cb": SB(8, F16), "sel0": SB(128, F32), "rsel": SB(2048, BF),
-    "m16": SB(272, F32), "rk": SB(272, F32), "c9": SB(16, F32), "zz": SB(512, BF), "ofq": SB(8, U16), "ofr": SB(2, U16),
+    "bks": SB(RO * NC * 272, F32), "bkl": SB([RO * NC, 272], F32), "yas": SB(1024, F32), "mss": SB(1024, F32),
+    "ci": SB(16, I32), "cf": SB(32, F32), "rr": SB(160, F32), "ones": SB(128, BF), "dgs": SB(128, F32), "idh": SB(128, BF),
+    "inn": SB(128, BF), "idn": SB(128, BF), "a16": SB(48, F32), "mso": SB((RO - 1) * 256, F32), "selw": SB(64, BF), "zw": SB(320, BF), "cb": SB(8, F16), "sel0": SB(128, F32), "msk": SB(128, F32), "i32": SB(128, F32),
+    "m16": SB(272, F32), "rk": SB(144, F32), "c9": SB(16, F32), "zz": SB(1024, BF), "ofq": SB(8, U16), "ofr": SB(2, U16),
 }
 for _k, (_p, _n, _d) in TILES.items():
-    SCRATCH[_k] = SB(POOLS[_p] * _n, _d)
+    SCRATCH[_k] = SB([POOLS[_p] * _n[0]] + _n[1:] if isinstance(_n, list) else POOLS[_p] * _n, _d)
 for _b in range(POOLS["ps"]):
     SCRATCH["ps%d" % _b] = ("psum", [128, 512], F32)
-LOADS = ["cur", "tok", "fwA", "hkA", "th", "hkB", "bwA", "vvA", "fwB", "bwB", "vvB"]
+for _b in range(POOLS["pa"]):
+    SCRATCH["pa%d" % _b] = ("psum", [128, 8, 64], F32)
+LOADS = ["cur", "tok", "fwA", "hkA", "hkB", "th", "bwA", "vvA", "fwB", "bwB", "vvB"]
+LOAD = 4200
 BYDMA = [k + "%d%d" % (t, c) for k in "oh" for t in range(RO) for c in range(NC) if k == "h"]
 EARLY = ("31",)
-TURN = True
+APART = ["h21", "o21", "h30", "o30", "h31", "o31"]
 SEMAPHORES = (["cV", "cA", "cP", "cG", "sent", "stored", "rtok", "rkey"] + ["l" + n for n in LOADS] + ["d" + n for n in BYDMA] + ["rM" + n for n in EARLY]
+              + ["w%s%d%d" % (k, t, c) for k in "oh" for t in range(RO) for c in range(NC)]
               + ["r%s%d%d" % (k, t, c) for k in "LNB" for t in range(RO) for c in range(NC)] + ["rC%d%d" % (t, c) for t in range(RO - 1) for c in range(NC)])
 
-REF = {"c": 0.9, "p": 0.52, "g": 1.56, "s": 3.8, "hop": 180.0, "net": 4000.0, "o": 10.0}
-
-CHECK = [REF, dict(REF, g=1.1, p=0.45, hop=120.0), dict(REF, g=2.0, p=0.45, hop=120.0, net=3000.0)]
+REF = {"c": 0.95, "p": 0.48, "g": 1.56, "s": 3.8, "hop": 180.0, "net": 4000.0, "o": 10.0, "r": 600.0, "d": 100.0, "l": 1.0}
+CHECK = [(dict(REF, c=0.83, p=0.42, hop=150.0, net=3000.0), 106.0), (dict(REF, c=0.95, p=0.48, g=1.45, s=2.5, hop=200.0, net=4200.0, r=800.0, d=130.0, l=1.2), 118.0),
+         (dict(REF, c=1.05, p=0.53, g=1.62, s=5.0, hop=120.0, net=2500.0, r=400.0, d=60.0, l=0.8), 132.0)]
 
 
 def dur(cost, M):
@@ -47,28 +55,31 @@ def dur(cost, M):
         if kind == "v": tot += max(64, n) * M["c"] + M["o"]
         elif kind == "g": tot += 60 + n * M["g"] * M["c"] + M["o"]
         elif kind == "s": tot += 60 + n * M["s"] * M["c"] + M["o"]
-        elif kind == "p": tot += n * M["p"]
         elif kind == "n": tot += n
+        else: tot += n * M[kind]
     return tot
 
 
-STAGES = [("o", 0), ("o", 0), ("o", -1), ("h", 1), ("o", 1), ("h", 2), ("b", 3)]
+STAGES = [("o", 0), ("o", 0), ("o", -1), ("h", 1), ("h", 2), ("o", 2), ("b", 3)]
 
 
-def build(where=None, stages=STAGES):
-    ops, ring, who = [], {}, ["s"]
+def build(stages=STAGES):
+    ops, ring, who, where = [], {}, ["s"], {}
 
     def op(eng, cost, fn, r, w, ps=None, sem=None, lat=0.0, alt=None):
         ops.append({"alts": [(eng, cost, fn)] + (alt or []), "r": r, "w": w, "ps": ps, "sem": sem, "lat": lat})
 
-    def tiles(*names):
-        p = TILES[names[0]][0]; k = ring.get(p, 0); ring[p] = k + 1
-        x = k if where is None else where[(p, k)]
-        return [((p, k, s), lambda T, a=0, b=None, st=1, s=s, n=TILES[s][1], rows=slice(None): T[s][rows, n * x + a:n * x + (n if b is None else b):st]) for s in names]
-
     def bank(p):
-        k = ring.get(p, 0); ring[p] = k + 1
+        c = [y for y in RINGS[p] if who[0] in y][0]; j = ring.get((p, c), 0); ring[p, c] = j + 1; k = ring.get(p, 0); ring[p] = k + 1
+        where[p, k] = sum(n for y, n in RINGS[p].items() if y < c) + j % RINGS[p][c]
         return p, k
+
+    def tiles(*names):
+        p, k = bank(TILES[names[0]][0]); x = where[p, k]
+        def view(s):
+            n = TILES[s][1]; n = n[0] if isinstance(n, list) else n
+            return lambda T, a=0, b=None, st=1, rows=slice(None), more=(): T[s][(rows, slice(n * x + a, n * x + (n if b is None else b), st)) + more]
+        return [((p, k, s), view(s)) for s in names]
 
     V = lambda n, fn, r, w, ps=None: op("V", [("v", n)], lambda e, T, B, X: [fn(e, T, B)], r, w, ps)
     A = lambda n, fn, r, w, ps=None: op("A", [("v", n)], lambda e, T, B, X: [fn(e, T, B)], r, w, ps)
@@ -85,25 +96,26 @@ def build(where=None, stages=STAGES):
         op("P", [("p", n)], lambda e, T, B, X: [e.matmul(*m) for m in mms(T, B)], r, [], k)
         return k
 
-    def load(q, name, fn, w, ns, n=1):
-        op(q, [("n", 60 * n)], lambda e, T, B, X: fn(e, T), [], w, sem="l" + name, lat=ns)
-    load("S", "cur", lambda e, T: [e.dma_start(T.curi[:], T.cur[:])], ["curi"], 2000)
-    load("S", "hkB", lambda e, T: [e.dma_start(T.hks[:, 2304:], T.hk[:, 2304:])], ["hkB"], 3000)
-    load("A", "tok", lambda e, T: [e.dma_start(T.toki[:], T.tok[:])], ["toki"], 2000)
-    load("A", "hkA", lambda e, T: [e.dma_start(T.hks[:, :2304], T.hk[:, :2304])], ["hkA"], 6500)
-    load("S", "fwA", lambda e, T: [e.dma_start(T.fws[:, :2048], T.fw[:, :2048])], ["fwA"], 6000)
-    load("S", "bwA", lambda e, T: [e.dma_start(T.bws[:, :2304], T.bw[:, :2304])], ["bwA"], 9500)
-    load("S", "th", lambda e, T: [e.dma_start(T.thi[x:x + 1, 128 * h:128 * h + 128], T.th[h::2, 32 * x:32 * x + 32]) for x in range(8) for h in range(2)], ["thi"], 3000, 16)
-    load("S", "vvA", lambda e, T: [e.dma_start(T.vvs[:, :2304], T.vv[:, :2304])], ["vvA"], 12000)
-    load("S", "fwB", lambda e, T: [e.dma_start(T.fws[:, 2048:], T.fw[:, 2048:2816])], ["fwB"], 13000)
-    load("S", "bwB", lambda e, T: [e.dma_start(T.bws[:, 2304:], T.bw[:, 2304:])], ["bwB"], 14000)
-    load("S", "vvB", lambda e, T: [e.dma_start(T.vvs[:, 2304:], T.vv[:, 2304:])], ["vvB"], 15000)
+    def load(q, name, fn, w, ns, n=1, r=()):
+        op(q, [("d", n)], lambda e, T, B, X: fn(e, T), list(r), w, sem="l" + name, lat=ns)
+    load("S", "cur", lambda e, T: [e.dma_start(T.curi[:], T.cur[:])], ["curi"], 1800)
+    load("A", "tok", lambda e, T: [e.dma_start(T.toki[:], T.tok[:])], ["toki"], 1800)
+    load("S", "fwA", lambda e, T: [e.dma_start(T.fws[:, :2048], T.fw[:, :2048])], ["fwA"], LOAD)
+    load("A", "hkA", lambda e, T: [e.dma_start(T.hks[:, :2304], T.hk[:, :2304])], ["hkA"], LOAD + 400)
+    load("A", "hkB", lambda e, T: [e.dma_start(T.hks[:, 2304:], T.hk[:, 2304:])], ["hkB"], LOAD + 800)
+    load("S", "th", lambda e, T: [e.dma_start(T.thi[x:x + 1], T.th[:, 32 * x:32 * x + 32]) for x in range(8)], ["thi"], LOAD, 8)
+    load("S", "bwA", lambda e, T: [e.dma_start(T.bws[:, :2304], T.bw[:, :2304])], ["bwA"], 3500, r=["fwA"])
+    load("S", "vvA", lambda e, T: [e.dma_start(T.vvs[:, :2304], T.vv[:, :2304])], ["vvA"], 5000, r=["hkA"])
+    load("S", "fwB", lambda e, T: [e.dma_start(T.fws[:, 2048:], T.fw[:, 2048:2816])], ["fwB"], 3500, r=["bwA"])
+    load("S", "bwB", lambda e, T: [e.dma_start(T.bws[:, 2304:], T.bw[:, 2304:])], ["bwB"], 4000, r=["bwA"])
+    load("S", "vvB", lambda e, T: [e.dma_start(T.vvs[:, 2304:], T.vv[:, 2304:])], ["vvB"], 4500, r=["bwA"])
 
     IO = dict(allow_small_or_imprecise_dtypes=True)
     G(1, lambda e, T: e.iota(T.ci[:, 0:1], [[1, 1]], 0, 1), [], ["ci0"])
     G(512, lambda e, T: e.iota(T.nnum[:, :512], [[-1, 512]], OFS, 0, **IO), [], ["num0"])
     A(512, lambda e, T, B: e.activation(T.nnum[:, 512:1024], T.nnum[:, :512], AF.Identity, bias=-512.0), ["num0"], ["num1"])
-    A(1024, lambda e, T, B: e.activation(T.nnum[:, 1024:2048], T.nnum[:, :1024], AF.Identity, bias=-1024.0), ["num0", "num1"], ["num2"])
+    V(512, lambda e, T, B: e.tensor_scalar(T.nnum[:, 1024:1536], T.nnum[:, :512], -1024.0, None, ALU.add), ["num0"], ["num2"])
+    A(512, lambda e, T, B: e.activation(T.nnum[:, 1536:2048], T.nnum[:, :512], AF.Identity, bias=-1536.0), ["num0"], ["num4"])
     G(160, lambda e, T: e.iota(T.rr[:], [[1, 160]], 0, 0, **IO), [], ["rr"])
     G(1024, lambda e, T: e.iota(T.nnum[:, 2048:], [[-1, 1024]], OFS - 2048, 0, **IO), [], ["num3"])
     ci = lambda T, k: T.ci[:, k:k + 1]
@@ -123,22 +135,17 @@ def build(where=None, stages=STAGES):
     col(9, 1, 15.0, -0.5, EQ, ADD)
     col(10, 4, 1000.0, [1], MUL, ADD)
     col(11, 5, 16.0, [10], MUL, ADD)
-    col(12, 3, 0.0, 1000.0, EQ, MUL)
-    col(26, 12, 1.0, -1.0, MUL, ADD)
-    col(13, 10, 1.0, [26], MUL, ADD)
-    col(14, 0, 1.0, [26], MUL, ADD)
-    col(15, 3, 7.0, -HB, EQ, MUL)
+    col(12, 4, -BIG, BIG, MUL, ADD)
+    col(13, 4, 1.0, 1 / BIG, MUL, ADD)
     col(16, 4, 4.0, [5], MUL, ADD)
     col(17, 1, 8.0, [16], MUL, ADD)
-    col(18, 7, -31.0, 0.0, MUL, ADD)
-    col(19, 1, 32.0, [18], MUL, ADD)
-    col(20, 2, 2.0, [19], MUL, ADD)
+    col(20, 1, 8.0, [2], MUL, ADD)
     col(21, 4, 1000.0, [0], MUL, ADD); col(22, 4, -1000.0, [0], MUL, ADD)
-    col(23, 6, 1000.0, [0], MUL, ADD); col(24, 6, -1000.0, [0], MUL, ADD)
-    col(25, 1, -0.5, -15 / 32, MUL, ADD)
+    col(25, 1, -1.0, -15 / 32, MUL, ADD); col(26, 1, -1.0, -31 / 32, MUL, ADD)
     V(1, lambda e, T, B: e.tensor_copy(T.ofr[:, 0:1], cf(T, 20)), ["cf20"], ["ofr"])
     V(8, lambda e, T, B: e.tensor_scalar(T.ofq[:], T.rr[:, 0:8], 128.0, cf(T, 17), MUL, ADD), ["rr", "cf17"], ["ofq"])
-    V(8, lambda e, T, B: e.tensor_scalar(T.cb[:], T.rr[:, 0:8], -8.0, cf(T, 25), MUL, ADD), ["rr", "cf25"], ["cb"])
+    op("V", [("v", 4)] * 2, lambda e, T, B, X: [e.tensor_scalar(T.cb[:, 4 * h:4 * h + 4], T.rr[:, 0:4], -16.0, cf(T, 25 + h), MUL, ADD) for h in range(2)],
+       ["rr", "cf25", "cf26"], ["cb"])
 
     def mark(name, a, b, k, val, shift=0.0, key=None):
         src = lambda T: T.rr[:, :b - a]
@@ -147,48 +154,48 @@ def build(where=None, stages=STAGES):
         else:
             V(b - a, lambda e, T, B: e.tensor_scalar(T[name][:, a:b], src(T), cf(T, k), cf(T, val[0]) if isinstance(val, list) else val, EQ, MUL),
               ["rr", "cf%d" % k] + (["cf%d" % val[0]] if isinstance(val, list) else []), [key or name])
-    mark("a16", 0, 16, 1, 1.0); mark("selw", 0, 64, 11, [8])
-    mark("inn", 0, 128, 0, -PEN); mark("inp", 0, 128, 14, PEN); mark("a16p", 0, 16, 10, 1.0); mark("b16p", 0, 16, 13, 1.0)
+    mark("a16", 0, 48, 1, 1.0, -16.0); mark("selw", 0, 64, 11, [8])
+    mark("inn", 0, 128, 0, -PEN); mark("idn", 0, 128, 0, -1.0); mark("dgs", 0, 128, 0, [13])
     mark("zw", 0, 160, 21, 1.0, -16.0, "zw0"); mark("zw", 160, 320, 22, 1.0, -1016.0, "zw1")
-    mark("yh", 0, 144, 23, 1.0, -8.0, "yh0"); mark("yh", 144, 288, 24, 1.0, -1008.0, "yh1")
-    V(256, lambda e, T, B: e.memset(T.zz[:], 0.0), [], ["zz"])
+    V(512, lambda e, T, B: e.memset(T.zz[:], 0.0), [], ["zz"])
     fill = lambda n, view, val, r, w: A(n, lambda e, T, B: e.activation(view(T), T.zz[:, :n], AF.Identity, bias=val), ["zz"] + r, w)
-    fill(192, lambda T: T.dq[:], 0.0, [], ["dq"])
-    op("V", [("v", 32)] * 4, lambda e, T, B, X: [e.tensor_tensor(T.dq[32 * x:32 * x + 32, 48 * x + 16:48 * x + 32], T.a16p[32 * x:32 * x + 32, :], T.b16p[32 * x:32 * x + 32, :], ALU.subtract)
-                                                 for x in range(4)], ["a16p", "b16p", "dq"], ["dq"])
-    for name, val, first in (("m16", 1.0, 0.0), ("rk", 1 / 32, -1e6)):
-        fill(272, lambda T, name=name: T[name][:], val, [], [name])
-        fill(17, lambda T, name=name: T[name][:, 0::16], first, [name], [name])
+    for name, n, val, first in (("m16", 272, 1.0, 0.0), ("rk", 144, 1 / 32, -1e6)):
+        fill(n, lambda T, name=name: T[name][:], val, [], [name])
+        fill(n // 16, lambda T, name=name: T[name][:, 0::16], first, [name], [name])
     fill(8, lambda T: T.c9[:, :8], 0.0, [], ["c9"]); fill(1, lambda T: T.c9[:, 8:9], -96.0, [], ["c9x"])
-    A(512, lambda e, T, B: e.activation(T.ones[:], T.zz[:], AF.Exp), ["zz"], ["ones"])
+    op("A", [("v", 32)] * 5, lambda e, T, B, X: [e.activation(T.msk[:, a:b:st], T.zz[:, :(b - a + st - 1) // st], AF.Identity, bias=v) for a, b, st, v in (
+        (0, 64, 2, 0.0), (1, 64, 2, cf(T, 12)), (64, 128, 4, 0.0), (65, 128, 2, 1.0), (66, 128, 4, cf(T, 12)))], ["zz", "cf12"], ["msk"])
+    A(128, lambda e, T, B: e.activation(T.ones[:], T.zz[:, :128], AF.Exp), ["zz"], ["ones"])
     G(256, lambda e, T: e.affine_select(T.thl[0:8, :], T.m16[0:8, 1:257], [[1, 8], [0, 32]], EQ, 0.0, 0, -1), ["m16"], ["thl"])
-    V(256, lambda e, T, B: e.tensor_scalar(T.thq[0:8, :], T.thi[0:8, :], -1.0, None, MUL), ["thi"], ["thq"])
+    op("V", [("v", 128)] * 2, lambda e, T, B, X: [e.tensor_scalar(T.thq[0:8, 128 * h:128 * h + 128], T.thi[0:8, h::2], -1.0, None, MUL) for h in range(2)], ["thi"], ["thq"])
     for name in ("idh", "i32"):
-        G(128, lambda e, T, name=name: e.affine_select(T[name][:], T.ones[:, :128], [[-1, 128]], EQ, 0.0, 0, 1), ["ones"], [name])
+        G(128, lambda e, T, name=name: e.affine_select(T[name][:], T.ones[:], [[-1, 128]], EQ, 0.0, 0, 1), ["ones"], [name])
 
     def init(pool, k): ops[-1]["init"] = (pool, k)
     for k in range(POOLS["ps"]):
         op("P", [("p", 256)], lambda e, T, B, X, k=k: [e.matmul(T["ps%d" % k][:, :256], T.zz[0:1, :128], T.zz[0:1, :256], True, True)], ["zz"], []); init("ps", k)
     for k in range(POOLS["qd"]):
-        if k < 2: V(512, lambda e, T, B, k=k: e.memset(T.qd[:, 1024 * k:1024 * k + 1024], 0.0), [], [])
-        else: G(1024, lambda e, T, k=k: e.iota(T.qd[:, 1024 * k:1024 * k + 1024], [[0, 1024]], 0, 0, **IO), [], [])
-        init("qd", k)
+        V(512, lambda e, T, B, k=k: e.memset(T.qd[:, 1024 * k:1024 * k + 1024], 0.0), [], []); init("qd", k)
+    zero = lambda view, key: V(512, lambda e, T, B: e.tensor_copy(view(T), T.zz[:]), ["zz", key], [key])
     for k in range(POOLS["qh"]):
-        op("V", [("v", 256)] * 2, lambda e, T, B, X, k=k: [e.tensor_copy(T.qh[:, 1024 * k + a:1024 * k + a + 512], T.zz[:]) for a in (0, 512)], ["zz"], []); init("qh", k)
-    for pool, name, n in (("rb", "rb", 256), ("tt", "tf", 64), ("xx", "zt", 128)):
+        zero(lambda T, k=k: T.qh[:, 1024 * k:1024 * k + 1024], "qz%d" % k); init("qh", k)
+    for k in range(POOLS["wx"]):
+        for a in range(0, 8, 2):
+            if k: G(512, lambda e, T, k=k, a=a: e.iota(T.wx[:, 8 * k + a:8 * k + a + 2], [[0, 512]], 0, 0, **IO), ["wz%d" % k], ["wz%d" % k])
+            elif a % 4 == 0: zero(lambda T, a=a: T.wx[:, a:a + 4], "wz0")
+        init("wx", k)
+    for pool, name, n in (("rb", "rb", 64), ("tt", "tf", 64), ("xx", "zt", 256)):
         for k in range(POOLS[pool]):
             fill(n, lambda T, o=TILES[name][1] * k, name=name, n=n: T[name][:, o:o + n], 0.0, [], []); init(pool, k)
     V(16, lambda e, T, B: e.tensor_copy(T.lsl[:, :16], T.curi[:]), ["curi"], ["Lc00", "Lc01"])
     for c in range(NC):
-        VG(128, lambda e, T, c=c: e.tensor_copy(T.nq[:, 640 * c + 256:640 * c + 384], T.nnum[:, :2048].indirect(T.lsl[:, 8 * c:8 * c + 8])), ["num0", "num1", "num2", "Lc0%d" % c], ["nc0%d" % c])
+        VG(128, lambda e, T, c=c: e.tensor_copy(T.nq[:, 640 * c + 256:640 * c + 384], T.nnum[:, :2048].indirect(T.lsl[:, 8 * c:8 * c + 8])), ["num0", "num1", "num2", "num4", "Lc0%d" % c], ["nc0%d" % c])
     V(64, lambda e, T, B: e.tensor_copy(T.toku[:], T.toki[:]), ["toki"], ["toku"])
     op("G", [("n", 3000)], lambda e, T, B, X: X["tokens"](), ["toku"], ["tokl"], sem="rtok", lat=-1)
-    for k in range(4):
-        G(512, lambda e, T, k=k: e.affine_select(T.rsel[:, 512 * k:512 * k + 512], T.ones[:], [[-1, 4], [-16, 8], [0, 16]], EQ, 0.0, -4 * k, 1), ["ones"], ["rsel%d" % k])
-    G(128, lambda e, T: e.affine_select(T.sel0[:], T.ones[:, :128], [[16, 8], [0, 16]], EQ, 0.0, 0, -1), ["ones"], ["sel0"])
+    G(128, lambda e, T: e.affine_select(T.sel0[:], T.ones[:], [[16, 8], [0, 16]], EQ, 0.0, 0, -1), ["ones"], ["sel0"])
 
     def send(name, src, dst, r, w, to, extra):
-        op("G", [("n", 600)], lambda e, T, B, X: X["send"](name, src(T), dst(T), to), r, w, sem=name, lat=-1 - extra)
+        op("G", [("r", 1)], lambda e, T, B, X: X["send"](name, src(T), dst(T), to), r, w, sem=name, lat=-1 - extra)
 
     gather(768, lambda T: T.tks[:], lambda T: T.hks[:, :], lambda T: T.tokl[:, 16:64], ["hkA", "hkB", "tokl"], ["tks"], "tk")
     send("rkey", lambda T: T.tks[:], lambda T: T.tkl[:], ["tks"], ["tkl"], -1, 2000)
@@ -202,12 +209,13 @@ def build(where=None, stages=STAGES):
         return [k + (0,), k + (1,)], v
 
     def scores(T, B, kg, qd, alone):
-        return [(B[32 * (u // 32):32 * (u // 32) + 16, u % 32:256:32], kg(T, 16 * u, 16 * u + 16), qd(T, u), alone, alone) for u in range(128)]
+        us = [y // 2 + 64 * (y % 2) if alone else y for y in range(128)]
+        return [(B[32 * (u // 32):32 * (u // 32) + 16, u % 32:256:32], kg(T, 16 * y, 16 * y + 16), qd(T, u), alone, alone) for y, u in enumerate(us)]
 
     def spread(name, src, rk):
         if name in BYDMA:
             (k, v), = tiles("qh")
-            op("S", [("n", 800)], lambda e, T, B, X: [e.dma_start(v(T, 128 * (4 * (h % 2) + h // 2), 128 * (4 * (h % 2) + h // 2) + 128, rows=slice(16 * h, 16 * h + 16)),
+            op("S", [("d", 8)], lambda e, T, B, X: [e.dma_start(v(T, 128 * (4 * (h % 2) + h // 2), 128 * (4 * (h % 2) + h // 2) + 128, rows=slice(16 * h, 16 * h + 16)),
                                                                   T.nq[16 * h:16 * h + 16, src:src + 128]) for h in range(8)], rk, [k], sem="d" + name, lat=2000)
             return k, lambda T, u: v(T, u, 1024, 128)
         (k, v), = tiles("qd")
@@ -223,60 +231,70 @@ def build(where=None, stages=STAGES):
         else:
             Lb, kl = (lambda T: T.lsl[:, 8 * (x + NC):8 * (x + NC) + 8]), "Lc%d%d" % (t + 1, c)
             ob, kb, oc, kc = 640 * (x + NC) + 256, "nc%d%d" % (t + 1, c), 640 * (x + NC) + 512, "hq" + tc
-        (kfm, fm), (kin, inv), (kee, ee), (khi, hi), (klo, lo), (kov, ofv) = tiles("fm", "inv", "ee", "hi", "lo", "ofv")
-        (kok, ofk), (kit, ivt) = tiles("ofk", "ivt")
+        (kfm, fm), (kin, inv), (kit, ivt) = tiles("fm", "inv", "ivt")
+        (kok, ofk), = tiles("ofk")
         VG(128, lambda e, T: e.tensor_tensor(fm(T), T.bws[:, :n].indirect(Lb(T)), T.nq[:, ob:ob + 128], ADD), ab("bw") + [kl, kb], [kfm])
-        V(64, lambda e, T, B: e.tensor_scalar(ofk(T), fm(T), -1.0, float(OFS), MUL, ADD), [kfm], [kok])
+        op("V", [("v", 64)] * 2, lambda e, T, B, X: [e.tensor_scalar(ofk(T, h, 128, 2), fm(T, 64 * h, 64 * h + 64), -1.0, float(OFS), MUL, ADD) for h in range(2)], [kfm], [kok])
         kk, kg = halves("kg", lambda T: T.hks[:, :n], ab("hk"), ofk, kok)
-        V(128, lambda e, T, B: e.tensor_tensor(inv(T), fm(T), T.nq[:, oc:oc + 128], ALU.is_ge), [kfm, kc], [kin])
-        ps = P(1024, lambda T, B: scores(T, B, kg, qd, True)[:64], [kk[0], kq])
+        ps = P(256, lambda T, B: [(B[:, 384:512], T.idh[:], fm(T), True, False), (B[:, 384:512], T.idn[:], T.nq[:, oc:oc + 128], False, True)], [kfm, kc, "idh", "idn"])
+        op("A", [("v", 128)], lambda e, T, B, X: [e.activation(inv(T), B[:, 384:512], AF.Relu, bias=1.0)], [], [kin], ps,
+           alt=[("V", [("v", 128)], lambda e, T, B, X: [e.tensor_scalar(inv(T), B[:, 384:512], 0.0, None, ALU.is_ge)])])
+        P(1024, lambda T, B: scores(T, B, kg, qd, True)[:64], [kk[0], kq], ps)
         P(1024, lambda T, B: scores(T, B, kg, qd, True)[64:], [kk[1], kq], ps)
         (k1, s1), = tiles("s1")
-        V(256, lambda e, T, B: e.tensor_scalar(s1(T), B[:, :256], 2048.0, -2048.0, ALU.min, ALU.max), [], [k1], ps)
-        if TURN:
-            V(64, lambda e, T, B: e.transpose(ivt(T), inv(T)), [kin], [kit])
-            ps = P(384, lambda T, B: [(B[:, :128], T.inn[:], ivt(T), True, False), (B[:, :128], s1(T, 0, 128), T.zw[:, 16:144], False, False),
-                                      (B[:, :128], s1(T, 128, 256), T.zw[:, 0:128], False, True)], [k1, kit, "zw0", "inn"])
-        else:
-            ps = P(768, lambda T, B: [(B[:, :128], s1(T, 0, 128), T.zw[:, 16:144], True, False)] + [
-                (B[32 * a:32 * a + 32, 32 * b:32 * b + 32], inv(T, 32 * b, 32 * b + 32), T.inn[:, 32 * a:32 * a + 32], False, False) for a in range(4) for b in range(4)] + [
-                (B[:, :128], s1(T, 128, 256), T.zw[:, 0:128], False, True)], [k1, kin, "zw0", "inn"])
-        (km, msc), = tiles("msc")
+        op("A", [("v", 256)], lambda e, T, B, X: [e.activation(s1(T), B[:, :256], AF.Copy)], [], [k1], ps, alt=[("V", [("v", 256)], lambda e, T, B, X: [e.tensor_copy(s1(T), B[:, :256])])])
+        ops[-1]["role"] = who[0] + "s1"
+        V(64, lambda e, T, B: e.transpose(ivt(T), inv(T)), [kin], [kit])
+        P(384, lambda T, B: [(B[:, 256:384], T.inn[:], ivt(T), True, False), (B[:, 256:384], s1(T, 0, 128), T.zw[:, 16:144], False, False),
+                             (B[:, 256:384], s1(T, 128, 256), T.zw[:, 0:128], False, True)], [k1, kit, "zw0", "inn"], ps)
         if own and t + 1 < RO:
+            ksm, msc = "so" + tc, lambda T, a, b, st=1: T.mso[:, 128 * x - 128 + a:128 * x - 128 + b:st]
             (kx, ks), = tiles("ks"); (kmi, mi), (kfq, fq), (kof, ofc) = tiles("mi", "fq", "ofc")
-            V(128, lambda e, T, B: e.tensor_tensor_scan(ks(T), T.rk[:, :128], B[:, :128], 0.0, ADD, ALU.max), ["rk"], [kx], ps)
+            V(128, lambda e, T, B: e.tensor_tensor_scan(ks(T), T.rk[:, :128], B[:, 256:384], 0.0, ADD, ALU.max), ["rk"], [kx], ps)
             V(8, lambda e, T, B: e.tensor_copy(mi(T), ks(T, 15, 128, 16)), [kx], [kmi])
             V(16, lambda e, T, B: e.tensor_tensor(fq(T), ks(T, 15, 128, 16), mi(T), ALU.subtract), [kx, kmi], [kfq])
-            p2 = P(384, lambda T, B: [m for b in range(2) for m in [(B[:, b:8:2], T.idh[:], T.cb[:, b:8:2], True, False)] + [
-                (B[:, b:8:2], T.zw[:, 160 * b + 16 - 16 * (h - b):160 * b + 144 - 16 * (h - b)], fq(T, h, 8, 2), False, h == 1) for h in range(2)]], [kfq, "idh", "cb", "zw0", "zw1"])
-            V(8, lambda e, T, B: e.tensor_scalar(ofc(T), B[:, :8], -32.0, None, MUL), [], [kof], p2)
+            P(384, lambda T, B: [m for b in range(2) for m in [(B[:, b:8:2], T.idh[:], T.cb[:, b:8:2], True, False)] + [
+                (B[:, b:8:2], T.zw[:, 160 * b + 16 - 16 * (h - b):160 * b + 144 - 16 * (h - b)], fq(T, h, 8, 2), False, h == 1) for h in range(2)]], [kfq, "idh", "cb", "zw0", "zw1"], ps)
+            V(8, lambda e, T, B: e.tensor_scalar(ofc(T), B[:, :8], -32.0, None, MUL), [], [kof], ps)
             VG(128, lambda e, T: e.tensor_tensor(T.crs[:, 128 * x:128 * x + 128], kg(T).indirect(ofc(T)), T.tkl[:, 128 * x:128 * x + 128], ALU.max), kk + [kof, "tkl"], ["cs" + tc])
             send("rC" + tc, lambda T: T.crs[:, 128 * x:128 * x + 128], lambda T: T.nq[:, 640 * (x + NC) + 128:640 * (x + NC) + 256], ["cs" + tc], ["qq%d%d" % (t + 1, c)], 1, 250)
             kmx, mx = kmi, mi
         else:
-            V(128, lambda e, T, B: e.tensor_tensor_scan(msc(T, 0, 128), T.m16[:, :128], B[:, :128], 0.0, MUL, ALU.max), ["m16"], [km + (0,)], ps)
+            (km, msc), = tiles("msc"); ksm = km + (1,)
+            V(128, lambda e, T, B: e.tensor_tensor_scan(msc(T, 0, 128), T.m16[:, :128], B[:, 256:384], 0.0, MUL, ALU.max), ["m16"], [km + (0,)], ps)
             kmx, mx = km + (0,), lambda T: msc(T, 15, 128, 16)
-        A(128, lambda e, T, B: e.activation(ee(T), B[:, :128], AF.Exp, scale=0.0078125), [], [kee], ps)
-        V(128, lambda e, T, B: e.tensor_tensor_scan(msc(T, 128, 256), T.m16[:, :128], ee(T), 0.0, MUL, ADD), ["m16", kee], [km + (1,)])
+        (khl, hl), = tiles("hl")
+        op("A", [("v", 128), ("v", 64), ("v", 64)], lambda e, T, B, X: [e.activation(o, B[:, a:b], AF.Exp, scale=0.0078125) for o, a, b in (
+            (B[:, 384:512], 256, 384), (hl(T, more=(0,)), 256, 320), (hl(T, more=(1,)), 320, 384))], [], [khl + (0,)], ps)
+        op("V", [("v", 64)] * 2, lambda e, T, B, X: [e.tensor_tensor(hl(T, more=(2 + h,)), B[:, 384 + 64 * h:448 + 64 * h], hl(T, more=(h,)), ALU.subtract) for h in range(2)],
+           [khl + (0,)], [khl + (1,)], ps)
+        V(128, lambda e, T, B: e.tensor_tensor_scan(msc(T, 128, 256), T.m16[:, :128], B[:, 384:512], 0.0, MUL, ADD), ["m16"], [ksm], ps)
         yield
-        who[0] = "o" if own else "h"
-        ps = P(1280, lambda T, B: [(B[:, :128], T.inn[:], inv(T), True, False)] + [
-            (B[32 * a:32 * a + 32, 32 * b:32 * b + 32], T.dq[:, 48 * b + 16 - 16 * h:48 * b + 48 - 16 * h], s1(T, 128 * h + 32 * a, 128 * h + 32 * a + 32), False, False)
-            for a in range(4) for h in range(2) for b in range(4)] + [(B[:, :128], T.inp[:], inv(T), False, True)], [kin, k1, "inn", "inp", "dq"])
-        op("A", [("v", 128)] * 2, lambda e, T, B, X: [e.activation(o, B[:, :128], AF.Exp, bias=cf(T, 15), scale=0.0078125) for o in (hi(T), B[:, 128:256])], ["cf15"], [khi], ps)
-        V(128, lambda e, T, B: e.tensor_tensor(lo(T), B[:, 128:256], hi(T), ALU.subtract), [khi], [klo], ps)
-        ps = P(256, lambda T, B: [(B[:, 64 * h:64 * h + 64], T.yh[:, 144 * h + 8 - 8 * (u - h):144 * h + 136 - 8 * (u - h)], fm(T, u, 128, 2), u == 0, u == 1)
-                                  for h in range(2) for u in range(2)], [kfm, "yh0", "yh1"])
-        V(128, lambda e, T, B: e.tensor_scalar(ofv(T), B[:, :128], -1.0, float(OFS), MUL, ADD), [], [kov], ps)
-        kv, vg = halves("vg", lambda T: T.vvs[:, :n], ab("vv"), ofv, kov)
-        (kso, so), = tiles("so")
+        who[0] = "O" if own else "H"
+        (kwc, wc), = tiles("wc"); (kwx, wx), = tiles("wx"); (kvt, vt), = tiles("vt")
+        V(128, lambda e, T, B: e.transpose(wc(T), hl(T)), [khl + (0,), khl + (1,)], [kwc])
+        op("S", [("d", 8)], lambda e, T, B, X: [e.dma_start(wx(T, h, h + 1, rows=slice(16 * h, 16 * h + 16)), wc(T, rows=slice(16 * h, 16 * h + 16))) for h in range(8)],
+           [kwc], [kwx], sem="w" + "ho"[own] + tc, lat=2000)
+        kv, vg = halves("vg", lambda T: T.vvs[:, :n], ab("vv"), ofk, kok)
+        apart = "ho"[own] + tc in APART; nr = 8 if apart else 4; oa = 272 * x + 16
+        theirs = (lambda T: T.bkl[:, x, 16:144]) if "h" + tc in APART else lambda T: T.bkl[:, x, 17:272:2]
+        ps = P(64 * nr, lambda T, B: [(B[:, 0:nr], T.zz[0:1, :128], T.zz[0:1, :64 * nr], True, False)], ["zz"], None, "pa") if own else None
         for h in range(2):
-            for b in range(2):
-                ps = P(1024, lambda T, B, h=h, b=b: [(B[:, i:512:8], T.rsel[:, 128 * (8 * h + i):128 * (8 * h + i) + 128], y(T, 64 * b, 64 * b + 64), j == 0, j == 1)
-                                                     for i in range(8) for j, y in enumerate((hi, lo))], [khi, klo, "rsel%d" % (2 * h), "rsel%d" % (2 * h + 1)])
-                o = 1024 * h + 512 * b
-                V(512, lambda e, T, B, o=o: e.tensor_tensor_scan(so(T, o, o + 512), vg(T, o, o + 512), B[:, :], 0.0, ADD, MUL), [kv[h]], [kso + (h, b)], ps)
-        return kmx, mx, km + (1,), msc, so, [kso + (h, b) for h in range(2) for b in range(2)]
+            V(512, lambda e, T, B, h=h: e.transpose(vt(T, 1024 * h, 1024 * h + 1024), vg(T, 1024 * h, 1024 * h + 1024)), [kv[h]], [kvt + (h,)])
+            if apart:
+                ps = P(1024, lambda T, B, h=h: [(B[32 * (b // 16):32 * (b // 16) + 32, b // 8 % 2::2, 8 * (b % 8):8 * (b % 8) + 8], vt(T, 32 * b, 32 * b + 32),
+                                                 wx(T, more=(slice(4 * h, 4 * h + 4), b % 32)), not own, not own) for b in range(32 * h, 32 * h + 32)], [kvt + (h,), kwx], ps, "pa")
+            else:
+                ps = P(2048, lambda T, B, h=h: [(B[32 * (b // 16):32 * (b // 16) + 32, 0:4, 4 * (b % 16):4 * (b % 16) + 4], vt(T, 32 * b, 32 * b + 32),
+                                                 wx(T, more=(slice(4 * h + y, 4 * h + 4, 2), b % 32)), y == 0 and not own, y == 1 and not own) for b in range(32 * h, 32 * h + 32) for y in range(2)],
+                       [kvt + (h,), kwx], ps, "pa")
+        if own: P(512, lambda T, B: [(B[:, 0:nr, nr // 2 - 1::nr // 2], T.i32[:], theirs(T), False, True)], ["bl" + tc, "i32"], ps)
+        if own or apart: (ksl, sel), = tiles("sel")
+        else: ksl, sel = "ba" + tc, lambda T, a, b: T.bks[:, oa + a:oa + b]
+        op("V", [("v", 64)] * nr, lambda e, T, B, X: [e.tensor_tensor_scan(sel(T, 64 * a, 64 * a + 64), T.msk[:, 16 * nr - 64:16 * nr], B[:, a], 0.0, MUL, ADD) for a in range(nr)],
+           ["msk"], [ksl], ps)
+        if apart and not own: G(128, lambda e, T: e.affine_select(T.bks[:, oa:oa + 128], sel(T, 3, 512, 4), [[0, 128]], EQ, 0.0, 0, 0), [ksl], ["ba" + tc])
+        return kmx, mx, ksm, msc, ksl, lambda T, a: sel(T, 16 * nr * a + nr // 2 - 1, 16 * nr * a + 16 * nr, nr // 2)
 
     keep, run = {}, {}
     for t in range(RO):
@@ -289,28 +307,30 @@ def build(where=None, stages=STAGES):
                 V(64, lambda e, T, B: e.tensor_scalar(ofk(T), fr(T), float(OFS), None, ADD), [kf], [kok])
                 kk, kg = halves("kg", lambda T: T.hks[:, :n], ["hkA"] + (["hkB"] if t else []), ofk, kok)
                 yield
-                q = lambda T: T.nq[:, on + 128:on + 256]
-                if t == 0: VG(128, lambda e, T: e.tensor_copy(q(T), T.hks[:, :].indirect(T.toku[:, 8 * c:8 * c + 8])), ["hkA", "hkB", "toku"], ["qq" + tc])
+                who[0] = "s"; q = lambda T: T.nq[:, on + 128:on + 256]
+                if t == 0: gather(128, q, lambda T: T.hks[:, :], lambda T: T.toku[:, 8 * c:8 * c + 8], ["hkA", "hkB", "toku"], ["qq" + tc], "q")
                 kq, qd = spread("o" + tc, on + 128, ["qq" + tc])
-                ps = P(1024 + 256, lambda T, B: [(B[:, :256], T.thl[0:8, 128 * c:128 * c + 128], T.thq[0:8, :], True, False)] + scores(T, B, kg, qd, False)[:64], [kk[0], kq, "thl", "thq"])
-                P(1024 + 64, lambda T, B: scores(T, B, kg, qd, False)[64:] + [(B[:, :CLOSE], T.zz[0:1, :128], T.zz[0:1, :CLOSE], False, True)], [kk[1], kq, "zz"], ps)
+                ps = P(256, lambda T, B: [(B[:, :256], T.thl[0:8, 128 * c:128 * c + 128], T.thq[0:8, :], True, False)], ["thl", "thq"])
+                P(1024, lambda T, B: scores(T, B, kg, qd, False)[:64], [kk[0], kq], ps)
+                close = lambda T, B, a: [(B[:, a:a + CLOSE], T.zz[0:1, :128], T.zz[0:1, :CLOSE], False, True)]
+                P(1024 + 64, lambda T, B: scores(T, B, kg, qd, False)[64:] + close(T, B, 0), [kk[1], kq, "zz"], ps)
                 (ksg, sg), = tiles("sg")
                 A(256, lambda e, T, B: e.activation(sg(T), B[:, :256], AF.Sign, bias=cf(T, 9)), ["cf9"], [ksg], ps)
-                ps = P(1024 + 128 + 64, lambda T, B: [(B[:, :128], fr(T), T.idh[:], True, False)] + [
-                    (B[32 * a:32 * a + 32, 32 * (h % 4) + 16 * (h // 4):32 * (h % 4) + 16 * (h // 4) + 16], sg(T, 32 * h, 32 * h + 32), T.selw[:, 16 * a:16 * a + 16], False, False)
-                    for a in range(4) for h in range(8)] + [(B[:, :min(CLOSE, 128)], T.zz[0:1, :128], T.zz[0:1, :min(CLOSE, 128)], False, True)], [kf, ksg, "idh", "selw", "zz"])
-                (kx, ks), = tiles("ks"); (kt, tf), = tiles("tf"); (kr, rb), = tiles("rb"); (ky, yt), = tiles("yt")
-                V(128, lambda e, T, B: e.tensor_tensor_scan(ks(T), T.m16[:, :128], B[:, :128], 0.0, MUL, ALU.max), ["m16"], [kx], ps)
+                P(128, lambda T, B: [(B[:, 256:384], fr(T), T.idh[:], True, False)], [kf, "idh"], ps)
+                P(1024 + 64, lambda T, B: [(B[32 * a:32 * a + 32, 256 + 32 * (h % 4) + 16 * (h // 4):272 + 32 * (h % 4) + 16 * (h // 4)], sg(T, 32 * h, 32 * h + 32), T.selw[:, 16 * a:16 * a + 16],
+                                            False, False) for a in range(4) for h in range(8)] + close(T, B, 256), [ksg, "selw", "zz"], ps)
+                (kx, ks), = tiles("ks"); (kt, tf), = tiles("tf"); (kr, rb), = tiles("rb")
+                V(128, lambda e, T, B: e.tensor_tensor_scan(ks(T), T.m16[:, :128], B[:, 256:384], 0.0, MUL, ALU.max), ["m16"], [kx], ps)
                 V(8, lambda e, T, B: e.tensor_scalar(tf(T, 48, 56), ks(T, 15, 128, 16), 2.0 ** 35 - 2048, -2.0 ** 35, ADD, ADD), [kx], [kt + (0,)])
                 V(16, lambda e, T, B: e.tensor_tensor(tf(T, 0, 8), ks(T, 15, 128, 16), tf(T, 48, 56), ALU.subtract), [kx, kt + (0,)], [kt + (1,)])
                 V(9, lambda e, T, B: e.tensor_tensor_scan(tf(T, 32, 41), T.c9[:, :9], tf(T, 0, 9), 0.0, ADD, ALU.max), ["c9", "c9x", kt + (1,)], [kt + (2,)])
                 V(8, lambda e, T, B: e.tensor_scalar(tf(T, 16, 24), tf(T, 0, 8), tf(T, 40, 41), tf(T, 39, 40), ALU.is_lt, MUL), [kt + (1,), kt + (2,)], [kt + (3,)])
                 VG(16, lambda e, T: e.tensor_tensor(rb(T).indirect(T.ofr[:, 0:1]), tf(T, 0, 16), tf(T, 16, 32), ALU.max), [kt + (1,), kt + (3,), "ofr"], [kr], "s")
-                ps = P(512, lambda T, B: [(B[:, 16 * y:16 * y + 16], rb(T, y, 256, 2), T.a16[:], True, True) for y in range(2)], [kr, "a16"])
-                V(32, lambda e, T, B: e.transpose(yt(T), B[:, :32]), [], [ky], ps)
-                V(8, lambda e, T, B: e.tensor_copy(T.lso[:, 8 * x:8 * x + 8], yt(T, 0, 8)), [ky], ["Lb" + tc])
+                P(1024, lambda T, B: [(B[32 * (h // 2):32 * (h // 2) + 32, :8], T.a16[:, 16 - 16 * (h % 2):48 - 16 * (h % 2)], rb(T, 8 * h, 8 * h + 8), h % 2 == 0, h % 2 == 1)
+                                      for h in range(8)], [kr, "a16"], ps)
+                V(8, lambda e, T, B: e.tensor_copy(T.lso[:, 8 * x:8 * x + 8], B[:, :8]), [], ["Lb" + tc], ps)
                 send("rL" + tc, lambda T: T.lso[:, 8 * x:8 * x + 8], lambda T: T.lsl[:, 8 * (x + NC):8 * (x + NC) + 8], ["Lb" + tc], ["Lc%d%d" % (t + 1, c)], 1, 0)
-                VG(128, lambda e, T: e.tensor_copy(T.nq[:, on:on + 128], T.nnum[:, :n].indirect(T.lso[:, 8 * x:8 * x + 8])), ["num0", "num1", "num2", "num3", "Lb" + tc], ["nb" + tc])
+                gather(128, lambda T: T.nq[:, on:on + 128], lambda T: T.nnum[:, :n], lambda T: T.lso[:, 8 * x:8 * x + 8], ["num0", "num1", "num2", "num3", "num4", "Lb" + tc], ["nb" + tc], "nb")
                 send("rN" + tc, lambda T: T.nq[:, on:on + 384], lambda T: T.nq[:, on + 640 * NC + 256:on + 640 * NC + 640], ["nb" + tc, "qq" + tc, "nc" + tc],
                      ["nc%d%d" % (t + 1, c), "hq" + tc], 1, 700)
                 yield
@@ -318,32 +338,37 @@ def build(where=None, stages=STAGES):
             run["o", NC * t + c] = scan()
         for c in range(NC):
             def helper(t=t, c=c):
-                x = NC * t + c; tc = "%d%d" % (t, c); ob = 144 * x; oq = 640 * (x + NC) + 384
+                x = NC * t + c; tc = "%d%d" % (t, c); ob = 272 * x; oq = 640 * (x + NC) + 384; who[0] = "h"
                 kq, qd = spread("h" + tc, oq, ["hq" + tc])
-                kmx, mx, ksm, msc, so, kso = yield from read(t, c, False, kq, qd)
-                A(16, lambda e, T, B: e.activation(T.bks[:, ob + 128:ob + 144], msc(T, 15, 256, 16), AF.Copy), [kmx, ksm], ["bm" + tc])
-                V(256, lambda e, T, B: e.tensor_tensor(T.bks[:, ob:ob + 128], so(T, 7, 1024, 8), so(T, 1031, 2048, 8), ADD), kso, ["ba" + tc])
+                kmx, mx, ksm, msc, ksl, sel = yield from read(t, c, False, kq, qd)
+                G(16, lambda e, T: e.affine_select(T.bks[:, ob:ob + 16], msc(T, 15, 256, 16), [[0, 16]], EQ, 0.0, 0, 0), [kmx, ksm], ["bm" + tc])
+                part = lambda name, a, b, r, w: send(name + tc, lambda T: T.bks[:, ob + a:ob + b], lambda T: T.bkl[:, x, a:b], r, w, -1, 3.5 * (b - a))
+                end = 144 if "h" + tc in APART else 272
                 if tc in EARLY:
-                    send("rM" + tc, lambda T: T.bks[:, ob + 128:ob + 144], lambda T: T.bkl[:, ob + 128:ob + 144], ["bm" + tc], ["bn" + tc], -1, 0)
-                    send("rB" + tc, lambda T: T.bks[:, ob:ob + 128], lambda T: T.bkl[:, ob:ob + 128], ["ba" + tc], ["bl" + tc], -1, 550)
-                else: send("rB" + tc, lambda T: T.bks[:, ob:ob + 144], lambda T: T.bkl[:, ob:ob + 144], ["bm" + tc, "ba" + tc], ["bl" + tc, "bn" + tc], -1, 600)
+                    part("rM", 0, 16, ["bm" + tc], ["bn" + tc]); part("rB", 16, end, ["ba" + tc], ["bl" + tc])
+                else: part("rB", 0, end, ["bm" + tc, "ba" + tc], ["bl" + tc, "bn" + tc])
             run["h", NC * t + c] = helper()
         for c in range(NC):
             def both(t=t, c=c):
-                kmx, mx, ksm, msc, so, kso = keep[NC * t + c]
-                tc = "%d%d" % (t, c); ob = 144 * (NC * t + c); oy = 256 * t + 128 * c; bl = "bl" + tc
+                cs = [c] if t + 1 == RO else list(range(NC)) if c + 1 == NC else []
+                if not cs:
+                    yield
+                n = len(cs); x = NC * t + cs[0]; oy = 128 * x; who[0] = "b"; names = lambda s: [s + "%d%d" % (t, y) for y in cs]
+                mx = keep[x][1] if n == 1 else lambda T: T.mi[:, 8 * x:8 * x + 16]
                 (kz, zt), (kx, xx), (kf, fa) = tiles("zt", "xx", "fa")
-                V(16, lambda e, T, B: e.tensor_tensor(zt(T, 0, 128, 16), mx(T), T.bkl[:, ob + 128:ob + 136], ALU.max), [kmx, "bn" + tc], [kz + (0,)])
-                V(16, lambda e, T, B: e.tensor_tensor(xx(T, 0, 8), msc(T, 143, 256, 16), T.bkl[:, ob + 136:ob + 144], ADD), [ksm, "bn" + tc], [kx + (0,)])
-                A(8, lambda e, T, B: e.activation(xx(T, 8, 16), zt(T, 0, 128, 16), AF.Exp, scale=-0.0078125), [kz + (0,)], [kx + (1,)])
-                V(16, lambda e, T, B: e.tensor_tensor(zt(T, 1, 128, 16), xx(T, 0, 8), xx(T, 8, 16), MUL), [kx + (0,), kx + (1,)], [kz + (1,)])
-                V(128, lambda e, T, B: e.transpose(T.mss[:, oy:oy + 128], zt(T)), [kz + (0,), kz + (1,)], ["mo" + tc])
-                ps = P(512, lambda T, B: [(B[:, :128], T.sel0[:], T.mss[:, oy:oy + 128], True, True)], ["mo" + tc, "sel0"])
-                A(128, lambda e, T, B: e.activation(fa(T), B[:, :128], AF.Exp, bias=HB, scale=-0.0078125), [], [kf], ps)
-                ps = P(1536, lambda T, B: [(B[:, :128], T.i32[:], y, j == 0, j == 2) for j, y in enumerate((so(T, 7, 1024, 8), so(T, 1031, 2048, 8), T.bkl[:, ob:ob + 128]))],
-                       kso + [bl, "i32"])
-                V(128, lambda e, T, B: e.tensor_tensor(T.yas[:, oy:oy + 128], B[:, :128], fa(T), MUL), [kf], ["yo" + tc], ps)
-                op("S", [("n", 60)], lambda e, T, B, X: [e.dma_start(T.ya[:, oy:oy + 128], T.yas[:, oy:oy + 128])], ["yo" + tc], [], sem="stored", lat=2500)
+                V(32, lambda e, T, B: e.tensor_tensor(zt(T, 0, 128 * n, 16), mx(T), T.bkl[:, x:x + n, 0:8], ALU.max), [keep[x + y][0] for y in range(n)] + names("bn"), [kz + (0,)])
+                V(32, lambda e, T, B: e.tensor_tensor(xx(T, 0, 8 * n), keep[x][3](T, 143, 128 + 128 * n, 16), T.bkl[:, x:x + n, 8:16], ADD), [keep[x + y][2] for y in range(n)] + names("bn"), [kx + (0,)])
+                A(16, lambda e, T, B: e.activation(xx(T, 16, 16 + 8 * n), zt(T, 0, 128 * n, 16), AF.Exp, scale=-0.0078125), [kz + (0,)], [kx + (1,)])
+                V(32, lambda e, T, B: e.tensor_tensor(zt(T, 1, 128 * n, 16), xx(T, 0, 8 * n), xx(T, 16, 16 + 8 * n), MUL), [kx + (0,), kx + (1,)], [kz + (1,)])
+                V(128 * n, lambda e, T, B: e.transpose(T.mss[:, oy:oy + 128 * n], zt(T, 0, 128 * n)), [kz + (0,), kz + (1,)], names("mo"))
+                ps = P(512 * n, lambda T, B: [(B[:, :128 * n], T.sel0[:], T.mss[:, oy:oy + 128 * n], True, True)], names("mo") + ["sel0"])
+                A(128 * n, lambda e, T, B: e.activation(fa(T, 0, 128 * n), B[:, :128 * n], AF.Exp, scale=-0.0078125), [], [kf], ps)
+                for y in range(n):
+                    P(2048, lambda T, B, sel=keep[x + y][5]: [(B[32 * a:32 * a + 32, 32 * z:32 * z + 32], T.dgs[:, 32 * z:32 * z + 32], sel(T, a), True, True)
+                                                              for a in range(4) for z in range(4)], [keep[x + y][4], "dgs"], ps)
+                    op("V", [("v", 64)] * 2, lambda e, T, B, X, o=128 * y: [e.tensor_tensor(T.yas[:, oy + o + 64 * h:oy + o + 64 * h + 64], B[:, h:128:2], fa(T, o + 64 * h, o + 64 * h + 64), MUL)
+                                                                            for h in range(2)], [kf], [names("yo")[y]], ps)
+                op("S", [("d", 1)], lambda e, T, B, X: [e.dma_start(T.ya[:, oy:oy + 128 * n], T.yas[:, oy:oy + 128 * n])], names("yo"), [], sem="stored", lat=2500)
                 if t >= RO - 2 and c == NC - 1:
                     a, b = (0, 768) if t == RO - 2 else (768, 1024)
                     op("S", [("n", 120)], lambda e, T, B, X: [e.dma_start(T.ym[:, a:b], T.mss[0::16, a:b]), e.dma_start(T.ys[:, a:b], T.mss[1::16, a:b])],
@@ -367,14 +392,22 @@ def build(where=None, stages=STAGES):
             d.update(acc.get(o["ps"], [])); acc.setdefault(o["ps"], []).append(i)
         for k in o["r"]: readers.setdefault(k, []).append(i)
         for k in o["w"]: lastw[k] = i; readers[k] = []
-        d.discard(i); o["dep"] = sorted(d)
+        d.discard(i); o["dep"] = d
         o["tiles"] = sorted(set(k[:2] for k in o["r"] + o["w"] if isinstance(k, tuple)) | ({o["ps"]} if o["ps"] is not None else set()))
+        o["bank"] = o["ps"] and o["ps"][0] + str(where[o["ps"]])
+    users = {}; last = {o["init"]: [i] for i, o in enumerate(ops) if "init" in o}
+    for i, o in enumerate(ops):
+        for k in o["tiles"]: users.setdefault(k, []).append(i)
+    for k in sorted(users):
+        for i in users[k]: ops[i]["dep"].update(last.get((k[0], where[k]), []))
+        last[k[0], where[k]] = users[k]
+    for i, o in enumerate(ops): o["dep"] = sorted(o["dep"]); assert max(o["dep"], default=-1) < i, (i, o["w"], o["ps"])
     return ops
 
 
 def after(o, M):
     if o["sem"] is None: return M["hop"]
-    return o["lat"] if o["lat"] >= 0 else M["net"] - o["lat"]
+    return o["lat"] * M["l"] if o["lat"] >= 0 else M["net"] - o["lat"]
 
 
 def plan(ops, M, per, look, sticky, idle, marg, slack=1e9, cap=99, lead=99, ahead=(0,) * 7):
@@ -516,15 +549,174 @@ def replay(ops, order, extra, M):
 
 
 CLOSE = 8
-PLAN = (6000.0, 0.15, 500.0, 170.0, 250.0, 1e9, 20, 99, (-2, 2, 4, -2, -4, 0, -6))
+PLAN = (9500.0, 0.15, 100.0, 250.0, 400.0, 4000.0, 22, 99, (0, 4, -2, 2, -7, -2, -4))
 CACHE = {}
+
+
+def lay(ops, pick, seq, M, forward):
+    busy = {e: [] for e in "VAPGS"}; st = {}
+    for i in seq:
+        o = ops[i]; e, cost, _ = o["alts"][pick[i]]; du = dur(cost, M)
+        t = max([st[j][1] + after(ops[j], M) for j in o["dep"]], default=0.0) if forward else max([st[j][1] for j in o["succ"]], default=0.0) + after(o, M)
+        q = busy[e]; k = 0
+        while k < len(q) and t + du > q[k][0] + 1e-6: t = max(t, q[k][1]); k += 1
+        q.insert(k, (t, t + du)); st[i] = (t, t + du)
+    return st
+
+
+def arrange(ops, M, per, ahead, onv, rounds=3):
+    n = len(ops)
+    for o in ops: o["succ"] = []
+    for i, o in enumerate(ops):
+        for d in o["dep"]: ops[d]["succ"].append(i)
+    pick = [int(len(o["alts"]) > 1 and onv(o)) for o in ops]; pr = [0.0] * n
+    for i in range(n - 1, -1, -1):
+        o = ops[i]
+        pr[i] = dur(o["alts"][pick[i]][1], M) + after(o, M) + max([pr[j] for j in o["succ"]], default=-o.get("turn", 0) * per)
+    pr = [p + (1000.0 * ahead[o["stage"]] if "stage" in o else 0.0) for p, o in zip(pr, ops)]
+    for i in range(n - 1, -1, -1): pr[i] = max([pr[i]] + [1 + pr[j] for j in ops[i]["succ"]])
+    first = lambda i: (0, i) if i < len(LOADS) else (1, 0)
+    seq = sorted(range(n), key=lambda i: first(i) + (-pr[i], i)); best = None
+    for _ in range(rounds + 1):
+        st = lay(ops, pick, seq, M, True); seq = sorted(seq, key=lambda i: st[i][0])
+        order = [(i, pick[i]) for i in seq]; total = sum(replay(ops, order, {}, C)[0] / w for C, w in CHECK)
+        if best is None or total < best[0]: best = (total, order)
+        seq = sorted(seq[::-1], key=lambda i: -st[i][1]); st = lay(ops, pick, seq, M, False)
+        seq = sorted(seq[::-1], key=lambda i: first(i) + (-st[i][1],))
+    return best[1]
+
+
+def plan2(ops, M, per, ahead, look, sticky, bias, vmin, slack):
+    n = len(ops); succ = [[] for _ in ops]
+    for i, o in enumerate(ops):
+        for d in o["dep"]: succ[d].append(i)
+    du = [[dur(a[1], M) for a in o["alts"][:2]] for o in ops]; pr = [0.0] * n
+    for i in range(n - 1, -1, -1):
+        o = ops[i]; pr[i] = du[i][0] + after(o, M) + max([pr[j] for j in succ[i]], default=-o.get("turn", 0) * per)
+    pr = [p + (1000.0 * ahead[o["stage"]] if "stage" in o else 0.0) for p, o in zip(pr, ops)]
+    for i in range(len(LOADS)): pr[i] = 1e9 - i
+    for i in range(n - 1, -1, -1): pr[i] = max([pr[i]] + [du[i][0] + after(ops[i], M) + pr[j] for j in succ[i]])
+    free = {e: 0.0 for e in "VAPGS"}; left = [len(o["dep"]) for o in ops]; avail = [0.0] * n; order = []
+    ready = [i for i in range(n) if not left[i]]
+    rest = {e: sum(du[i][0] for i, o in enumerate(ops) if o["alts"][0][0] == e) for e in "VAPGS"}
+    while ready:
+        cand = [(max(avail[i], free[ops[i]["alts"][x][0]]) + (bias if x else 0), i, x) for i in ready for x in range(len(du[i]))
+                if not x or du[i][1] < 500 or free["V"] + rest["V"] + 2 * du[i][1] + slack <= free["A"] + rest["A"]]
+        t0 = min(c[0] for c in cand)
+        now = max((c for c in cand if c[0] <= t0 + 1.0), key=lambda c: (pr[c[1]] - (vmin if c[2] else 0), -c[2]))
+        eng = ops[now[1]]["alts"][now[2]][0]
+        soon = [c for c in cand if ops[c[1]]["alts"][c[2]][0] == eng and c[0] < t0 + look * du[now[1]][now[2]] and pr[c[1]] - (vmin if c[2] else 0) > pr[now[1]] - (vmin if now[2] else 0) + sticky]
+        if soon: now = max(soon, key=lambda c: pr[c[1]] - 4 * (c[0] - t0))
+        st, i, x = now; e = ops[i]["alts"][x][0]; st = max(avail[i], free[e])
+        free[e] = st + du[i][x]; order.append((i, x)); ready.remove(i); rest[ops[i]["alts"][0][0]] -= du[i][0]
+        for j in succ[i]:
+            avail[j] = max(avail[j], free[e] + after(ops[i], M)); left[j] -= 1
+            if not left[j]: ready.append(j)
+    return order
+
+
+def polish(ops, order, M, rounds=2):
+    for o in ops: o["succ"] = []
+    for i, o in enumerate(ops):
+        for d in o["dep"]: ops[d]["succ"].append(i)
+    pick = dict(order); seq = [i for i, x in order]
+    first = lambda i: (0, i) if i < len(LOADS) else (1, 0)
+    tot = lambda q: sum(replay(ops, q, {}, C)[0] / w for C, w in CHECK)
+    best = (tot(order), order)
+    st = lay(ops, pick, seq, M, True)
+    for _ in range(rounds):
+        seq = sorted(seq[::-1], key=lambda i: -st[i][1]); st = lay(ops, pick, seq, M, False)
+        seq = sorted(seq[::-1], key=lambda i: first(i) + (-st[i][1],))
+        st = lay(ops, pick, seq, M, True); seq = sorted(seq, key=lambda i: st[i][0])
+        q = [(i, pick[i]) for i in seq]; s = tot(q)
+        if s < best[0]: best = (s, q)
+    return best[1]
+
+
+def improve(ops, order, iters, seed=1, temp=0.0004, lam=0.15):
+    n = len(ops); state = [seed]; S = 32; head = len(LOADS)
+
+    def rnd(k=None):
+        state[0] = (state[0] * 1103515245 + 12345) % 2147483648
+        return state[0] / 2147483648 if k is None else (state[0] >> 8) % k
+    dep = [o["dep"] for o in ops]; deps = [set(d) for d in dep]
+    eng = [["VAPGS".index(a[0]) for a in o["alts"]] for o in ops]
+    tab = [[[dur(a[1], M) for a in o["alts"]] for o in ops] for M, w in CHECK]
+    af = [[after(o, M) for o in ops] for M, w in CHECK]
+
+    def run(seq, pick, m, old, k0):
+        if old is None: done = [0.0] * n; par = [None] * n; snap = [([0.0] * 5, [None] * 5)]
+        else: done = old[0][:]; par = old[1][:]; snap = old[2][:k0 // S + 1]
+        free = snap[-1][0][:]; last = snap[-1][1][:]; D = tab[m]; F = af[m]
+        for k in range(k0 // S * S, n, S):
+            for i in seq[k:k + S]:
+                x = pick[i]; e = eng[i][x]; st = free[e]; p = last[e]; q = True
+                for j in dep[i]:
+                    if done[j] > st: st = done[j]; p = j; q = False
+                free[e] = st = st + D[i][x]; last[e] = i; done[i] = st + F[i]; par[i] = (p, q)
+            snap.append((free[:], last[:]))
+        return done, par, snap
+
+    def total(seq, pick, old, k0):
+        out = [run(seq, pick, m, old and old[m], k0) for m in range(len(CHECK))]
+        return sum((max(r[0]) + lam * sum(r[0]) / n) / w for r, (M, w) in zip(out, CHECK)) / len(CHECK) / 1000, out
+    seq = [i for i, x in order]; pick = [x for i, x in sorted(order)]
+    cur, res = total(seq, pick, None, 0); best = (cur, seq, pick)
+    flex = [i for i, o in enumerate(ops) if len(o["alts"]) > 1]; pairs = [i for i in flex if len(ops[i]["alts"]) == 3 and ops[i]["alts"][2][1]]
+    for it in range(iters):
+        done, par, _ = res[rnd(len(res))]; r = rnd(); s2 = seq; p2 = pick
+        tie = lambda j, y: pick[j] == 2 and pick[y] == 2 and j == y + 1 and not tab[0][j][2]
+        if r < 0.12:
+            i = flex[rnd(len(flex))]
+            if pick[i] == 2: continue
+            p2 = list(pick); p2[i] = 1 - pick[i]; a = seq.index(i)
+            near = [j for j in seq[max(0, a - 60):a + 60] if len(eng[j]) > 1 and pick[j] == 1 - pick[i] and tab[0][j][0] == tab[0][i][0]]
+            if near and rnd() < 0.6: j = near[rnd(len(near))]; p2[j] = pick[i]; a = min(a, seq.index(j))
+        elif r < 0.2:
+            i = pairs[rnd(len(pairs))]; p2 = list(pick); a = min(seq.index(i), seq.index(i + 1))
+            if pick[i] == 2: p2[i] = 0; p2[i + 1] = rnd(2)
+            else: p2[i] = p2[i + 1] = 2; s2 = seq[:a] + [i, i + 1] + [j for j in seq[a:] if j != i and j != i + 1]
+        else:
+            if r < 0.8:
+                c = []; i = max(range(n), key=lambda j: done[j])
+                while i is not None:
+                    p, q = par[i]
+                    if q and p is not None and p >= head: c.append((i, p))
+                    i = p
+                if not c: continue
+                i, p = c[rnd(len(c))]
+            else:
+                i = rnd(n); p, q = par[i]
+                if not q or p is None or p < head: continue
+            a, b = seq.index(p), seq.index(i)
+            if rnd() < 0.5:
+                if rnd() < 0.3: a = min(a, max(head, a - (5, 15, 30)[rnd(3)]))
+                got = {i}; mv = [i]
+                for j in seq[b - 1:a - 1:-1]:
+                    if any(j in deps[y] or tie(y, j) for y in got): got.add(j); mv.append(j)
+                if p in got: continue
+                s2 = seq[:a] + mv[::-1] + [j for j in seq[a:b + 1] if j not in got] + seq[b + 1:]
+            else:
+                b = min(n - 1, b + (0, 0, 5, 15, 30)[rnd(5)]); got = {p}; mv = [p]
+                for j in seq[a + 1:b + 1]:
+                    if deps[j] & got or (j - 1 in got and tie(j, j - 1)): got.add(j); mv.append(j)
+                if i in got: continue
+                s2 = seq[:a] + [j for j in seq[a:b + 1] if j not in got] + mv + seq[b + 1:]
+        v, out = total(s2, p2, res, a)
+        if v <= cur or rnd() < math.exp((cur - v) / (temp * (1 - it / iters) + 1e-9)):
+            seq, pick, cur, res = s2, p2, v, out
+            if v < best[0]: best = (v, seq, pick)
+    return [(i, best[2][i]) for i in best[1]]
+
+
+ARR = (4500.0, (-2, -1, -12, 4, -3, -17, -7), 0.3, 250.0, 50.0, 4000.0, -500.0)
+ITERS = 36000
 
 
 def schedule():
     if "s" not in CACHE:
-        ops = build(); order, where, extra = plan(ops, REF, *PLAN)
-        order = justify(ops, order, extra, REF); where, extra = place(ops, order, REF); order = join(ops, order, extra)
-        CACHE["s"] = (ops, order, where, extra, build(where))
+        ops = build()
+        CACHE["s"] = (ops, improve(ops, polish(ops, plan2(ops, REF, *ARR), REF), ITERS))
     return CACHE["s"]
 
 
@@ -532,7 +724,7 @@ def rank_program(g, core, T, topo):
     rank = T.rank_of(core)
     if rank is None:
         return
-    ops, order, where, extra, calls = schedule()
+    ops, order = schedule()
     N = len(T.cores); peer = lambda k: T.cores[(rank + k) % N]
     sent = [0]; arrive = {}
 
@@ -561,14 +753,14 @@ def rank_program(g, core, T, topo):
     Q = {"V": g.vector, "A": g.scalar, "P": g.tensor, "G": g, "S": g.sync}
     count = {}; mark = {}; waited = {e: {} for e in Q}
     for i, x in order:
-        o = ops[i]; e, _, fn = calls[i]["alts"][x]
+        o = ops[i]; e, _, fn = o["alts"][x]
         need = {}
-        for d in o["dep"] + extra.get(i, []):
+        for d in o["dep"]:
             s, v = mark[d]; need[s] = max(need.get(s, 0), v)
         for s, v in need.items():
             if waited[e].get(s, 0) < v:
                 Q[e].wait_ge(T.sem[s], v); waited[e][s] = v
-        B = T[o["ps"][0] + str(where[o["ps"]])] if o["ps"] is not None else None
+        B = T[o["bank"]] if o["bank"] else None
         ins = fn(Q[e], T, B, X)
         s = o["sem"] or "c" + e
         if o["sem"] and e == "G":

@@ -6,10 +6,11 @@ from concourse.mybir import AluOpType as ALU, ActivationFunctionType as AF
 W, RO, NC = 3072, 4, 2
 RINGS = {"kg": {"s": 3, "o": 2, "h": 2}, "vg": {"O": 2, "H": 2}, "vt": {"O": 2, "H": 2}, "wx": {"OH": 3}, "hl": {"o": 8, "h": 4}, "wc": {"O": 2, "H": 2},
          "sel": {"O": 3, "H": 2}, "qd": {"s": 2}, "qh": {"h": 2}, "sg": {"s": 2}, "s1": {"o": 2, "h": 2}, "rb": {"s": 2}, "fr": {"s": 3}, "rd": {"o": 2, "h": 2},
-         "ofk": {"s": 2, "o": 8, "h": 4}, "ks": {"s": 2, "o": 2}, "msc": {"o": 2, "h": 4}, "tt": {"s": 2}, "cy": {"o": 6}, "xx": {"b": 2},
+         "ofk": {"s": 2, "o": 8, "h": 4}, "ks": {"o": 2}, "msc": {"o": 2, "h": 4}, "tt": {"s": 2}, "cy": {"o": 6}, "xx": {"b": 2},
          "ps": {"so": 3, "h": 1, "b": 1}, "pa": {"OH": 3}}
 POOLS = {p: sum(r.values()) for p, r in RINGS.items()}
 PEN, BIG = 4096.0, 2.0 ** 40
+HIT = 5120.0
 OFS = 1024
 F32, BF, F16, I32, U16 = "float32", "bfloat16", "float16", "int32", "uint16"
 SB = lambda n, d: ("sbuf", [128] + (n if isinstance(n, list) else [n]), d)
@@ -17,16 +18,16 @@ TILES = {"kg": ("kg", 2048, BF), "vg": ("vg", 2048, BF), "vt": ("vt", 2048, BF),
          "wc": ("wc", 256, BF), "sel": ("sel", 512, F32), "qd": ("qd", 1024, BF), "qh": ("qh", 1024, F16), "sg": ("sg", 256, BF), "s1": ("s1", 256, F16),
          "rb": ("rb", 128, F32), "fr": ("fr", 128, F16), "fm": ("rd", 128, F16), "inv": ("rd", 128, BF), "ivt": ("rd", 128, BF),
          "ofk": ("ofk", 128, U16), "ks": ("ks", 128, F32), "msc": ("msc", 256, F32),
-         "tf": ("tt", 64, F32), "mi": ("cy", 8, I32), "fq": ("cy", 8, BF), "ofc": ("cy", 8, U16),
-         "zt": ("xx", 256, F32), "xx": ("xx", 32, F32), "fa": ("xx", 256, F32)}
+         "tf": ("tt", 64, F32), "kz": ("tt", 256, F32), "dz": ("tt", 128, F32), "mi": ("cy", 8, I32), "fq": ("cy", 8, BF), "ofc": ("cy", 8, U16),
+         "zt": ("xx", 256, F32), "xx": ("xx", 32, F32), "mh": ("xx", 256, F16)}
 SCRATCH = {
     "hks": SB(W, BF), "vvs": SB(W, BF), "fws": SB(2816, BF), "bws": SB(W, BF), "nnum": SB(W, F32),
     "curi": SB(16, I32), "toki": SB(64, I32), "toku": SB(64, U16), "tokl": SB(64, U16), "thi": SB([8, 32], I32), "thq": SB(256, F16), "thl": SB(256, BF),
     "lsl": SB((RO + 1) * NC * 8, U16), "lso": SB(RO * NC * 8, U16), "nq": SB((RO + 1) * NC * 640, F16),
     "crs": SB((RO - 1) * 256, F16), "tks": SB((RO - 1) * 256, BF), "tkl": SB((RO - 1) * 256, BF),
     "bks": SB(RO * NC * 272, F32), "bkl": SB([RO * NC, 272], F32), "yas": SB(1024, F32), "mss": SB(1024, F32),
-    "ci": SB(16, I32), "cf": SB(32, F32), "rr": SB(160, F32), "ones": SB(128, BF), "dgs": SB(128, F32), "idh": SB(128, BF),
-    "inn": SB(128, BF), "idn": SB(128, BF), "a16": SB(48, F32), "mso": SB((RO - 1) * 256, F32), "selw": SB(64, BF), "zw": SB(320, BF), "cb": SB(8, F16), "sel0": SB(128, F32), "msk": SB(128, F32), "i32": SB(128, F32),
+    "ci": SB(16, I32), "cf": SB(32, F32), "rr": SB(160, F32), "ones": SB(128, BF), "idh": SB(128, BF),
+    "inn": SB(128, BF), "idn": SB(128, BF), "a16": SB(48, F32), "mso": SB((RO - 1) * 256, F32), "selw": SB(64, BF), "rev": SB(128, BF), "zw": SB(320, BF), "cb": SB(8, F16), "sel0": SB(128, BF), "msk": SB(192, F32), "i32": SB(128, F32),
     "m16": SB(272, F32), "rk": SB(144, F32), "c9": SB(16, F32), "zz": SB(1024, BF), "ofq": SB(8, U16), "ofr": SB(2, U16),
 }
 for _k, (_p, _n, _d) in TILES.items():
@@ -34,19 +35,19 @@ for _k, (_p, _n, _d) in TILES.items():
 for _b in range(POOLS["ps"]):
     SCRATCH["ps%d" % _b] = ("psum", [128, 512], F32)
 for _b in range(POOLS["pa"]):
-    SCRATCH["pa%d" % _b] = ("psum", [128, 8, 64], F32)
+    SCRATCH["pa%d" % _b] = ("psum", [128, 4, 128], F32)
 LOADS = ["cur", "tok", "fwA", "hkA", "hkB", "th", "bwA", "vvA", "fwB", "bwB", "vvB"]
 LOAD = 4200
 BYDMA = [k + "%d%d" % (t, c) for k in "oh" for t in range(RO) for c in range(NC) if k == "h"]
 EARLY = ("31",)
-APART = ["h21", "o21", "h30", "o30", "h31", "o31"]
+APART = ["o21", "o30", "o31", "h31"]
 SEMAPHORES = (["cV", "cA", "cP", "cG", "sent", "stored", "rtok", "rkey"] + ["l" + n for n in LOADS] + ["d" + n for n in BYDMA] + ["rM" + n for n in EARLY]
               + ["w%s%d%d" % (k, t, c) for k in "oh" for t in range(RO) for c in range(NC)]
               + ["r%s%d%d" % (k, t, c) for k in "LNB" for t in range(RO) for c in range(NC)] + ["rC%d%d" % (t, c) for t in range(RO - 1) for c in range(NC)])
 
-REF = {"c": 0.95, "p": 0.48, "g": 1.56, "s": 3.8, "hop": 180.0, "net": 4000.0, "o": 10.0, "r": 600.0, "d": 100.0, "l": 1.0}
-CHECK = [(dict(REF, c=0.83, p=0.42, hop=150.0, net=3000.0), 106.0), (dict(REF, c=0.95, p=0.48, g=1.45, s=2.5, hop=200.0, net=4200.0, r=800.0, d=130.0, l=1.2), 118.0),
-         (dict(REF, c=1.05, p=0.53, g=1.62, s=5.0, hop=120.0, net=2500.0, r=400.0, d=60.0, l=0.8), 132.0)]
+REF = {"c": 0.9, "p": 0.5, "g": 1.7, "s": 3.8, "hop": 220.0, "net": 4000.0, "o": 10.0, "r": 700.0, "d": 130.0, "l": 1.0}
+CHECK = [(dict(REF, c=0.83, p=0.46, g=1.55, hop=220.0, net=3200.0, d=120.0), 105.0), (dict(REF, c=0.95, p=0.5, g=1.75, s=2.5, hop=180.0, net=4200.0, o=15.0, r=850.0, d=160.0, l=1.15), 128.0),
+         (dict(REF, c=1.0, p=0.54, g=2.0, s=4.0, hop=170.0, net=2800.0, r=500.0, d=70.0, l=0.9), 142.0), (dict(REF, c=0.9, p=0.5, g=1.2, hop=200.0, net=3500.0), 160.0)]
 
 
 def dur(cost, M):
@@ -131,12 +132,13 @@ def build(stages=STAGES):
         r = ["cf%d" % j for j in [a] + (s2 if isinstance(s2, list) else [])]
         if o0 == MUL: A(1, lambda e, T, B: e.activation(cf(T, k), cf(T, a), AF.Identity, bias=sc(T), scale=s1), r, ["cf%d" % k])
         else: V(1, lambda e, T, B: e.tensor_scalar(cf(T, k), cf(T, a), s1, sc(T), o0, o1), r, ["cf%d" % k])
-    col(8, 1, -4096.0, 17 * 4096.0 + OFS, MUL, ADD)
+    col(8, 1, -1.0, 15.0, MUL, ADD)
+    col(14, 2, 16.0, [8], MUL, ADD)
     col(9, 1, 15.0, -0.5, EQ, ADD)
-    col(10, 4, 1000.0, [1], MUL, ADD)
+    col(10, 4, 1000.0, [8], MUL, ADD)
     col(11, 5, 16.0, [10], MUL, ADD)
     col(12, 4, -BIG, BIG, MUL, ADD)
-    col(13, 4, 1.0, 1 / BIG, MUL, ADD)
+    col(13, 4, math.log(BIG), -math.log(BIG), MUL, ADD)
     col(16, 4, 4.0, [5], MUL, ADD)
     col(17, 1, 8.0, [16], MUL, ADD)
     col(20, 1, 8.0, [2], MUL, ADD)
@@ -154,8 +156,8 @@ def build(stages=STAGES):
         else:
             V(b - a, lambda e, T, B: e.tensor_scalar(T[name][:, a:b], src(T), cf(T, k), cf(T, val[0]) if isinstance(val, list) else val, EQ, MUL),
               ["rr", "cf%d" % k] + (["cf%d" % val[0]] if isinstance(val, list) else []), [key or name])
-    mark("a16", 0, 48, 1, 1.0, -16.0); mark("selw", 0, 64, 11, [8])
-    mark("inn", 0, 128, 0, -PEN); mark("idn", 0, 128, 0, -1.0); mark("dgs", 0, 128, 0, [13])
+    mark("a16", 0, 48, 1, 1.0, -16.0); mark("selw", 0, 64, 11, HIT); mark("rev", 0, 128, 14, 1.0)
+    mark("inn", 0, 128, 0, -PEN); mark("idn", 0, 128, 0, -1.0)
     mark("zw", 0, 160, 21, 1.0, -16.0, "zw0"); mark("zw", 160, 320, 22, 1.0, -1016.0, "zw1")
     V(512, lambda e, T, B: e.memset(T.zz[:], 0.0), [], ["zz"])
     fill = lambda n, view, val, r, w: A(n, lambda e, T, B: e.activation(view(T), T.zz[:, :n], AF.Identity, bias=val), ["zz"] + r, w)
@@ -164,7 +166,7 @@ def build(stages=STAGES):
         fill(n // 16, lambda T, name=name: T[name][:, 0::16], first, [name], [name])
     fill(8, lambda T: T.c9[:, :8], 0.0, [], ["c9"]); fill(1, lambda T: T.c9[:, 8:9], -96.0, [], ["c9x"])
     op("A", [("v", 32)] * 5, lambda e, T, B, X: [e.activation(T.msk[:, a:b:st], T.zz[:, :(b - a + st - 1) // st], AF.Identity, bias=v) for a, b, st, v in (
-        (0, 64, 2, 0.0), (1, 64, 2, cf(T, 12)), (64, 128, 4, 0.0), (65, 128, 2, 1.0), (66, 128, 4, cf(T, 12)))], ["zz", "cf12"], ["msk"])
+        (0, 64, 2, 0.0), (1, 64, 2, cf(T, 12)), (64, 192, 4, 0.0), (65, 192, 2, 1.0), (66, 192, 4, cf(T, 12)))], ["zz", "cf12"], ["msk"])
     A(128, lambda e, T, B: e.activation(T.ones[:], T.zz[:, :128], AF.Exp), ["zz"], ["ones"])
     G(256, lambda e, T: e.affine_select(T.thl[0:8, :], T.m16[0:8, 1:257], [[1, 8], [0, 32]], EQ, 0.0, 0, -1), ["m16"], ["thl"])
     op("V", [("v", 128)] * 2, lambda e, T, B, X: [e.tensor_scalar(T.thq[0:8, 128 * h:128 * h + 128], T.thi[0:8, h::2], -1.0, None, MUL) for h in range(2)], ["thi"], ["thq"])
@@ -184,7 +186,10 @@ def build(stages=STAGES):
             if k: G(512, lambda e, T, k=k, a=a: e.iota(T.wx[:, 8 * k + a:8 * k + a + 2], [[0, 512]], 0, 0, **IO), ["wz%d" % k], ["wz%d" % k])
             elif a % 4 == 0: zero(lambda T, a=a: T.wx[:, a:a + 4], "wz0")
         init("wx", k)
-    for pool, name, n in (("rb", "rb", 64), ("tt", "tf", 64), ("xx", "zt", 256)):
+    for k in range(POOLS["tt"]):
+        op("A", [("v", 16), ("v", 8)], lambda e, T, B, X, k=k: [e.activation(T.tf[:, 64 * k + 16:64 * k + 32], T.zz[:, :16], AF.Copy),
+                                                                e.activation(T.kz[:, 256 * k + 143:256 * k + 256:16], T.zz[:, :8], AF.Copy)], ["zz"], []); init("tt", k)
+    for pool, name, n in (("rb", "rb", 64), ("xx", "zt", 256)):
         for k in range(POOLS[pool]):
             fill(n, lambda T, o=TILES[name][1] * k, name=name, n=n: T[name][:, o:o + n], 0.0, [], []); init(pool, k)
     V(16, lambda e, T, B: e.tensor_copy(T.lsl[:, :16], T.curi[:]), ["curi"], ["Lc00", "Lc01"])
@@ -209,8 +214,8 @@ def build(stages=STAGES):
         return [k + (0,), k + (1,)], v
 
     def scores(T, B, kg, qd, alone):
-        us = [y // 2 + 64 * (y % 2) if alone else y for y in range(128)]
-        return [(B[32 * (u // 32):32 * (u // 32) + 16, u % 32:256:32], kg(T, 16 * y, 16 * y + 16), qd(T, u), alone, alone) for y, u in enumerate(us)]
+        at = [64 * (u % 2) + u // 2 if alone else u for u in range(128)]
+        return [(B[32 * (y // 32):32 * (y // 32) + 16, y % 32:256:32], kg(T, 16 * u, 16 * u + 16), qd(T, u), alone, alone) for u, y in enumerate(at)]
 
     def spread(name, src, rk):
         if name in BYDMA:
@@ -234,9 +239,10 @@ def build(stages=STAGES):
         (kfm, fm), (kin, inv), (kit, ivt) = tiles("fm", "inv", "ivt")
         (kok, ofk), = tiles("ofk")
         VG(128, lambda e, T: e.tensor_tensor(fm(T), T.bws[:, :n].indirect(Lb(T)), T.nq[:, ob:ob + 128], ADD), ab("bw") + [kl, kb], [kfm])
-        op("V", [("v", 64)] * 2, lambda e, T, B, X: [e.tensor_scalar(ofk(T, h, 128, 2), fm(T, 64 * h, 64 * h + 64), -1.0, float(OFS), MUL, ADD) for h in range(2)], [kfm], [kok])
+        V(64, lambda e, T, B: e.tensor_scalar(ofk(T), fm(T), -1.0, float(OFS), MUL, ADD), [kfm], [kok])
         kk, kg = halves("kg", lambda T: T.hks[:, :n], ab("hk"), ofk, kok)
-        ps = P(256, lambda T, B: [(B[:, 384:512], T.idh[:], fm(T), True, False), (B[:, 384:512], T.idn[:], T.nq[:, oc:oc + 128], False, True)], [kfm, kc, "idh", "idn"])
+        ps = P(256, lambda T, B: [m for h in range(2) for m in ((B[:, 384 + 64 * h:448 + 64 * h], T.idh[:], fm(T, h, 128, 2), True, False),
+                                                                (B[:, 384 + 64 * h:448 + 64 * h], T.idn[:], T.nq[:, oc + h:oc + 128:2], False, True))], [kfm, kc, "idh", "idn"])
         op("A", [("v", 128)], lambda e, T, B, X: [e.activation(inv(T), B[:, 384:512], AF.Relu, bias=1.0)], [], [kin], ps,
            alt=[("V", [("v", 128)], lambda e, T, B, X: [e.tensor_scalar(inv(T), B[:, 384:512], 0.0, None, ALU.is_ge)])])
         P(1024, lambda T, B: scores(T, B, kg, qd, True)[:64], [kk[0], kq], ps)
@@ -256,7 +262,8 @@ def build(stages=STAGES):
             P(384, lambda T, B: [m for b in range(2) for m in [(B[:, b:8:2], T.idh[:], T.cb[:, b:8:2], True, False)] + [
                 (B[:, b:8:2], T.zw[:, 160 * b + 16 - 16 * (h - b):160 * b + 144 - 16 * (h - b)], fq(T, h, 8, 2), False, h == 1) for h in range(2)]], [kfq, "idh", "cb", "zw0", "zw1"], ps)
             V(8, lambda e, T, B: e.tensor_scalar(ofc(T), B[:, :8], -32.0, None, MUL), [], [kof], ps)
-            VG(128, lambda e, T: e.tensor_tensor(T.crs[:, 128 * x:128 * x + 128], kg(T).indirect(ofc(T)), T.tkl[:, 128 * x:128 * x + 128], ALU.max), kk + [kof, "tkl"], ["cs" + tc])
+            op("V", [("g", 64)] * 2, lambda e, T, B, X: [e.tensor_tensor(T.crs[:, 128 * x + h:128 * x + 128:2], kg(T).indirect(ofc(T, 4 * h, 4 * h + 4)), T.tkl[:, 128 * x + h:128 * x + 128:2], ALU.max)
+                                                         for h in range(2)], kk + [kof, "tkl"], ["cs" + tc])
             send("rC" + tc, lambda T: T.crs[:, 128 * x:128 * x + 128], lambda T: T.nq[:, 640 * (x + NC) + 128:640 * (x + NC) + 256], ["cs" + tc], ["qq%d%d" % (t + 1, c)], 1, 250)
             kmx, mx = kmi, mi
         else:
@@ -276,25 +283,28 @@ def build(stages=STAGES):
         op("S", [("d", 8)], lambda e, T, B, X: [e.dma_start(wx(T, h, h + 1, rows=slice(16 * h, 16 * h + 16)), wc(T, rows=slice(16 * h, 16 * h + 16))) for h in range(8)],
            [kwc], [kwx], sem="w" + "ho"[own] + tc, lat=2000)
         kv, vg = halves("vg", lambda T: T.vvs[:, :n], ab("vv"), ofk, kok)
-        apart = "ho"[own] + tc in APART; nr = 8 if apart else 4; oa = 272 * x + 16
-        theirs = (lambda T: T.bkl[:, x, 16:144]) if "h" + tc in APART else lambda T: T.bkl[:, x, 17:272:2]
-        ps = P(64 * nr, lambda T, B: [(B[:, 0:nr], T.zz[0:1, :128], T.zz[0:1, :64 * nr], True, False)], ["zz"], None, "pa") if own else None
+        apart = "ho"[own] + tc in APART; wd = 128 if apart else 64; st = wd // 32; oa = 272 * x + 16
+        ps = P(4 * wd, lambda T, B: [(B[:, :, :wd], T.zz[0:1, :128], T.zz[0:1, :4 * wd], True, False)], ["zz"], None, "pa") if own else None
         for h in range(2):
             V(512, lambda e, T, B, h=h: e.transpose(vt(T, 1024 * h, 1024 * h + 1024), vg(T, 1024 * h, 1024 * h + 1024)), [kv[h]], [kvt + (h,)])
             if apart:
-                ps = P(1024, lambda T, B, h=h: [(B[32 * (b // 16):32 * (b // 16) + 32, b // 8 % 2::2, 8 * (b % 8):8 * (b % 8) + 8], vt(T, 32 * b, 32 * b + 32),
+                ps = P(1024, lambda T, B, h=h: [(B[32 * (b // 16):32 * (b // 16) + 32, :, 8 * (b % 16):8 * (b % 16) + 8], vt(T, 32 * b, 32 * b + 32),
                                                  wx(T, more=(slice(4 * h, 4 * h + 4), b % 32)), not own, not own) for b in range(32 * h, 32 * h + 32)], [kvt + (h,), kwx], ps, "pa")
             else:
-                ps = P(2048, lambda T, B, h=h: [(B[32 * (b // 16):32 * (b // 16) + 32, 0:4, 4 * (b % 16):4 * (b % 16) + 4], vt(T, 32 * b, 32 * b + 32),
+                ps = P(2048, lambda T, B, h=h: [(B[32 * (b // 16):32 * (b // 16) + 32, :, 4 * (b % 16):4 * (b % 16) + 4], vt(T, 32 * b, 32 * b + 32),
                                                  wx(T, more=(slice(4 * h + y, 4 * h + 4, 2), b % 32)), y == 0 and not own, y == 1 and not own) for b in range(32 * h, 32 * h + 32) for y in range(2)],
                        [kvt + (h,), kwx], ps, "pa")
-        if own: P(512, lambda T, B: [(B[:, 0:nr, nr // 2 - 1::nr // 2], T.i32[:], theirs(T), False, True)], ["bl" + tc, "i32"], ps)
-        if own or apart: (ksl, sel), = tiles("sel")
-        else: ksl, sel = "ba" + tc, lambda T, a, b: T.bks[:, oa + a:oa + b]
-        op("V", [("v", 64)] * nr, lambda e, T, B, X: [e.tensor_tensor_scan(sel(T, 64 * a, 64 * a + 64), T.msk[:, 16 * nr - 64:16 * nr], B[:, a], 0.0, MUL, ADD) for a in range(nr)],
+        if not own and not apart:
+            op("A", [("v", 256)], lambda e, T, B, X: [e.activation(T.bks[:, oa:oa + 256], B[:, :, :64], AF.Copy)], [], ["ba" + tc], ps,
+               alt=[("V", [("v", 256)], lambda e, T, B, X: [e.tensor_copy(T.bks[:, oa:oa + 256], B[:, :, :64])])])
+            return kmx, mx, ksm, msc, None, None
+        if own and "h" + tc in APART: P(512, lambda T, B: [(B[:, :, st - 1:wd:st], T.i32[:], T.bkl[:, x, 16:144], False, True)], ["bl" + tc, "i32"], ps)
+        elif own: P(1024, lambda T, B: [(B[:, :, st // 2 - 1:wd:st // 2], T.i32[:], T.bkl[:, x, 16:272], False, True)], ["bl" + tc, "i32"], ps)
+        (ksl, sel), = tiles("sel")
+        op("V", [("v", wd)] * 4, lambda e, T, B, X: [e.tensor_tensor_scan(sel(T, wd * a, wd * a + wd), T.msk[:, wd - 64:2 * wd - 64], B[:, a, :wd], 0.0, MUL, ADD) for a in range(4)],
            ["msk"], [ksl], ps)
-        if apart and not own: G(128, lambda e, T: e.affine_select(T.bks[:, oa:oa + 128], sel(T, 3, 512, 4), [[0, 128]], EQ, 0.0, 0, 0), [ksl], ["ba" + tc])
-        return kmx, mx, ksm, msc, ksl, lambda T, a: sel(T, 16 * nr * a + nr // 2 - 1, 16 * nr * a + 16 * nr, nr // 2)
+        if not own: G(128, lambda e, T: e.affine_select(T.bks[:, oa:oa + 128], sel(T, 3, 512, 4), [[0, 128]], EQ, 0.0, 0, 0), [ksl], ["ba" + tc])
+        return kmx, mx, ksm, msc, ksl, lambda T: sel(T, st - 1, 4 * wd, st)
 
     keep, run = {}, {}
     for t in range(RO):
@@ -306,6 +316,8 @@ def build(stages=STAGES):
                    ["fwA"] + (["fwB"] if t else []) + ["Lc" + tc, "nc" + tc], [kf])
                 V(64, lambda e, T, B: e.tensor_scalar(ofk(T), fr(T), float(OFS), None, ADD), [kf], [kok])
                 kk, kg = halves("kg", lambda T: T.hks[:, :n], ["hkA"] + (["hkB"] if t else []), ofk, kok)
+                if x == 1:
+                    ops[-1]["r"] = ops[-1]["r"] + ["hits0"]; ops[-2]["alts"].pop(); ops[-1]["alts"].pop()
                 yield
                 who[0] = "s"; q = lambda T: T.nq[:, on + 128:on + 256]
                 if t == 0: gather(128, q, lambda T: T.hks[:, :], lambda T: T.toku[:, 8 * c:8 * c + 8], ["hkA", "hkB", "toku"], ["qq" + tc], "q")
@@ -316,19 +328,19 @@ def build(stages=STAGES):
                 P(1024 + 64, lambda T, B: scores(T, B, kg, qd, False)[64:] + close(T, B, 0), [kk[1], kq, "zz"], ps)
                 (ksg, sg), = tiles("sg")
                 A(256, lambda e, T, B: e.activation(sg(T), B[:, :256], AF.Sign, bias=cf(T, 9)), ["cf9"], [ksg], ps)
-                P(128, lambda T, B: [(B[:, 256:384], fr(T), T.idh[:], True, False)], [kf, "idh"], ps)
+                P(128, lambda T, B: [(B[:, 256:384], fr(T), T.rev[:], True, False)], [kf, "rev"], ps)
                 P(1024 + 64, lambda T, B: [(B[32 * a:32 * a + 32, 256 + 32 * (h % 4) + 16 * (h // 4):272 + 32 * (h % 4) + 16 * (h // 4)], sg(T, 32 * h, 32 * h + 32), T.selw[:, 16 * a:16 * a + 16],
                                             False, False) for a in range(4) for h in range(8)] + close(T, B, 256), [ksg, "selw", "zz"], ps)
-                (kx, ks), = tiles("ks"); (kt, tf), = tiles("tf"); (kr, rb), = tiles("rb")
-                V(128, lambda e, T, B: e.tensor_tensor_scan(ks(T), T.m16[:, :128], B[:, 256:384], 0.0, MUL, ALU.max), ["m16"], [kx], ps)
-                V(8, lambda e, T, B: e.tensor_scalar(tf(T, 48, 56), ks(T, 15, 128, 16), 2.0 ** 35 - 2048, -2.0 ** 35, ADD, ADD), [kx], [kt + (0,)])
-                V(16, lambda e, T, B: e.tensor_tensor(tf(T, 0, 8), ks(T, 15, 128, 16), tf(T, 48, 56), ALU.subtract), [kx, kt + (0,)], [kt + (1,)])
-                V(9, lambda e, T, B: e.tensor_tensor_scan(tf(T, 32, 41), T.c9[:, :9], tf(T, 0, 9), 0.0, ADD, ALU.max), ["c9", "c9x", kt + (1,)], [kt + (2,)])
-                V(8, lambda e, T, B: e.tensor_scalar(tf(T, 16, 24), tf(T, 0, 8), tf(T, 40, 41), tf(T, 39, 40), ALU.is_lt, MUL), [kt + (1,), kt + (2,)], [kt + (3,)])
-                VG(16, lambda e, T: e.tensor_tensor(rb(T).indirect(T.ofr[:, 0:1]), tf(T, 0, 16), tf(T, 16, 32), ALU.max), [kt + (1,), kt + (3,), "ofr"], [kr], "s")
+                (kx, ks), (kd, dz), (kt, tf) = tiles("kz", "dz", "tf"); (kr, rb), = tiles("rb")
+                op("A", [("v", 128)], lambda e, T, B, X: [e.activation(dz(T), B[:, 256:384], AF.Relu, scale=-4.0)], [], [kd, "hits%d" % x], ps,
+                   alt=[("V", [("v", 128)], lambda e, T, B, X: [e.tensor_scalar(dz(T), B[:, 256:384], 0.0, 1e4, ALU.is_lt, MUL)])])
+                V(128, lambda e, T, B: e.tensor_tensor_scan(ks(T, 0, 128), dz(T), B[:, 256:384], 0.0, ALU.min, ALU.max), [kd], [kx], ps)
+                V(9, lambda e, T, B: e.tensor_tensor_scan(tf(T, 32, 41), T.c9[:, :9], ks(T, 15, 144, 16), 0.0, ADD, ALU.max), ["c9", "c9x", kx], [kt + (2,)])
+                V(8, lambda e, T, B: e.tensor_scalar(tf(T, 16, 24), ks(T, 15, 128, 16), tf(T, 40, 41), tf(T, 39, 40), ALU.is_lt, MUL), [kx, kt + (2,)], [kt + (3,)])
+                VG(16, lambda e, T: e.tensor_tensor(rb(T).indirect(T.ofr[:, 0:1]), ks(T, 15, 256, 16), tf(T, 16, 32), ALU.max), [kx, kt + (3,), "ofr"], [kr], "s")
                 P(1024, lambda T, B: [(B[32 * (h // 2):32 * (h // 2) + 32, :8], T.a16[:, 16 - 16 * (h % 2):48 - 16 * (h % 2)], rb(T, 8 * h, 8 * h + 8), h % 2 == 0, h % 2 == 1)
                                       for h in range(8)], [kr, "a16"], ps)
-                V(8, lambda e, T, B: e.tensor_copy(T.lso[:, 8 * x:8 * x + 8], B[:, :8]), [], ["Lb" + tc], ps)
+                V(8, lambda e, T, B: e.tensor_scalar(T.lso[:, 8 * x:8 * x + 8], B[:, :8], OFS - HIT, None, ADD), [], ["Lb" + tc], ps)
                 send("rL" + tc, lambda T: T.lso[:, 8 * x:8 * x + 8], lambda T: T.lsl[:, 8 * (x + NC):8 * (x + NC) + 8], ["Lb" + tc], ["Lc%d%d" % (t + 1, c)], 1, 0)
                 gather(128, lambda T: T.nq[:, on:on + 128], lambda T: T.nnum[:, :n], lambda T: T.lso[:, 8 * x:8 * x + 8], ["num0", "num1", "num2", "num3", "num4", "Lb" + tc], ["nb" + tc], "nb")
                 send("rN" + tc, lambda T: T.nq[:, on:on + 384], lambda T: T.nq[:, on + 640 * NC + 256:on + 640 * NC + 640], ["nb" + tc, "qq" + tc, "nc" + tc],
@@ -355,20 +367,24 @@ def build(stages=STAGES):
                     yield
                 n = len(cs); x = NC * t + cs[0]; oy = 128 * x; who[0] = "b"; names = lambda s: [s + "%d%d" % (t, y) for y in cs]
                 mx = keep[x][1] if n == 1 else lambda T: T.mi[:, 8 * x:8 * x + 16]
-                (kz, zt), (kx, xx), (kf, fa) = tiles("zt", "xx", "fa")
+                (kz, zt), (kx, xx), (kf, mh) = tiles("zt", "xx", "mh")
                 V(32, lambda e, T, B: e.tensor_tensor(zt(T, 0, 128 * n, 16), mx(T), T.bkl[:, x:x + n, 0:8], ALU.max), [keep[x + y][0] for y in range(n)] + names("bn"), [kz + (0,)])
                 V(32, lambda e, T, B: e.tensor_tensor(xx(T, 0, 8 * n), keep[x][3](T, 143, 128 + 128 * n, 16), T.bkl[:, x:x + n, 8:16], ADD), [keep[x + y][2] for y in range(n)] + names("bn"), [kx + (0,)])
                 A(16, lambda e, T, B: e.activation(xx(T, 16, 16 + 8 * n), zt(T, 0, 128 * n, 16), AF.Exp, scale=-0.0078125), [kz + (0,)], [kx + (1,)])
                 V(32, lambda e, T, B: e.tensor_tensor(zt(T, 1, 128 * n, 16), xx(T, 0, 8 * n), xx(T, 16, 16 + 8 * n), MUL), [kx + (0,), kx + (1,)], [kz + (1,)])
-                V(128 * n, lambda e, T, B: e.transpose(T.mss[:, oy:oy + 128 * n], zt(T, 0, 128 * n)), [kz + (0,), kz + (1,)], names("mo"))
-                ps = P(512 * n, lambda T, B: [(B[:, :128 * n], T.sel0[:], T.mss[:, oy:oy + 128 * n], True, True)], names("mo") + ["sel0"])
-                A(128 * n, lambda e, T, B: e.activation(fa(T, 0, 128 * n), B[:, :128 * n], AF.Exp, scale=-0.0078125), [], [kf], ps)
+                op("V", [("v", 64)] * 2 * n, lambda e, T, B, X: [e.transpose(T.mss[:, oy + 128 * (h // 2) + h % 2:oy + 128 * (h // 2) + 128:2], zt(T, 64 * h, 64 * h + 64)) for h in range(2 * n)],
+                   [kz + (0,), kz + (1,)], names("mo"))
+                if t + 1 < RO: G(128 * n, lambda e, T: e.affine_select(mh(T, 0, 128 * n), T.mss[:, oy:oy + 128 * n], [[0, 128 * n]], EQ, 0.0, 0, 0), names("mo"), [kf])
+                else: A(128, lambda e, T, B: e.activation(mh(T, 0, 128), T.mss[:, oy:oy + 128], AF.Copy), names("mo"), [kf])
+                ps = P(512 * n, lambda T, B: [(B[32 * (z % 4):32 * (z % 4) + 32, 128 * (z // 4) + 32 * a:128 * (z // 4) + 32 * a + 32], T.sel0[:, 32 * a:32 * a + 32], mh(T, 32 * z, 32 * z + 32), True, True)
+                                              for z in range(4 * n) for a in range(4)], [kf, "sel0"])
+                A(128 * n, lambda e, T, B: e.activation(B[:, 256:256 + 128 * n], B[:, :128 * n], AF.Exp, bias=cf(T, 13), scale=-0.0078125), ["cf13"], [], ps)
                 for y in range(n):
-                    P(2048, lambda T, B, sel=keep[x + y][5]: [(B[32 * a:32 * a + 32, 32 * z:32 * z + 32], T.dgs[:, 32 * z:32 * z + 32], sel(T, a), True, True)
-                                                              for a in range(4) for z in range(4)], [keep[x + y][4], "dgs"], ps)
-                    op("V", [("v", 64)] * 2, lambda e, T, B, X, o=128 * y: [e.tensor_tensor(T.yas[:, oy + o + 64 * h:oy + o + 64 * h + 64], B[:, h:128:2], fa(T, o + 64 * h, o + 64 * h + 64), MUL)
-                                                                            for h in range(2)], [kf], [names("yo")[y]], ps)
-                op("S", [("d", 1)], lambda e, T, B, X: [e.dma_start(T.ya[:, oy:oy + 128 * n], T.yas[:, oy:oy + 128 * n])], names("yo"), [], sem="stored", lat=2500)
+                    o = oy + 128 * y
+                    V(128, lambda e, T, B, o=o, y=y: e.tensor_tensor(T.yas[:, o:o + 128], keep[x + y][5](T), B[:, 256 + 128 * y:384 + 128 * y], MUL), [keep[x + y][4]], [names("yo")[y]], ps)
+                    for q, zs in [("S", (z,)) for z in range(4)] if t + 1 < RO else (("S", (0, 1)), ("A", (2, 3))):
+                        op(q, [("d", 4 * len(zs))], lambda e, T, B, X, o=o, zs=zs: [e.dma_start(T.ya[32 * a:32 * a + 32, o + 32 * z:o + 32 * z + 32], T.yas[32 * z:32 * z + 32, o + 32 * a:o + 32 * a + 32])
+                                                                                    for z in zs for a in range(4)], [names("yo")[y]], [], sem="stored", lat=2300)
                 if t >= RO - 2 and c == NC - 1:
                     a, b = (0, 768) if t == RO - 2 else (768, 1024)
                     op("S", [("n", 120)], lambda e, T, B, X: [e.dma_start(T.ym[:, a:b], T.mss[0::16, a:b]), e.dma_start(T.ys[:, a:b], T.mss[1::16, a:b])],
@@ -388,8 +404,9 @@ def build(stages=STAGES):
         for k in o["w"]:
             if k in lastw: d.add(lastw[k])
             d.update(readers.get(k, []))
+        o["line"] = set()
         if o["ps"] is not None:
-            d.update(acc.get(o["ps"], [])); acc.setdefault(o["ps"], []).append(i)
+            o["line"].update(acc.get(o["ps"], [])); acc.setdefault(o["ps"], []).append(i)
         for k in o["r"]: readers.setdefault(k, []).append(i)
         for k in o["w"]: lastw[k] = i; readers[k] = []
         d.discard(i); o["dep"] = d
@@ -399,9 +416,11 @@ def build(stages=STAGES):
     for i, o in enumerate(ops):
         for k in o["tiles"]: users.setdefault(k, []).append(i)
     for k in sorted(users):
-        for i in users[k]: ops[i]["dep"].update(last.get((k[0], where[k]), []))
+        for i in users[k]: ops[i]["line" if k[0] in ("ps", "pa") else "dep"].update(last.get((k[0], where[k]), []))
         last[k[0], where[k]] = users[k]
-    for i, o in enumerate(ops): o["dep"] = sorted(o["dep"]); assert max(o["dep"], default=-1) < i, (i, o["w"], o["ps"])
+    for i, o in enumerate(ops):
+        same = lambda j: len(o["alts"]) == len(ops[j]["alts"]) == 1 and o["alts"][0][0] == ops[j]["alts"][0][0] != "A"
+        o["wait"] = sorted(o["dep"] | set(j for j in o["line"] if not same(j))); o["dep"] = sorted(o["dep"] | o["line"])
     return ops
 
 
@@ -543,7 +562,7 @@ def replay(ops, order, extra, M):
     free = {e: 0.0 for e in "VAPGS"}; done = {}; busy = {e: 0.0 for e in "VAPGS"}
     for i, x in order:
         o = ops[i]; e, cost, _ = o["alts"][x]
-        st = max([free[e]] + [done[d] for d in o["dep"] + extra.get(i, [])])
+        st = max([free[e]] + [done[d] for d in o["wait"]])
         d = dur(cost, M); free[e] = st + d; busy[e] += d; done[i] = free[e] + after(o, M)
     return max(done.values()), busy
 
@@ -557,7 +576,8 @@ def lay(ops, pick, seq, M, forward):
     busy = {e: [] for e in "VAPGS"}; st = {}
     for i in seq:
         o = ops[i]; e, cost, _ = o["alts"][pick[i]]; du = dur(cost, M)
-        t = max([st[j][1] + after(ops[j], M) for j in o["dep"]], default=0.0) if forward else max([st[j][1] for j in o["succ"]], default=0.0) + after(o, M)
+        if forward: t = max([st[j][1] + (after(ops[j], M) if j in o["wait"] else 0.0) for j in o["dep"]], default=0.0)
+        else: t = max([st[j][1] + (after(o, M) if i in ops[j]["wait"] else 0.0) for j in o["succ"]], default=after(o, M))
         q = busy[e]; k = 0
         while k < len(q) and t + du > q[k][0] + 1e-6: t = max(t, q[k][1]); k += 1
         q.insert(k, (t, t + du)); st[i] = (t, t + du)
@@ -586,14 +606,15 @@ def arrange(ops, M, per, ahead, onv, rounds=3):
     return best[1]
 
 
-def plan2(ops, M, per, ahead, look, sticky, bias, vmin, slack):
+def plan2(ops, M, per, ahead, look, sticky, bias, vmin, slack, seed=0, noise=0.0):
     n = len(ops); succ = [[] for _ in ops]
     for i, o in enumerate(ops):
         for d in o["dep"]: succ[d].append(i)
     du = [[dur(a[1], M) for a in o["alts"][:2]] for o in ops]; pr = [0.0] * n
     for i in range(n - 1, -1, -1):
         o = ops[i]; pr[i] = du[i][0] + after(o, M) + max([pr[j] for j in succ[i]], default=-o.get("turn", 0) * per)
-    pr = [p + (1000.0 * ahead[o["stage"]] if "stage" in o else 0.0) for p, o in zip(pr, ops)]
+    shift = lambda o: 1000.0 * ahead[o["stage"]] + noise * math.sin(seed * (1 + o["stage"] + 7 * (o["turn"] + 2)) + seed * seed)
+    pr = [p + (shift(o) if "stage" in o else 0.0) for p, o in zip(pr, ops)]
     for i in range(len(LOADS)): pr[i] = 1e9 - i
     for i in range(n - 1, -1, -1): pr[i] = max([pr[i]] + [du[i][0] + after(ops[i], M) + pr[j] for j in succ[i]])
     free = {e: 0.0 for e in "VAPGS"}; left = [len(o["dep"]) for o in ops]; avail = [0.0] * n; order = []
@@ -610,7 +631,7 @@ def plan2(ops, M, per, ahead, look, sticky, bias, vmin, slack):
         st, i, x = now; e = ops[i]["alts"][x][0]; st = max(avail[i], free[e])
         free[e] = st + du[i][x]; order.append((i, x)); ready.remove(i); rest[ops[i]["alts"][0][0]] -= du[i][0]
         for j in succ[i]:
-            avail[j] = max(avail[j], free[e] + after(ops[i], M)); left[j] -= 1
+            avail[j] = max(avail[j], free[e] + (after(ops[i], M) if i in ops[j]["wait"] else 0.0)); left[j] -= 1
             if not left[j]: ready.append(j)
     return order
 
@@ -639,7 +660,7 @@ def improve(ops, order, iters, seed=1, temp=0.0004, lam=0.15):
     def rnd(k=None):
         state[0] = (state[0] * 1103515245 + 12345) % 2147483648
         return state[0] / 2147483648 if k is None else (state[0] >> 8) % k
-    dep = [o["dep"] for o in ops]; deps = [set(d) for d in dep]
+    dep = [o["wait"] for o in ops]; deps = [set(o["dep"]) for o in ops]
     eng = [["VAPGS".index(a[0]) for a in o["alts"]] for o in ops]
     tab = [[[dur(a[1], M) for a in o["alts"]] for o in ops] for M, w in CHECK]
     af = [[after(o, M) for o in ops] for M, w in CHECK]
@@ -678,13 +699,19 @@ def improve(ops, order, iters, seed=1, temp=0.0004, lam=0.15):
             else: p2[i] = p2[i + 1] = 2; s2 = seq[:a] + [i, i + 1] + [j for j in seq[a:] if j != i and j != i + 1]
         else:
             if r < 0.8:
-                c = []; i = max(range(n), key=lambda j: done[j])
+                c = []; turns = []; i = done.index(max(done))
                 while i is not None:
                     p, q = par[i]
-                    if q and p is not None and p >= head: c.append((i, p))
+                    if not q: turns.append((len(c), i))
+                    elif p is not None and p >= head: c.append((i, p))
                     i = p
                 if not c: continue
-                i, p = c[rnd(len(c))]
+                k, y = turns[rnd(len(turns))] if turns and r < 0.65 else (rnd(len(c)), None)
+                i, p = c[max(0, min(len(c) - 1, k + rnd(6) - 3 if y is not None else k))]
+                if y is not None and y >= head and r < 0.35:
+                    later = [j for j in seq[seq.index(y) + 1:][:60] if eng[j][pick[j]] == eng[y][pick[y]]]
+                    if not later: continue
+                    i, p = later[rnd(len(later))], y
             else:
                 i = rnd(n); p, q = par[i]
                 if not q or p is None or p < head: continue
@@ -709,14 +736,16 @@ def improve(ops, order, iters, seed=1, temp=0.0004, lam=0.15):
     return [(i, best[2][i]) for i in best[1]]
 
 
-ARR = (4500.0, (-2, -1, -12, 4, -3, -17, -7), 0.3, 250.0, 50.0, 4000.0, -500.0)
-ITERS = 36000
+ARR = (4000.0, (0, 2, -7, 23, 4, -46, -5), 0.3, 0.0, 50.0, 4000.0, -1500.0, 481, 3000.0)
+ITERS = (32000, 14000)
 
 
 def schedule():
     if "s" not in CACHE:
-        ops = build()
-        CACHE["s"] = (ops, improve(ops, polish(ops, plan2(ops, REF, *ARR), REF), ITERS))
+        ops = build(); cheap = CHECK.pop()
+        order = improve(ops, polish(ops, plan2(ops, REF, *ARR), REF), ITERS[0])
+        CHECK.append(cheap)
+        CACHE["s"] = (ops, improve(ops, order, ITERS[1], 2, 0.0002))
     return CACHE["s"]
 
 
@@ -755,7 +784,7 @@ def rank_program(g, core, T, topo):
     for i, x in order:
         o = ops[i]; e, _, fn = o["alts"][x]
         need = {}
-        for d in o["dep"]:
+        for d in o["wait"]:
             s, v = mark[d]; need[s] = max(need.get(s, 0), v)
         for s, v in need.items():
             if waited[e].get(s, 0) < v:

import math
import numpy as np
from concourse.bass import DstId, RemoteDMATransfer
from concourse.mybir import AluOpType as ALU, ActivationFunctionType as AF

W, RO, NC = 3072, 4, 2
RINGS = {"kg": {"s": 3, "o": 2, "h": 2}, "vg": {"O": 2, "H": 2}, "vt": {"O": 2, "H": 2}, "wx": {"OH": 3}, "hl": {"o": 8, "h": 4}, "wc": {"O": 2, "H": 2},
         "sel": {"O": 3, "H": 2}, "qd": {"s": 2}, "qh": {"h": 2}, "sg": {"s": 2}, "s1": {"o": 2, "h": 2}, "rb": {"s": 2}, "fr": {"s": 3}, "rd": {"o": 2, "h": 2},
         "ofk": {"s": 2, "o": 8, "h": 4}, "ks": {"o": 2}, "msc": {"o": 2, "h": 4}, "tt": {"s": 2}, "cy": {"o": 6}, "xx": {"b": 2},
         "ps": {"so": 3, "h": 1, "b": 1}, "pa": {"OH": 3}}
POOLS = {p: sum(r.values()) for p, r in RINGS.items()}
PEN, BIG = 4096.0, 2.0 ** 40
HIT = 5120.0
OFS = 1024
F32, BF, F16, I32, U16 = "float32", "bfloat16", "float16", "int32", "uint16"
SB = lambda n, d: ("sbuf", [128] + (n if isinstance(n, list) else [n]), d)
TILES = {"kg": ("kg", 2048, BF), "vg": ("vg", 2048, BF), "vt": ("vt", 2048, BF), "wx": ("wx", [8, 8, 32], BF), "hl": ("hl", [4, 4, 16], BF),
         "wc": ("wc", 256, BF), "sel": ("sel", 512, F32), "qd": ("qd", 1024, BF), "qh": ("qh", 1024, F16), "sg": ("sg", 256, BF), "s1": ("s1", 256, F16),
         "rb": ("rb", 128, F32), "fr": ("fr", 128, F16), "fm": ("rd", 128, F16), "inv": ("rd", 128, BF), "ivt": ("rd", 128, BF),
         "ofk": ("ofk", 128, U16), "ks": ("ks", 128, F32), "msc": ("msc", 256, F32),
         "tf": ("tt", 64, F32), "kz": ("tt", 256, F32), "dz": ("tt", 128, F32), "mi": ("cy", 8, I32), "fq": ("cy", 8, BF), "ofc": ("cy", 8, U16),
         "zt": ("xx", 256, F32), "xx": ("xx", 32, F32), "mh": ("xx", 256, F16)}
SCRATCH = {
    "hks": SB(W, BF), "vvs": SB(W, BF), "fws": SB(2816, BF), "bws": SB(W, BF), "nnum": SB(W, F32),
    "curi": SB(16, I32), "toki": SB(64, I32), "toku": SB(64, U16), "tokl": SB(64, U16), "thi": SB([8, 32], I32), "thq": SB(256, F16), "thl": SB(256, BF),
    "lsl": SB((RO + 1) * NC * 8, U16), "lso": SB(RO * NC * 8, U16), "nq": SB((RO + 1) * NC * 640, F16),
    "crs": SB((RO - 1) * 256, F16), "tks": SB((RO - 1) * 256, BF), "tkl": SB((RO - 1) * 256, BF),
    "bks": SB(RO * NC * 272, F32), "bkl": SB([RO * NC, 272], F32), "yas": SB(1024, F32), "mss": SB(1024, F32),
    "ci": SB(16, I32), "cf": SB(32, F32), "rr": SB(160, F32), "ones": SB(128, BF), "idh": SB(128, BF),
    "inn": SB(128, BF), "idn": SB(128, BF), "a16": SB(48, F32), "mso": SB((RO - 1) * 256, F32), "selw": SB(64, BF), "rev": SB(128, BF), "zw": SB(320, BF), "cb": SB(8, F16), "sel0": SB(128, BF), "msk": SB(192, F32), "i32": SB(128, F32),
    "m16": SB(272, F32), "rk": SB(144, F32), "c9": SB(16, F32), "zz": SB(1024, BF), "ofq": SB(8, U16), "ofr": SB(2, U16),
}
for _k, (_p, _n, _d) in TILES.items():
    SCRATCH[_k] = SB([POOLS[_p] * _n[0]] + _n[1:] if isinstance(_n, list) else POOLS[_p] * _n, _d)
for _b in range(POOLS["ps"]):
    SCRATCH["ps%d" % _b] = ("psum", [128, 512], F32)
for _b in range(POOLS["pa"]):
    SCRATCH["pa%d" % _b] = ("psum", [128, 4, 128], F32)
LOADS = ["cur", "tok", "fwA", "hkA", "hkB", "th", "bwA", "vvA", "fwB", "bwB", "vvB"]
LOAD = 4200
BYDMA = [k + "%d%d" % (t, c) for k in "oh" for t in range(RO) for c in range(NC) if k == "h"]
EARLY = ("31",)
APART = ["o21", "o30", "o31", "h31"]
SEMAPHORES = (["cV", "cA", "cP", "cG", "sent", "stored", "rtok", "rkey"] + ["l" + n for n in LOADS] + ["d" + n for n in BYDMA] + ["rM" + n for n in EARLY]
              + ["w%s%d%d" % (k, t, c) for k in "oh" for t in range(RO) for c in range(NC)]
              + ["r%s%d%d" % (k, t, c) for k in "LNB" for t in range(RO) for c in range(NC)] + ["rC%d%d" % (t, c) for t in range(RO - 1) for c in range(NC)])

REF = {"c": 0.9, "p": 0.5, "g": 1.7, "s": 3.8, "hop": 220.0, "net": 4000.0, "o": 10.0, "r": 700.0, "d": 130.0, "l": 1.0}
CHECK = [(dict(REF, c=0.83, p=0.46, g=1.55, hop=220.0, net=3200.0, d=120.0), 105.0), (dict(REF, c=0.95, p=0.5, g=1.75, s=2.5, hop=180.0, net=4200.0, o=15.0, r=850.0, d=160.0, l=1.15), 128.0),
         (dict(REF, c=1.0, p=0.54, g=2.0, s=4.0, hop=170.0, net=2800.0, r=500.0, d=70.0, l=0.9), 142.0), (dict(REF, c=0.9, p=0.5, g=1.2, hop=200.0, net=3500.0), 160.0)]


def dur(cost, M):
    tot = 0.0
    for kind, n in cost:
        if kind == "v": tot += max(64, n) * M["c"] + M["o"]
        elif kind == "g": tot += 60 + n * M["g"] * M["c"] + M["o"]
        elif kind == "s": tot += 60 + n * M["s"] * M["c"] + M["o"]
        elif kind == "n": tot += n
        else: tot += n * M[kind]
    return tot


STAGES = [("o", 0), ("o", 0), ("o", -1), ("h", 1), ("h", 2), ("o", 2), ("b", 3)]


def build(stages=STAGES):
    ops, ring, who, where = [], {}, ["s"], {}

    def op(eng, cost, fn, r, w, ps=None, sem=None, lat=0.0, alt=None):
        ops.append({"alts": [(eng, cost, fn)] + (alt or []), "r": r, "w": w, "ps": ps, "sem": sem, "lat": lat})

    def bank(p):
        c = [y for y in RINGS[p] if who[0] in y][0]; j = ring.get((p, c), 0); ring[p, c] = j + 1; k = ring.get(p, 0); ring[p] = k + 1
        where[p, k] = sum(n for y, n in RINGS[p].items() if y < c) + j % RINGS[p][c]
        return p, k

    def tiles(*names):
        p, k = bank(TILES[names[0]][0]); x = where[p, k]
        def view(s):
            n = TILES[s][1]; n = n[0] if isinstance(n, list) else n
            return lambda T, a=0, b=None, st=1, rows=slice(None), more=(): T[s][(rows, slice(n * x + a, n * x + (n if b is None else b), st)) + more]
        return [((p, k, s), view(s)) for s in names]

    V = lambda n, fn, r, w, ps=None: op("V", [("v", n)], lambda e, T, B, X: [fn(e, T, B)], r, w, ps)
    A = lambda n, fn, r, w, ps=None: op("A", [("v", n)], lambda e, T, B, X: [fn(e, T, B)], r, w, ps)
    G = lambda n, fn, r, w: op("G", [("n", 170 + 2.0 * n)], lambda e, T, B, X: [fn(e, T)], r, w)
    VG = lambda n, fn, r, w, kind="g": op("V", [(kind, n)], lambda e, T, B, X: [fn(e, T)], r, w)

    def gather(n, out, win, off, r, w, role):
        op("A", [("g", n)], lambda e, T, B, X: [e.activation(out(T), win(T).indirect(off(T)), AF.Copy)], r, w,
           alt=[("V", [("g", n)], lambda e, T, B, X: [e.tensor_copy(out(T), win(T).indirect(off(T)))])])
        ops[-1]["role"] = who[0] + role

    def P(n, mms, r, ps=None, pool="ps"):
        k = bank(pool) if ps is None else ps
        op("P", [("p", n)], lambda e, T, B, X: [e.matmul(*m) for m in mms(T, B)], r, [], k)
        return k

    def load(q, name, fn, w, ns, n=1, r=()):
        op(q, [("d", n)], lambda e, T, B, X: fn(e, T), list(r), w, sem="l" + name, lat=ns)
    load("S", "cur", lambda e, T: [e.dma_start(T.curi[:], T.cur[:])], ["curi"], 1800)
    load("A", "tok", lambda e, T: [e.dma_start(T.toki[:], T.tok[:])], ["toki"], 1800)
    load("S", "fwA", lambda e, T: [e.dma_start(T.fws[:, :2048], T.fw[:, :2048])], ["fwA"], LOAD)
    load("A", "hkA", lambda e, T: [e.dma_start(T.hks[:, :2304], T.hk[:, :2304])], ["hkA"], LOAD + 400)
    load("A", "hkB", lambda e, T: [e.dma_start(T.hks[:, 2304:], T.hk[:, 2304:])], ["hkB"], LOAD + 800)
    load("S", "th", lambda e, T: [e.dma_start(T.thi[x:x + 1], T.th[:, 32 * x:32 * x + 32]) for x in range(8)], ["thi"], LOAD, 8)
    load("S", "bwA", lambda e, T: [e.dma_start(T.bws[:, :2304], T.bw[:, :2304])], ["bwA"], 3500, r=["fwA"])
    load("S", "vvA", lambda e, T: [e.dma_start(T.vvs[:, :2304], T.vv[:, :2304])], ["vvA"], 5000, r=["hkA"])
    load("S", "fwB", lambda e, T: [e.dma_start(T.fws[:, 2048:], T.fw[:, 2048:2816])], ["fwB"], 3500, r=["bwA"])
    load("S", "bwB", lambda e, T: [e.dma_start(T.bws[:, 2304:], T.bw[:, 2304:])], ["bwB"], 4000, r=["bwA"])
    load("S", "vvB", lambda e, T: [e.dma_start(T.vvs[:, 2304:], T.vv[:, 2304:])], ["vvB"], 4500, r=["bwA"])

    IO = dict(allow_small_or_imprecise_dtypes=True)
    G(1, lambda e, T: e.iota(T.ci[:, 0:1], [[1, 1]], 0, 1), [], ["ci0"])
    G(512, lambda e, T: e.iota(T.nnum[:, :512], [[-1, 512]], OFS, 0, **IO), [], ["num0"])
    A(512, lambda e, T, B: e.activation(T.nnum[:, 512:1024], T.nnum[:, :512], AF.Identity, bias=-512.0), ["num0"], ["num1"])
    V(512, lambda e, T, B: e.tensor_scalar(T.nnum[:, 1024:1536], T.nnum[:, :512], -1024.0, None, ALU.add), ["num0"], ["num2"])
    A(512, lambda e, T, B: e.activation(T.nnum[:, 1536:2048], T.nnum[:, :512], AF.Identity, bias=-1536.0), ["num0"], ["num4"])
    G(160, lambda e, T: e.iota(T.rr[:], [[1, 160]], 0, 0, **IO), [], ["rr"])
    G(1024, lambda e, T: e.iota(T.nnum[:, 2048:], [[-1, 1024]], OFS - 2048, 0, **IO), [], ["num3"])
    ci = lambda T, k: T.ci[:, k:k + 1]
    cf = lambda T, k: T.cf[:, k:k + 1]
    AND, SHR, EQ, MUL, ADD = ALU.bitwise_and, ALU.arith_shift_right, ALU.is_equal, ALU.mult, ALU.add

    BITS = ((0, 15), (4, 7), (0, 7), (4, 1), (5, 3), (3, 1), (0, 1))
    op("V", [("v", 1)] * 7, lambda e, T, B, X: [e.tensor_scalar(ci(T, k + 1), ci(T, 0), a, b, SHR, AND) for k, (a, b) in enumerate(BITS)], ["ci0"], ["ci1"])
    V(8, lambda e, T, B: e.tensor_copy(T.cf[:, 0:8], T.ci[:, 0:8]), ["ci0", "ci1"], ["cf%d" % k for k in range(8)])

    def col(k, a, s1, s2, o0, o1):
        sc = lambda T: cf(T, s2[0]) if isinstance(s2, list) else s2
        r = ["cf%d" % j for j in [a] + (s2 if isinstance(s2, list) else [])]
        if o0 == MUL: A(1, lambda e, T, B: e.activation(cf(T, k), cf(T, a), AF.Identity, bias=sc(T), scale=s1), r, ["cf%d" % k])
        else: V(1, lambda e, T, B: e.tensor_scalar(cf(T, k), cf(T, a), s1, sc(T), o0, o1), r, ["cf%d" % k])
    col(8, 1, -1.0, 15.0, MUL, ADD)
    col(14, 2, 16.0, [8], MUL, ADD)
    col(9, 1, 15.0, -0.5, EQ, ADD)
    col(10, 4, 1000.0, [8], MUL, ADD)
    col(11, 5, 16.0, [10], MUL, ADD)
    col(12, 4, -BIG, BIG, MUL, ADD)
    col(13, 4, math.log(BIG), -math.log(BIG), MUL, ADD)
    col(16, 4, 4.0, [5], MUL, ADD)
    col(17, 1, 8.0, [16], MUL, ADD)
    col(20, 1, 8.0, [2], MUL, ADD)
    col(21, 4, 1000.0, [0], MUL, ADD); col(22, 4, -1000.0, [0], MUL, ADD)
    col(25, 1, -1.0, -15 / 32, MUL, ADD); col(26, 1, -1.0, -31 / 32, MUL, ADD)
    V(1, lambda e, T, B: e.tensor_copy(T.ofr[:, 0:1], cf(T, 20)), ["cf20"], ["ofr"])
    V(8, lambda e, T, B: e.tensor_scalar(T.ofq[:], T.rr[:, 0:8], 128.0, cf(T, 17), MUL, ADD), ["rr", "cf17"], ["ofq"])
    op("V", [("v", 4)] * 2, lambda e, T, B, X: [e.tensor_scalar(T.cb[:, 4 * h:4 * h + 4], T.rr[:, 0:4], -16.0, cf(T, 25 + h), MUL, ADD) for h in range(2)],
       ["rr", "cf25", "cf26"], ["cb"])

    def mark(name, a, b, k, val, shift=0.0, key=None):
        src = lambda T: T.rr[:, :b - a]
        if shift:
            V(b - a, lambda e, T, B: e.tensor_scalar(T[name][:, a:b], src(T), shift, cf(T, k), ADD, EQ), ["rr", "cf%d" % k], [key or name])
        else:
            V(b - a, lambda e, T, B: e.tensor_scalar(T[name][:, a:b], src(T), cf(T, k), cf(T, val[0]) if isinstance(val, list) else val, EQ, MUL),
              ["rr", "cf%d" % k] + (["cf%d" % val[0]] if isinstance(val, list) else []), [key or name])
    mark("a16", 0, 48, 1, 1.0, -16.0); mark("selw", 0, 64, 11, HIT); mark("rev", 0, 128, 14, 1.0)
    mark("inn", 0, 128, 0, -PEN); mark("idn", 0, 128, 0, -1.0)
    mark("zw", 0, 160, 21, 1.0, -16.0, "zw0"); mark("zw", 160, 320, 22, 1.0, -1016.0, "zw1")
    V(512, lambda e, T, B: e.memset(T.zz[:], 0.0), [], ["zz"])
    fill = lambda n, view, val, r, w: A(n, lambda e, T, B: e.activation(view(T), T.zz[:, :n], AF.Identity, bias=val), ["zz"] + r, w)
    for name, n, val, first in (("m16", 272, 1.0, 0.0), ("rk", 144, 1 / 32, -1e6)):
        fill(n, lambda T, name=name: T[name][:], val, [], [name])
        fill(n // 16, lambda T, name=name: T[name][:, 0::16], first, [name], [name])
    fill(8, lambda T: T.c9[:, :8], 0.0, [], ["c9"]); fill(1, lambda T: T.c9[:, 8:9], -96.0, [], ["c9x"])
    op("A", [("v", 32)] * 5, lambda e, T, B, X: [e.activation(T.msk[:, a:b:st], T.zz[:, :(b - a + st - 1) // st], AF.Identity, bias=v) for a, b, st, v in (
        (0, 64, 2, 0.0), (1, 64, 2, cf(T, 12)), (64, 192, 4, 0.0), (65, 192, 2, 1.0), (66, 192, 4, cf(T, 12)))], ["zz", "cf12"], ["msk"])
    A(128, lambda e, T, B: e.activation(T.ones[:], T.zz[:, :128], AF.Exp), ["zz"], ["ones"])
    G(256, lambda e, T: e.affine_select(T.thl[0:8, :], T.m16[0:8, 1:257], [[1, 8], [0, 32]], EQ, 0.0, 0, -1), ["m16"], ["thl"])
    op("V", [("v", 128)] * 2, lambda e, T, B, X: [e.tensor_scalar(T.thq[0:8, 128 * h:128 * h + 128], T.thi[0:8, h::2], -1.0, None, MUL) for h in range(2)], ["thi"], ["thq"])
    for name in ("idh", "i32"):
        G(128, lambda e, T, name=name: e.affine_select(T[name][:], T.ones[:], [[-1, 128]], EQ, 0.0, 0, 1), ["ones"], [name])

    def init(pool, k): ops[-1]["init"] = (pool, k)
    for k in range(POOLS["ps"]):
        op("P", [("p", 256)], lambda e, T, B, X, k=k: [e.matmul(T["ps%d" % k][:, :256], T.zz[0:1, :128], T.zz[0:1, :256], True, True)], ["zz"], []); init("ps", k)
    for k in range(POOLS["qd"]):
        V(512, lambda e, T, B, k=k: e.memset(T.qd[:, 1024 * k:1024 * k + 1024], 0.0), [], []); init("qd", k)
    zero = lambda view, key: V(512, lambda e, T, B: e.tensor_copy(view(T), T.zz[:]), ["zz", key], [key])
    for k in range(POOLS["qh"]):
        zero(lambda T, k=k: T.qh[:, 1024 * k:1024 * k + 1024], "qz%d" % k); init("qh", k)
    for k in range(POOLS["wx"]):
        for a in range(0, 8, 2):
            if k: G(512, lambda e, T, k=k, a=a: e.iota(T.wx[:, 8 * k + a:8 * k + a + 2], [[0, 512]], 0, 0, **IO), ["wz%d" % k], ["wz%d" % k])
            elif a % 4 == 0: zero(lambda T, a=a: T.wx[:, a:a + 4], "wz0")
        init("wx", k)
    for k in range(POOLS["tt"]):
        op("A", [("v", 16), ("v", 8)], lambda e, T, B, X, k=k: [e.activation(T.tf[:, 64 * k + 16:64 * k + 32], T.zz[:, :16], AF.Copy),
                                                                e.activation(T.kz[:, 256 * k + 143:256 * k + 256:16], T.zz[:, :8], AF.Copy)], ["zz"], []); init("tt", k)
    for pool, name, n in (("rb", "rb", 64), ("xx", "zt", 256)):
        for k in range(POOLS[pool]):
            fill(n, lambda T, o=TILES[name][1] * k, name=name, n=n: T[name][:, o:o + n], 0.0, [], []); init(pool, k)
    V(16, lambda e, T, B: e.tensor_copy(T.lsl[:, :16], T.curi[:]), ["curi"], ["Lc00", "Lc01"])
    for c in range(NC):
        VG(128, lambda e, T, c=c: e.tensor_copy(T.nq[:, 640 * c + 256:640 * c + 384], T.nnum[:, :2048].indirect(T.lsl[:, 8 * c:8 * c + 8])), ["num0", "num1", "num2", "num4", "Lc0%d" % c], ["nc0%d" % c])
    V(64, lambda e, T, B: e.tensor_copy(T.toku[:], T.toki[:]), ["toki"], ["toku"])
    op("G", [("n", 3000)], lambda e, T, B, X: X["tokens"](), ["toku"], ["tokl"], sem="rtok", lat=-1)
    G(128, lambda e, T: e.affine_select(T.sel0[:], T.ones[:], [[16, 8], [0, 16]], EQ, 0.0, 0, -1), ["ones"], ["sel0"])

    def send(name, src, dst, r, w, to, extra):
        op("G", [("r", 1)], lambda e, T, B, X: X["send"](name, src(T), dst(T), to), r, w, sem=name, lat=-1 - extra)

    gather(768, lambda T: T.tks[:], lambda T: T.hks[:, :], lambda T: T.tokl[:, 16:64], ["hkA", "hkB", "tokl"], ["tks"], "tk")
    send("rkey", lambda T: T.tks[:], lambda T: T.tkl[:], ["tks"], ["tkl"], -1, 2000)

    def halves(name, win, wk, off, ok):
        (k, v), = tiles(name)
        for h in range(2):
            gather(1024, lambda T, h=h: v(T, 1024 * h, 1024 * h + 1024), win, lambda T, h=h: off(T, 64 * h, 64 * h + 64), wk + [ok], [k + (h,)], name + str(h))
        ops[-2]["alts"].append(("A", [("g", 2048)], lambda e, T, B, X: [e.activation(v(T), win(T).indirect(off(T)), AF.Copy)]))
        ops[-1]["alts"].append(("A", [], lambda e, T, B, X: []))
        return [k + (0,), k + (1,)], v

    def scores(T, B, kg, qd, alone):
        at = [64 * (u % 2) + u // 2 if alone else u for u in range(128)]
        return [(B[32 * (y // 32):32 * (y // 32) + 16, y % 32:256:32], kg(T, 16 * u, 16 * u + 16), qd(T, u), alone, alone) for u, y in enumerate(at)]

    def spread(name, src, rk):
        if name in BYDMA:
            (k, v), = tiles("qh")
            op("S", [("d", 8)], lambda e, T, B, X: [e.dma_start(v(T, 128 * (4 * (h % 2) + h // 2), 128 * (4 * (h % 2) + h // 2) + 128, rows=slice(16 * h, 16 * h + 16)),
                                                                  T.nq[16 * h:16 * h + 16, src:src + 128]) for h in range(8)], rk, [k], sem="d" + name, lat=2000)
            return k, lambda T, u: v(T, u, 1024, 128)
        (k, v), = tiles("qd")
        VG(128, lambda e, T: e.tensor_copy(v(T).indirect(T.ofq[:]), T.nq[:, src:src + 128]), rk + ["ofq"], [k], "s")
        return k, lambda T, u: v(T, 8 * u, 8 * u + 8)

    def read(t, c, own, kq, qd):
        n = 2304 + 256 * t; who[0] = "o" if own else "h"; tc = "%d%d" % (t, c); x = NC * t + c
        ab = lambda s: [s + "A"] + ([s + "B"] if t else [])
        if own:
            Lb, kl = (lambda T: T.lso[:, 8 * x:8 * x + 8]), "Lb" + tc
            ob, kb, oc, kc = 640 * x, "nb" + tc, 640 * x + 256, "nc" + tc
        else:
            Lb, kl = (lambda T: T.lsl[:, 8 * (x + NC):8 * (x + NC) + 8]), "Lc%d%d" % (t + 1, c)
            ob, kb, oc, kc = 640 * (x + NC) + 256, "nc%d%d" % (t + 1, c), 640 * (x + NC) + 512, "hq" + tc
        (kfm, fm), (kin, inv), (kit, ivt) = tiles("fm", "inv", "ivt")
        (kok, ofk), = tiles("ofk")
        VG(128, lambda e, T: e.tensor_tensor(fm(T), T.bws[:, :n].indirect(Lb(T)), T.nq[:, ob:ob + 128], ADD), ab("bw") + [kl, kb], [kfm])
        V(64, lambda e, T, B: e.tensor_scalar(ofk(T), fm(T), -1.0, float(OFS), MUL, ADD), [kfm], [kok])
        kk, kg = halves("kg", lambda T: T.hks[:, :n], ab("hk"), ofk, kok)
        ps = P(256, lambda T, B: [m for h in range(2) for m in ((B[:, 384 + 64 * h:448 + 64 * h], T.idh[:], fm(T, h, 128, 2), True, False),
                                                                (B[:, 384 + 64 * h:448 + 64 * h], T.idn[:], T.nq[:, oc + h:oc + 128:2], False, True))], [kfm, kc, "idh", "idn"])
        op("A", [("v", 128)], lambda e, T, B, X: [e.activation(inv(T), B[:, 384:512], AF.Relu, bias=1.0)], [], [kin], ps,
           alt=[("V", [("v", 128)], lambda e, T, B, X: [e.tensor_scalar(inv(T), B[:, 384:512], 0.0, None, ALU.is_ge)])])
        P(1024, lambda T, B: scores(T, B, kg, qd, True)[:64], [kk[0], kq], ps)
        P(1024, lambda T, B: scores(T, B, kg, qd, True)[64:], [kk[1], kq], ps)
        (k1, s1), = tiles("s1")
        op("A", [("v", 256)], lambda e, T, B, X: [e.activation(s1(T), B[:, :256], AF.Copy)], [], [k1], ps, alt=[("V", [("v", 256)], lambda e, T, B, X: [e.tensor_copy(s1(T), B[:, :256])])])
        ops[-1]["role"] = who[0] + "s1"
        V(64, lambda e, T, B: e.transpose(ivt(T), inv(T)), [kin], [kit])
        P(384, lambda T, B: [(B[:, 256:384], T.inn[:], ivt(T), True, False), (B[:, 256:384], s1(T, 0, 128), T.zw[:, 16:144], False, False),
                             (B[:, 256:384], s1(T, 128, 256), T.zw[:, 0:128], False, True)], [k1, kit, "zw0", "inn"], ps)
        if own and t + 1 < RO:
            ksm, msc = "so" + tc, lambda T, a, b, st=1: T.mso[:, 128 * x - 128 + a:128 * x - 128 + b:st]
            (kx, ks), = tiles("ks"); (kmi, mi), (kfq, fq), (kof, ofc) = tiles("mi", "fq", "ofc")
            V(128, lambda e, T, B: e.tensor_tensor_scan(ks(T), T.rk[:, :128], B[:, 256:384], 0.0, ADD, ALU.max), ["rk"], [kx], ps)
            V(8, lambda e, T, B: e.tensor_copy(mi(T), ks(T, 15, 128, 16)), [kx], [kmi])
            V(16, lambda e, T, B: e.tensor_tensor(fq(T), ks(T, 15, 128, 16), mi(T), ALU.subtract), [kx, kmi], [kfq])
            P(384, lambda T, B: [m for b in range(2) for m in [(B[:, b:8:2], T.idh[:], T.cb[:, b:8:2], True, False)] + [
                (B[:, b:8:2], T.zw[:, 160 * b + 16 - 16 * (h - b):160 * b + 144 - 16 * (h - b)], fq(T, h, 8, 2), False, h == 1) for h in range(2)]], [kfq, "idh", "cb", "zw0", "zw1"], ps)
            V(8, lambda e, T, B: e.tensor_scalar(ofc(T), B[:, :8], -32.0, None, MUL), [], [kof], ps)
            op("V", [("g", 64)] * 2, lambda e, T, B, X: [e.tensor_tensor(T.crs[:, 128 * x + h:128 * x + 128:2], kg(T).indirect(ofc(T, 4 * h, 4 * h + 4)), T.tkl[:, 128 * x + h:128 * x + 128:2], ALU.max)
                                                         for h in range(2)], kk + [kof, "tkl"], ["cs" + tc])
            send("rC" + tc, lambda T: T.crs[:, 128 * x:128 * x + 128], lambda T: T.nq[:, 640 * (x + NC) + 128:640 * (x + NC) + 256], ["cs" + tc], ["qq%d%d" % (t + 1, c)], 1, 250)
            kmx, mx = kmi, mi
        else:
            (km, msc), = tiles("msc"); ksm = km + (1,)
            V(128, lambda e, T, B: e.tensor_tensor_scan(msc(T, 0, 128), T.m16[:, :128], B[:, 256:384], 0.0, MUL, ALU.max), ["m16"], [km + (0,)], ps)
            kmx, mx = km + (0,), lambda T: msc(T, 15, 128, 16)
        (khl, hl), = tiles("hl")
        op("A", [("v", 128), ("v", 64), ("v", 64)], lambda e, T, B, X: [e.activation(o, B[:, a:b], AF.Exp, scale=0.0078125) for o, a, b in (
            (B[:, 384:512], 256, 384), (hl(T, more=(0,)), 256, 320), (hl(T, more=(1,)), 320, 384))], [], [khl + (0,)], ps)
        op("V", [("v", 64)] * 2, lambda e, T, B, X: [e.tensor_tensor(hl(T, more=(2 + h,)), B[:, 384 + 64 * h:448 + 64 * h], hl(T, more=(h,)), ALU.subtract) for h in range(2)],
           [khl + (0,)], [khl + (1,)], ps)
        V(128, lambda e, T, B: e.tensor_tensor_scan(msc(T, 128, 256), T.m16[:, :128], B[:, 384:512], 0.0, MUL, ADD), ["m16"], [ksm], ps)
        yield
        who[0] = "O" if own else "H"
        (kwc, wc), = tiles("wc"); (kwx, wx), = tiles("wx"); (kvt, vt), = tiles("vt")
        V(128, lambda e, T, B: e.transpose(wc(T), hl(T)), [khl + (0,), khl + (1,)], [kwc])
        op("S", [("d", 8)], lambda e, T, B, X: [e.dma_start(wx(T, h, h + 1, rows=slice(16 * h, 16 * h + 16)), wc(T, rows=slice(16 * h, 16 * h + 16))) for h in range(8)],
           [kwc], [kwx], sem="w" + "ho"[own] + tc, lat=2000)
        kv, vg = halves("vg", lambda T: T.vvs[:, :n], ab("vv"), ofk, kok)
        apart = "ho"[own] + tc in APART; wd = 128 if apart else 64; st = wd // 32; oa = 272 * x + 16
        ps = P(4 * wd, lambda T, B: [(B[:, :, :wd], T.zz[0:1, :128], T.zz[0:1, :4 * wd], True, False)], ["zz"], None, "pa") if own else None
        for h in range(2):
            V(512, lambda e, T, B, h=h: e.transpose(vt(T, 1024 * h, 1024 * h + 1024), vg(T, 1024 * h, 1024 * h + 1024)), [kv[h]], [kvt + (h,)])
            if apart:
                ps = P(1024, lambda T, B, h=h: [(B[32 * (b // 16):32 * (b // 16) + 32, :, 8 * (b % 16):8 * (b % 16) + 8], vt(T, 32 * b, 32 * b + 32),
                                                 wx(T, more=(slice(4 * h, 4 * h + 4), b % 32)), not own, not own) for b in range(32 * h, 32 * h + 32)], [kvt + (h,), kwx], ps, "pa")
            else:
                ps = P(2048, lambda T, B, h=h: [(B[32 * (b // 16):32 * (b // 16) + 32, :, 4 * (b % 16):4 * (b % 16) + 4], vt(T, 32 * b, 32 * b + 32),
                                                 wx(T, more=(slice(4 * h + y, 4 * h + 4, 2), b % 32)), y == 0 and not own, y == 1 and not own) for b in range(32 * h, 32 * h + 32) for y in range(2)],
                       [kvt + (h,), kwx], ps, "pa")
        if not own and not apart:
            op("A", [("v", 256)], lambda e, T, B, X: [e.activation(T.bks[:, oa:oa + 256], B[:, :, :64], AF.Copy)], [], ["ba" + tc], ps,
               alt=[("V", [("v", 256)], lambda e, T, B, X: [e.tensor_copy(T.bks[:, oa:oa + 256], B[:, :, :64])])])
            return kmx, mx, ksm, msc, None, None
        if own and "h" + tc in APART: P(512, lambda T, B: [(B[:, :, st - 1:wd:st], T.i32[:], T.bkl[:, x, 16:144], False, True)], ["bl" + tc, "i32"], ps)
        elif own: P(1024, lambda T, B: [(B[:, :, st // 2 - 1:wd:st // 2], T.i32[:], T.bkl[:, x, 16:272], False, True)], ["bl" + tc, "i32"], ps)
        (ksl, sel), = tiles("sel")
        op("V", [("v", wd)] * 4, lambda e, T, B, X: [e.tensor_tensor_scan(sel(T, wd * a, wd * a + wd), T.msk[:, wd - 64:2 * wd - 64], B[:, a, :wd], 0.0, MUL, ADD) for a in range(4)],
           ["msk"], [ksl], ps)
        if not own: G(128, lambda e, T: e.affine_select(T.bks[:, oa:oa + 128], sel(T, 3, 512, 4), [[0, 128]], EQ, 0.0, 0, 0), [ksl], ["ba" + tc])
        return kmx, mx, ksm, msc, ksl, lambda T: sel(T, st - 1, 4 * wd, st)

    keep, run = {}, {}
    for t in range(RO):
        for c in range(NC):
            def scan(t=t, c=c):
                n = 2304 + 256 * t; x = NC * t + c; tc = "%d%d" % (t, c); on = 640 * x; who[0] = "s"
                (kf, fr), = tiles("fr"); (kok, ofk), = tiles("ofk")
                VG(128, lambda e, T: e.tensor_tensor(fr(T), T.fws[:, :n - 256].indirect(T.lsl[:, 8 * x:8 * x + 8]), T.nq[:, on + 256:on + 384], ALU.subtract),
                   ["fwA"] + (["fwB"] if t else []) + ["Lc" + tc, "nc" + tc], [kf])
                V(64, lambda e, T, B: e.tensor_scalar(ofk(T), fr(T), float(OFS), None, ADD), [kf], [kok])
                kk, kg = halves("kg", lambda T: T.hks[:, :n], ["hkA"] + (["hkB"] if t else []), ofk, kok)
                if x == 1:
                    ops[-1]["r"] = ops[-1]["r"] + ["hits0"]; ops[-2]["alts"].pop(); ops[-1]["alts"].pop()
                yield
                who[0] = "s"; q = lambda T: T.nq[:, on + 128:on + 256]
                if t == 0: gather(128, q, lambda T: T.hks[:, :], lambda T: T.toku[:, 8 * c:8 * c + 8], ["hkA", "hkB", "toku"], ["qq" + tc], "q")
                kq, qd = spread("o" + tc, on + 128, ["qq" + tc])
                ps = P(256, lambda T, B: [(B[:, :256], T.thl[0:8, 128 * c:128 * c + 128], T.thq[0:8, :], True, False)], ["thl", "thq"])
                P(1024, lambda T, B: scores(T, B, kg, qd, False)[:64], [kk[0], kq], ps)
                close = lambda T, B, a: [(B[:, a:a + CLOSE], T.zz[0:1, :128], T.zz[0:1, :CLOSE], False, True)]
                P(1024 + 64, lambda T, B: scores(T, B, kg, qd, False)[64:] + close(T, B, 0), [kk[1], kq, "zz"], ps)
                (ksg, sg), = tiles("sg")
                A(256, lambda e, T, B: e.activation(sg(T), B[:, :256], AF.Sign, bias=cf(T, 9)), ["cf9"], [ksg], ps)
                P(128, lambda T, B: [(B[:, 256:384], fr(T), T.rev[:], True, False)], [kf, "rev"], ps)
                P(1024 + 64, lambda T, B: [(B[32 * a:32 * a + 32, 256 + 32 * (h % 4) + 16 * (h // 4):272 + 32 * (h % 4) + 16 * (h // 4)], sg(T, 32 * h, 32 * h + 32), T.selw[:, 16 * a:16 * a + 16],
                                            False, False) for a in range(4) for h in range(8)] + close(T, B, 256), [ksg, "selw", "zz"], ps)
                (kx, ks), (kd, dz), (kt, tf) = tiles("kz", "dz", "tf"); (kr, rb), = tiles("rb")
                op("A", [("v", 128)], lambda e, T, B, X: [e.activation(dz(T), B[:, 256:384], AF.Relu, scale=-4.0)], [], [kd, "hits%d" % x], ps,
                   alt=[("V", [("v", 128)], lambda e, T, B, X: [e.tensor_scalar(dz(T), B[:, 256:384], 0.0, 1e4, ALU.is_lt, MUL)])])
                V(128, lambda e, T, B: e.tensor_tensor_scan(ks(T, 0, 128), dz(T), B[:, 256:384], 0.0, ALU.min, ALU.max), [kd], [kx], ps)
                V(9, lambda e, T, B: e.tensor_tensor_scan(tf(T, 32, 41), T.c9[:, :9], ks(T, 15, 144, 16), 0.0, ADD, ALU.max), ["c9", "c9x", kx], [kt + (2,)])
                V(8, lambda e, T, B: e.tensor_scalar(tf(T, 16, 24), ks(T, 15, 128, 16), tf(T, 40, 41), tf(T, 39, 40), ALU.is_lt, MUL), [kx, kt + (2,)], [kt + (3,)])
                VG(16, lambda e, T: e.tensor_tensor(rb(T).indirect(T.ofr[:, 0:1]), ks(T, 15, 256, 16), tf(T, 16, 32), ALU.max), [kx, kt + (3,), "ofr"], [kr], "s")
                P(1024, lambda T, B: [(B[32 * (h // 2):32 * (h // 2) + 32, :8], T.a16[:, 16 - 16 * (h % 2):48 - 16 * (h % 2)], rb(T, 8 * h, 8 * h + 8), h % 2 == 0, h % 2 == 1)
                                      for h in range(8)], [kr, "a16"], ps)
                V(8, lambda e, T, B: e.tensor_scalar(T.lso[:, 8 * x:8 * x + 8], B[:, :8], OFS - HIT, None, ADD), [], ["Lb" + tc], ps)
                send("rL" + tc, lambda T: T.lso[:, 8 * x:8 * x + 8], lambda T: T.lsl[:, 8 * (x + NC):8 * (x + NC) + 8], ["Lb" + tc], ["Lc%d%d" % (t + 1, c)], 1, 0)
                gather(128, lambda T: T.nq[:, on:on + 128], lambda T: T.nnum[:, :n], lambda T: T.lso[:, 8 * x:8 * x + 8], ["num0", "num1", "num2", "num3", "num4", "Lb" + tc], ["nb" + tc], "nb")
                send("rN" + tc, lambda T: T.nq[:, on:on + 384], lambda T: T.nq[:, on + 640 * NC + 256:on + 640 * NC + 640], ["nb" + tc, "qq" + tc, "nc" + tc],
                     ["nc%d%d" % (t + 1, c), "hq" + tc], 1, 700)
                yield
                keep[x] = yield from read(t, c, True, kq, qd)
            run["o", NC * t + c] = scan()
        for c in range(NC):
            def helper(t=t, c=c):
                x = NC * t + c; tc = "%d%d" % (t, c); ob = 272 * x; oq = 640 * (x + NC) + 384; who[0] = "h"
                kq, qd = spread("h" + tc, oq, ["hq" + tc])
                kmx, mx, ksm, msc, ksl, sel = yield from read(t, c, False, kq, qd)
                G(16, lambda e, T: e.affine_select(T.bks[:, ob:ob + 16], msc(T, 15, 256, 16), [[0, 16]], EQ, 0.0, 0, 0), [kmx, ksm], ["bm" + tc])
                part = lambda name, a, b, r, w: send(name + tc, lambda T: T.bks[:, ob + a:ob + b], lambda T: T.bkl[:, x, a:b], r, w, -1, 3.5 * (b - a))
                end = 144 if "h" + tc in APART else 272
                if tc in EARLY:
                    part("rM", 0, 16, ["bm" + tc], ["bn" + tc]); part("rB", 16, end, ["ba" + tc], ["bl" + tc])
                else: part("rB", 0, end, ["bm" + tc, "ba" + tc], ["bl" + tc, "bn" + tc])
            run["h", NC * t + c] = helper()
        for c in range(NC):
            def both(t=t, c=c):
                cs = [c] if t + 1 == RO else list(range(NC)) if c + 1 == NC else []
                if not cs:
                    yield
                n = len(cs); x = NC * t + cs[0]; oy = 128 * x; who[0] = "b"; names = lambda s: [s + "%d%d" % (t, y) for y in cs]
                mx = keep[x][1] if n == 1 else lambda T: T.mi[:, 8 * x:8 * x + 16]
                (kz, zt), (kx, xx), (kf, mh) = tiles("zt", "xx", "mh")
                V(32, lambda e, T, B: e.tensor_tensor(zt(T, 0, 128 * n, 16), mx(T), T.bkl[:, x:x + n, 0:8], ALU.max), [keep[x + y][0] for y in range(n)] + names("bn"), [kz + (0,)])
                V(32, lambda e, T, B: e.tensor_tensor(xx(T, 0, 8 * n), keep[x][3](T, 143, 128 + 128 * n, 16), T.bkl[:, x:x + n, 8:16], ADD), [keep[x + y][2] for y in range(n)] + names("bn"), [kx + (0,)])
                A(16, lambda e, T, B: e.activation(xx(T, 16, 16 + 8 * n), zt(T, 0, 128 * n, 16), AF.Exp, scale=-0.0078125), [kz + (0,)], [kx + (1,)])
                V(32, lambda e, T, B: e.tensor_tensor(zt(T, 1, 128 * n, 16), xx(T, 0, 8 * n), xx(T, 16, 16 + 8 * n), MUL), [kx + (0,), kx + (1,)], [kz + (1,)])
                op("V", [("v", 64)] * 2 * n, lambda e, T, B, X: [e.transpose(T.mss[:, oy + 128 * (h // 2) + h % 2:oy + 128 * (h // 2) + 128:2], zt(T, 64 * h, 64 * h + 64)) for h in range(2 * n)],
                   [kz + (0,), kz + (1,)], names("mo"))
                if t + 1 < RO: G(128 * n, lambda e, T: e.affine_select(mh(T, 0, 128 * n), T.mss[:, oy:oy + 128 * n], [[0, 128 * n]], EQ, 0.0, 0, 0), names("mo"), [kf])
                else: A(128, lambda e, T, B: e.activation(mh(T, 0, 128), T.mss[:, oy:oy + 128], AF.Copy), names("mo"), [kf])
                ps = P(512 * n, lambda T, B: [(B[32 * (z % 4):32 * (z % 4) + 32, 128 * (z // 4) + 32 * a:128 * (z // 4) + 32 * a + 32], T.sel0[:, 32 * a:32 * a + 32], mh(T, 32 * z, 32 * z + 32), True, True)
                                              for z in range(4 * n) for a in range(4)], [kf, "sel0"])
                A(128 * n, lambda e, T, B: e.activation(B[:, 256:256 + 128 * n], B[:, :128 * n], AF.Exp, bias=cf(T, 13), scale=-0.0078125), ["cf13"], [], ps)
                for y in range(n):
                    o = oy + 128 * y
                    V(128, lambda e, T, B, o=o, y=y: e.tensor_tensor(T.yas[:, o:o + 128], keep[x + y][5](T), B[:, 256 + 128 * y:384 + 128 * y], MUL), [keep[x + y][4]], [names("yo")[y]], ps)
                    for q, zs in [("S", (z,)) for z in range(4)] if t + 1 < RO else (("S", (0, 1)), ("A", (2, 3))):
                        op(q, [("d", 4 * len(zs))], lambda e, T, B, X, o=o, zs=zs: [e.dma_start(T.ya[32 * a:32 * a + 32, o + 32 * z:o + 32 * z + 32], T.yas[32 * z:32 * z + 32, o + 32 * a:o + 32 * a + 32])
                                                                                    for z in zs for a in range(4)], [names("yo")[y]], [], sem="stored", lat=2300)
                if t >= RO - 2 and c == NC - 1:
                    a, b = (0, 768) if t == RO - 2 else (768, 1024)
                    op("S", [("n", 120)], lambda e, T, B, X: [e.dma_start(T.ym[:, a:b], T.mss[0::16, a:b]), e.dma_start(T.ys[:, a:b], T.mss[1::16, a:b])],
                       ["mo%d%d" % (y, z) for y in range(a // 256, b // 256) for z in range(NC)], [], sem="stored", lat=2200)
                yield
            run["b", NC * t + c] = both()
    for k in range(-NC, RO * NC + 8):
        for j, (name, lag) in enumerate(stages):
            if 0 <= k - lag < RO * NC:
                first = len(ops); next(run[name, k - lag], None)
                for o in ops[first:]: o["turn"] = k; o["stage"] = j
    lastw, readers, acc = {}, {}, {}
    for i, o in enumerate(ops):
        d = set()
        for k in o["r"]:
            if k in lastw: d.add(lastw[k])
        for k in o["w"]:
            if k in lastw: d.add(lastw[k])
            d.update(readers.get(k, []))
        o["line"] = set()
        if o["ps"] is not None:
            o["line"].update(acc.get(o["ps"], [])); acc.setdefault(o["ps"], []).append(i)
        for k in o["r"]: readers.setdefault(k, []).append(i)
        for k in o["w"]: lastw[k] = i; readers[k] = []
        d.discard(i); o["dep"] = d
        o["tiles"] = sorted(set(k[:2] for k in o["r"] + o["w"] if isinstance(k, tuple)) | ({o["ps"]} if o["ps"] is not None else set()))
        o["bank"] = o["ps"] and o["ps"][0] + str(where[o["ps"]])
    users = {}; last = {o["init"]: [i] for i, o in enumerate(ops) if "init" in o}
    for i, o in enumerate(ops):
        for k in o["tiles"]: users.setdefault(k, []).append(i)
    for k in sorted(users):
        for i in users[k]: ops[i]["line" if k[0] in ("ps", "pa") else "dep"].update(last.get((k[0], where[k]), []))
        last[k[0], where[k]] = users[k]
    for i, o in enumerate(ops):
        same = lambda j: len(o["alts"]) == len(ops[j]["alts"]) == 1 and o["alts"][0][0] == ops[j]["alts"][0][0] != "A"
        o["wait"] = sorted(o["dep"] | set(j for j in o["line"] if not same(j))); o["dep"] = sorted(o["dep"] | o["line"])
    return ops


def after(o, M):
    if o["sem"] is None: return M["hop"]
    return o["lat"] * M["l"] if o["lat"] >= 0 else M["net"] - o["lat"]


def plan(ops, M, per, look, sticky, idle, marg, slack=1e9, cap=99, lead=99, ahead=(0,) * 7):
    n = len(ops)
    succ = [[] for _ in ops]
    for i, o in enumerate(ops):
        for d in o["dep"]: succ[d].append(i)
    pick = [0] * n
    du = [dur(o["alts"][pick[i]][1], M) for i, o in enumerate(ops)]
    pr = [0.0] * n
    for i in range(n - 1, -1, -1):
        o = ops[i]
        pr[i] = du[i] + after(o, M) + max([pr[j] for j in succ[i]], default=-o.get("turn", 0) * per)
    pr = [p + (1000.0 * ahead[o["stage"]] if "stage" in o else 0.0) for p, o in zip(pr, ops)]
    users = {}
    for i, o in enumerate(ops):
        for k in o["tiles"]: users.setdefault(k, []).append(i)
    for i, o in enumerate(ops):
        if "init" in o: pr[i] = 600 + pr[users[o["init"]][0]]
    for i, o in enumerate(ops):
        if o["sem"] in ["l" + k for k in LOADS]: pr[i] = 1e9 - i
    for i in range(n - 1, -1, -1): pr[i] = max([pr[i]] + [du[i] + after(ops[i], M) + pr[j] for j in succ[i]])
    last = {p: [[] for _ in range(m)] for p, m in POOLS.items()}
    held = {p: [0] * m for p, m in POOLS.items()}
    live = {p: np.zeros(n + 1, int) for p in POOLS}
    for k, u in users.items(): live[k[0]][u[0]:u[-1] + 1] += 1
    for i, o in enumerate(ops):
        if "init" in o: held[o["init"][0]][o["init"][1]] = 1; live[o["init"][0]][:i + 1] += 1
    cur = 0
    free = {e: 0.0 for e in "VAPGS"}; left = [len(o["dep"]) for o in ops]; avail = [0.0] * n; fin = [0.0] * n
    where = {}; prev = {}; since = {}; order = []; extra = {}; placed = [False] * (n + 1)
    ready = [i for i in range(n) if not left[i]]
    while ready:
        cand = []; spot = {}; most = {}; rdy = {}
        while placed[cur]: cur += 1
        for i in ready:
            o = ops[i]; r = avail[i]; ok = True
            for k in o["tiles"]:
                p = k[0]
                if k in where: r = max(r, since[k]); continue
                if p not in spot:
                    most[p] = np.maximum.accumulate(live[p][cur:])
                    fr = [(max([fin[j] for j in last[p][x]], default=-1e3), x) for x in range(POOLS[p]) if not held[p][x]]
                    spot[p] = (len(fr),) + min(fr) if fr else (0, 0, 0)
                if not spot[p][0] or (users[k][0] > cur and most[p][users[k][0] - 1 - cur] >= POOLS[p]): ok = False
                else: r = max(r, spot[p][1] + M["hop"])
            if ok: cand.append((max(r, free[o["alts"][pick[i]][0]]), i)); rdy[i] = r
        flex = [c for c in cand if len(ops[c[1]]["alts"]) > 1 and not pick[c[1]] and du[c[1]] > 500 and max(rdy[c[1]], free["V"]) + marg < c[0]]
        if flex:
            tv = min(max(rdy[c[1]], free["V"]) for c in flex)
            c = max((c for c in flex if max(rdy[c[1]], free["V"]) <= tv + 1), key=lambda c: pr[c[1]])
            nv = min([y[0] for y in cand if ops[y[1]]["alts"][pick[y[1]]][0] == "V" and pr[y[1]] > pr[c[1]] - slack], default=1e12)
            if tv <= min(y[0] for y in cand) and nv > tv + idle and sum(pick) < min(cap, lead + cap * ops[c[1]].get("turn", 0) / 8):
                pick[c[1]] = 1; cand.remove(c); cand.append((tv, c[1]))
        t0 = min(c[0] for c in cand)
        now = max((c for c in cand if c[0] <= t0 + 1.0), key=lambda c: pr[c[1]])
        eng = ops[now[1]]["alts"][pick[now[1]]][0]
        soon = [c for c in cand if ops[c[1]]["alts"][pick[c[1]]][0] == eng and c[0] < t0 + look * du[now[1]] and pr[c[1]] > pr[now[1]] + sticky]
        if soon: now = max(soon, key=lambda c: pr[c[1]] - 4 * (c[0] - t0))
        st, i = now; o = ops[i]; x = pick[i]; e = o["alts"][x][0]
        fin[i] = free[e] = st + du[i]; extra[i] = []
        if "init" in o: held[o["init"][0]][o["init"][1]] = 0; last[o["init"][0]][o["init"][1]] = [i]; live[o["init"][0]][:i + 1] -= 1
        for k in o["tiles"]:
            p = k[0]
            if k not in where:
                b = spot[p][2]; where[k] = b; prev[k] = last[p][b]; since[k] = spot[p][1] + M["hop"]
                last[p][b] = users[k]; held[p][b] = len(users[k])
                live[p][:users[k][0]] += 1
            held[p][where[k]] -= 1; extra[i] += prev[k]
            if not held[p][where[k]]: live[p][:users[k][-1] + 1] -= 1
        order.append((i, x)); ready.remove(i); placed[i] = True
        for j in succ[i]:
            avail[j] = max(avail[j], fin[i] + after(o, M)); left[j] -= 1
            if not left[j]: ready.append(j)
    return order, where, extra


def justify(ops, order, extra, M):
    n = len(ops); pick = dict(order); dep = [ops[i]["dep"] + extra[i] for i in range(n)]; succ = [[] for _ in ops]
    for i in range(n):
        for d in dep[i]: succ[d].append(i)
    du = [dur(o["alts"][pick[i]][1], M) for i, o in enumerate(ops)]; af = [after(o, M) for o in ops]

    def lay(seq, forward):
        busy = {e: [] for e in "VAPGS"}; st = {}
        for i in seq:
            t = max([st[j] + du[j] + af[j] for j in dep[i]], default=0.0) if forward else max([st[j] + du[j] for j in succ[i]], default=0.0) + af[i]
            q = busy[ops[i]["alts"][pick[i]][0]]; k = 0
            while k < len(q) and t + du[i] > q[k][0] + 1e-6: t = max(t, q[k][1]); k += 1
            q.insert(k, (t, t + du[i])); st[i] = t
        return st
    seq = [i for i, x in order]; st = lay(seq, True)
    seq = sorted(seq[::-1], key=lambda i: -st[i] - du[i]); st = lay(seq, False)
    seq = sorted(seq[::-1], key=lambda i: (0, i) if i < len(LOADS) else (1, -st[i] - du[i])); st = lay(seq, True)
    return [(i, pick[i]) for i in sorted(seq, key=lambda i: st[i])]


def place(ops, order, M):
    users = {}
    for i, o in enumerate(ops):
        for k in o["tiles"]: users.setdefault(k, []).append(i)
    last = {p: [[] for _ in range(m)] for p, m in POOLS.items()}; held = {p: [0] * m for p, m in POOLS.items()}
    for o in ops:
        if "init" in o: held[o["init"][0]][o["init"][1]] = 1
    free = {e: 0.0 for e in "VAPGS"}; done = {}; where = {}; prev = {}; extra = {}
    for i, x in order:
        o = ops[i]; e, cost, _ = o["alts"][x]; extra[i] = []
        if "init" in o: held[o["init"][0]][o["init"][1]] = 0; last[o["init"][0]][o["init"][1]] = [i]
        for k in o["tiles"]:
            p = k[0]
            if k not in where:
                b = min((max([done[j] for j in last[p][y]], default=0.0), y) for y in range(POOLS[p]) if not held[p][y])[1]
                where[k] = b; prev[k] = last[p][b]; last[p][b] = users[k]; held[p][b] = len(users[k])
            held[p][where[k]] -= 1; extra[i] += prev[k]
        free[e] = max([free[e]] + [done[d] for d in o["dep"] + extra[i]]) + dur(cost, M); done[i] = free[e] + after(o, M)
    return where, extra


def join(ops, order, extra):
    total = lambda q: sum(replay(ops, q, extra, M)[0] for M in CHECK)
    best = total(order)
    for i, o in enumerate(ops[:-1]):
        pick = dict(order)
        if len(o["alts"]) == 3 and o["alts"][2][1] and pick[i] == pick[i + 1] == 0:
            at = min(k for k, (j, x) in enumerate(order) if j in (i, i + 1))
            q = order[:at] + [(i, 2), (i + 1, 2)] + [y for y in order[at:] if y[0] not in (i, i + 1)]
            s = total(q)
            if s < best: best, order = s, q
    return order


def replay(ops, order, extra, M):
    free = {e: 0.0 for e in "VAPGS"}; done = {}; busy = {e: 0.0 for e in "VAPGS"}
    for i, x in order:
        o = ops[i]; e, cost, _ = o["alts"][x]
        st = max([free[e]] + [done[d] for d in o["wait"]])
        d = dur(cost, M); free[e] = st + d; busy[e] += d; done[i] = free[e] + after(o, M)
    return max(done.values()), busy


CLOSE = 8
PLAN = (9500.0, 0.15, 100.0, 250.0, 400.0, 4000.0, 22, 99, (0, 4, -2, 2, -7, -2, -4))
CACHE = {}


def lay(ops, pick, seq, M, forward):
    busy = {e: [] for e in "VAPGS"}; st = {}
    for i in seq:
        o = ops[i]; e, cost, _ = o["alts"][pick[i]]; du = dur(cost, M)
        if forward: t = max([st[j][1] + (after(ops[j], M) if j in o["wait"] else 0.0) for j in o["dep"]], default=0.0)
        else: t = max([st[j][1] + (after(o, M) if i in ops[j]["wait"] else 0.0) for j in o["succ"]], default=after(o, M))
        q = busy[e]; k = 0
        while k < len(q) and t + du > q[k][0] + 1e-6: t = max(t, q[k][1]); k += 1
        q.insert(k, (t, t + du)); st[i] = (t, t + du)
    return st


def arrange(ops, M, per, ahead, onv, rounds=3):
    n = len(ops)
    for o in ops: o["succ"] = []
    for i, o in enumerate(ops):
        for d in o["dep"]: ops[d]["succ"].append(i)
    pick = [int(len(o["alts"]) > 1 and onv(o)) for o in ops]; pr = [0.0] * n
    for i in range(n - 1, -1, -1):
        o = ops[i]
        pr[i] = dur(o["alts"][pick[i]][1], M) + after(o, M) + max([pr[j] for j in o["succ"]], default=-o.get("turn", 0) * per)
    pr = [p + (1000.0 * ahead[o["stage"]] if "stage" in o else 0.0) for p, o in zip(pr, ops)]
    for i in range(n - 1, -1, -1): pr[i] = max([pr[i]] + [1 + pr[j] for j in ops[i]["succ"]])
    first = lambda i: (0, i) if i < len(LOADS) else (1, 0)
    seq = sorted(range(n), key=lambda i: first(i) + (-pr[i], i)); best = None
    for _ in range(rounds + 1):
        st = lay(ops, pick, seq, M, True); seq = sorted(seq, key=lambda i: st[i][0])
        order = [(i, pick[i]) for i in seq]; total = sum(replay(ops, order, {}, C)[0] / w for C, w in CHECK)
        if best is None or total < best[0]: best = (total, order)
        seq = sorted(seq[::-1], key=lambda i: -st[i][1]); st = lay(ops, pick, seq, M, False)
        seq = sorted(seq[::-1], key=lambda i: first(i) + (-st[i][1],))
    return best[1]


def plan2(ops, M, per, ahead, look, sticky, bias, vmin, slack, seed=0, noise=0.0):
    n = len(ops); succ = [[] for _ in ops]
    for i, o in enumerate(ops):
        for d in o["dep"]: succ[d].append(i)
    du = [[dur(a[1], M) for a in o["alts"][:2]] for o in ops]; pr = [0.0] * n
    for i in range(n - 1, -1, -1):
        o = ops[i]; pr[i] = du[i][0] + after(o, M) + max([pr[j] for j in succ[i]], default=-o.get("turn", 0) * per)
    shift = lambda o: 1000.0 * ahead[o["stage"]] + noise * math.sin(seed * (1 + o["stage"] + 7 * (o["turn"] + 2)) + seed * seed)
    pr = [p + (shift(o) if "stage" in o else 0.0) for p, o in zip(pr, ops)]
    for i in range(len(LOADS)): pr[i] = 1e9 - i
    for i in range(n - 1, -1, -1): pr[i] = max([pr[i]] + [du[i][0] + after(ops[i], M) + pr[j] for j in succ[i]])
    free = {e: 0.0 for e in "VAPGS"}; left = [len(o["dep"]) for o in ops]; avail = [0.0] * n; order = []
    ready = [i for i in range(n) if not left[i]]
    rest = {e: sum(du[i][0] for i, o in enumerate(ops) if o["alts"][0][0] == e) for e in "VAPGS"}
    while ready:
        cand = [(max(avail[i], free[ops[i]["alts"][x][0]]) + (bias if x else 0), i, x) for i in ready for x in range(len(du[i]))
                if not x or du[i][1] < 500 or free["V"] + rest["V"] + 2 * du[i][1] + slack <= free["A"] + rest["A"]]
        t0 = min(c[0] for c in cand)
        now = max((c for c in cand if c[0] <= t0 + 1.0), key=lambda c: (pr[c[1]] - (vmin if c[2] else 0), -c[2]))
        eng = ops[now[1]]["alts"][now[2]][0]
        soon = [c for c in cand if ops[c[1]]["alts"][c[2]][0] == eng and c[0] < t0 + look * du[now[1]][now[2]] and pr[c[1]] - (vmin if c[2] else 0) > pr[now[1]] - (vmin if now[2] else 0) + sticky]
        if soon: now = max(soon, key=lambda c: pr[c[1]] - 4 * (c[0] - t0))
        st, i, x = now; e = ops[i]["alts"][x][0]; st = max(avail[i], free[e])
        free[e] = st + du[i][x]; order.append((i, x)); ready.remove(i); rest[ops[i]["alts"][0][0]] -= du[i][0]
        for j in succ[i]:
            avail[j] = max(avail[j], free[e] + (after(ops[i], M) if i in ops[j]["wait"] else 0.0)); left[j] -= 1
            if not left[j]: ready.append(j)
    return order


def polish(ops, order, M, rounds=2):
    for o in ops: o["succ"] = []
    for i, o in enumerate(ops):
        for d in o["dep"]: ops[d]["succ"].append(i)
    pick = dict(order); seq = [i for i, x in order]
    first = lambda i: (0, i) if i < len(LOADS) else (1, 0)
    tot = lambda q: sum(replay(ops, q, {}, C)[0] / w for C, w in CHECK)
    best = (tot(order), order)
    st = lay(ops, pick, seq, M, True)
    for _ in range(rounds):
        seq = sorted(seq[::-1], key=lambda i: -st[i][1]); st = lay(ops, pick, seq, M, False)
        seq = sorted(seq[::-1], key=lambda i: first(i) + (-st[i][1],))
        st = lay(ops, pick, seq, M, True); seq = sorted(seq, key=lambda i: st[i][0])
        q = [(i, pick[i]) for i in seq]; s = tot(q)
        if s < best[0]: best = (s, q)
    return best[1]


def improve(ops, order, iters, seed=1, temp=0.0004, lam=0.15):
    n = len(ops); state = [seed]; S = 32; head = len(LOADS)

    def rnd(k=None):
        state[0] = (state[0] * 1103515245 + 12345) % 2147483648
        return state[0] / 2147483648 if k is None else (state[0] >> 8) % k
    dep = [o["wait"] for o in ops]; deps = [set(o["dep"]) for o in ops]
    eng = [["VAPGS".index(a[0]) for a in o["alts"]] for o in ops]
    tab = [[[dur(a[1], M) for a in o["alts"]] for o in ops] for M, w in CHECK]
    af = [[after(o, M) for o in ops] for M, w in CHECK]

    def run(seq, pick, m, old, k0):
        if old is None: done = [0.0] * n; par = [None] * n; snap = [([0.0] * 5, [None] * 5)]
        else: done = old[0][:]; par = old[1][:]; snap = old[2][:k0 // S + 1]
        free = snap[-1][0][:]; last = snap[-1][1][:]; D = tab[m]; F = af[m]
        for k in range(k0 // S * S, n, S):
            for i in seq[k:k + S]:
                x = pick[i]; e = eng[i][x]; st = free[e]; p = last[e]; q = True
                for j in dep[i]:
                    if done[j] > st: st = done[j]; p = j; q = False
                free[e] = st = st + D[i][x]; last[e] = i; done[i] = st + F[i]; par[i] = (p, q)
            snap.append((free[:], last[:]))
        return done, par, snap

    def total(seq, pick, old, k0):
        out = [run(seq, pick, m, old and old[m], k0) for m in range(len(CHECK))]
        return sum((max(r[0]) + lam * sum(r[0]) / n) / w for r, (M, w) in zip(out, CHECK)) / len(CHECK) / 1000, out
    seq = [i for i, x in order]; pick = [x for i, x in sorted(order)]
    cur, res = total(seq, pick, None, 0); best = (cur, seq, pick)
    flex = [i for i, o in enumerate(ops) if len(o["alts"]) > 1]; pairs = [i for i in flex if len(ops[i]["alts"]) == 3 and ops[i]["alts"][2][1]]
    for it in range(iters):
        done, par, _ = res[rnd(len(res))]; r = rnd(); s2 = seq; p2 = pick
        tie = lambda j, y: pick[j] == 2 and pick[y] == 2 and j == y + 1 and not tab[0][j][2]
        if r < 0.12:
            i = flex[rnd(len(flex))]
            if pick[i] == 2: continue
            p2 = list(pick); p2[i] = 1 - pick[i]; a = seq.index(i)
            near = [j for j in seq[max(0, a - 60):a + 60] if len(eng[j]) > 1 and pick[j] == 1 - pick[i] and tab[0][j][0] == tab[0][i][0]]
            if near and rnd() < 0.6: j = near[rnd(len(near))]; p2[j] = pick[i]; a = min(a, seq.index(j))
        elif r < 0.2:
            i = pairs[rnd(len(pairs))]; p2 = list(pick); a = min(seq.index(i), seq.index(i + 1))
            if pick[i] == 2: p2[i] = 0; p2[i + 1] = rnd(2)
            else: p2[i] = p2[i + 1] = 2; s2 = seq[:a] + [i, i + 1] + [j for j in seq[a:] if j != i and j != i + 1]
        else:
            if r < 0.8:
                c = []; turns = []; i = done.index(max(done))
                while i is not None:
                    p, q = par[i]
                    if not q: turns.append((len(c), i))
                    elif p is not None and p >= head: c.append((i, p))
                    i = p
                if not c: continue
                k, y = turns[rnd(len(turns))] if turns and r < 0.65 else (rnd(len(c)), None)
                i, p = c[max(0, min(len(c) - 1, k + rnd(6) - 3 if y is not None else k))]
                if y is not None and y >= head and r < 0.35:
                    later = [j for j in seq[seq.index(y) + 1:][:60] if eng[j][pick[j]] == eng[y][pick[y]]]
                    if not later: continue
                    i, p = later[rnd(len(later))], y
            else:
                i = rnd(n); p, q = par[i]
                if not q or p is None or p < head: continue
            a, b = seq.index(p), seq.index(i)
            if rnd() < 0.5:
                if rnd() < 0.3: a = min(a, max(head, a - (5, 15, 30)[rnd(3)]))
                got = {i}; mv = [i]
                for j in seq[b - 1:a - 1:-1]:
                    if any(j in deps[y] or tie(y, j) for y in got): got.add(j); mv.append(j)
                if p in got: continue
                s2 = seq[:a] + mv[::-1] + [j for j in seq[a:b + 1] if j not in got] + seq[b + 1:]
            else:
                b = min(n - 1, b + (0, 0, 5, 15, 30)[rnd(5)]); got = {p}; mv = [p]
                for j in seq[a + 1:b + 1]:
                    if deps[j] & got or (j - 1 in got and tie(j, j - 1)): got.add(j); mv.append(j)
                if i in got: continue
                s2 = seq[:a] + [j for j in seq[a:b + 1] if j not in got] + mv + seq[b + 1:]
        v, out = total(s2, p2, res, a)
        if v <= cur or rnd() < math.exp((cur - v) / (temp * (1 - it / iters) + 1e-9)):
            seq, pick, cur, res = s2, p2, v, out
            if v < best[0]: best = (v, seq, pick)
    return [(i, best[2][i]) for i in best[1]]


ARR = (4000.0, (0, 2, -7, 23, 4, -46, -5), 0.3, 0.0, 50.0, 4000.0, -1500.0, 481, 3000.0)
ITERS = (32000, 14000)


def schedule():
    if "s" not in CACHE:
        ops = build(); cheap = CHECK.pop()
        order = improve(ops, polish(ops, plan2(ops, REF, *ARR), REF), ITERS[0])
        CHECK.append(cheap)
        CACHE["s"] = (ops, improve(ops, order, ITERS[1], 2, 0.0002))
    return CACHE["s"]


def rank_program(g, core, T, topo):
    rank = T.rank_of(core)
    if rank is None:
        return
    ops, order = schedule()
    N = len(T.cores); peer = lambda k: T.cores[(rank + k) % N]
    sent = [0]; arrive = {}

    def send(name, src, dst, to):
        rid, pid, _ = topo.addr(peer(to))
        g.remote_dma(dst, src, T.sem[name], T.sem.sent, pid, rid, topo.mask(core, peer(to)))
        sent[0] += len(topo.engines(core, peer(to))); arrive[name] = len(topo.engines(peer(-to), core))
        return []

    def share(src, dst, t):
        e = topo.engines(src, dst); h = len(e) // 2; q = h // 2
        return (e[:h], e[h:h + q], e[h + q:])[t - 1]

    def tokens():
        tr = []
        for t in range(1, RO):
            rid, pid, _ = topo.addr(peer(t)); e = share(core, peer(t), t)
            tr.append(RemoteDMATransfer(dst_ids=[DstId(rid=rid, pnc=pid)], dma_engine_mask=sum(1 << x for x in e), remote_sem=T.sem.rtok,
                                        src=T.toku[:, 16 * t:16 * t + 16], dst=T.tokl[:, 16 * t:16 * t + 16]))
            sent[0] += len(e)
        g.remote_dma_fused(tr, local_sem=T.sem.sent)
        arrive["rtok"] = sum(len(share(peer(-t), core, t)) for t in range(1, RO))
        return []

    X = {"send": send, "tokens": tokens}
    Q = {"V": g.vector, "A": g.scalar, "P": g.tensor, "G": g, "S": g.sync}
    count = {}; mark = {}; waited = {e: {} for e in Q}
    for i, x in order:
        o = ops[i]; e, _, fn = o["alts"][x]
        need = {}
        for d in o["wait"]:
            s, v = mark[d]; need[s] = max(need.get(s, 0), v)
        for s, v in need.items():
            if waited[e].get(s, 0) < v:
                Q[e].wait_ge(T.sem[s], v); waited[e][s] = v
        B = T[o["bank"]] if o["bank"] else None
        ins = fn(Q[e], T, B, X)
        s = o["sem"] or "c" + e
        if o["sem"] and e == "G":
            count[s] = arrive[s]
        for c in ins:
            step = 16 if o["sem"] else 1
            c.then_inc(T.sem[s], step); count[s] = count.get(s, 0) + step
        mark[i] = (s, count.get(s, 0))
    count["sent"] = sent[0]
    for s, v in count.items():
        if waited["G"].get(s, 0) < v: g.wait_ge(T.sem[s], v)
